import numpy as np, ml_dtypes
CORES = [51,54,179,182]
N = 4
BF = ml_dtypes.bfloat16
def gentries(a):
    return np.ascontiguousarray(a.reshape(8, 16, -1).transpose(0, 2, 1)).reshape(8, -1)
def gtable(e):
    e = np.asarray(e); return np.ascontiguousarray(e.reshape(8, -1, 16).transpose(0, 2, 1)).reshape(128, -1).astype(np.int32)
W, B, L, T, H, A = 2048, 11, 192, 4, 2, 688
def codes(rng, lo, hi):
    return np.floor(rng.random((N, 8, 16, W)) * (rng.integers(lo, hi + 1, (N, 8, 1, W)) + 1)).astype(np.int64)
def names(rng):
    hub = rng.integers(0, W, W // 16)
    def some(*shape):
        return np.where(rng.random(shape) < 0.5, hub[rng.integers(0, W // 16, shape)], rng.integers(0, W, shape))
    return some(N, 8, 16, W), some(N, 8, L)
def vals(rng, size):
    return np.clip(rng.standard_normal((N, 8, 16, W), dtype=np.float32) * np.exp2(size), -64, 64)
def plainvals(rng):
    return vals(rng, rng.integers(-2, 3, (N, 8, 16, 1)))
def pack(k, v, nm, s):
    two = nm[..., :W // 2] + W * nm[..., W // 2:]
    return {"kt": k.reshape(N, 128, W).astype(np.float32).astype(BF), "vt": v.reshape(N, 128, W).astype(np.float32).astype(BF),
            "bp": np.ascontiguousarray(two.reshape(N, 128, W // 2)).astype(np.int32), "st": np.stack([gtable(a) for a in s])}
def near():
    i, j = np.triu_indices(768); i = i + 256; j = j + 256; a = i * j
    where = np.full(2 ** 20 + 1, -1); where[a] = np.arange(len(a))
    b = (2 ** 36 + a // 2) // a; m = where[b]
    h = np.nonzero((m >= 0) & (np.abs(a * b - 2 ** 36) < 2 ** 13))[0]; m = m[h]
    z = np.concatenate([np.stack([i[h], j[h], i[m], j[m]], 1), np.stack([i[h], j[h], j[m], i[m]], 1)])
    y = z.astype(np.float32) * np.float32(2.0 ** -10); p = y[:, 0] * y[:, 1]; lim = np.float32(0.0625)
    return z[(((p * y[:, 2]) * y[:, 3]) < lim) != ((p * (y[:, 2] * y[:, 3])) < lim)]
def over(rng):
    i, j = np.triu_indices(768); i = i + 256; j = j + 256
    where = np.full(2 ** 20 + 1, -1); where[i * j] = np.arange(len(i))
    x = rng.integers(256, 1024, (3, 2 ** 19)); y = x.astype(np.float32) * np.float32(2.0 ** -10); R = (y[0] * y[1]) * y[2]
    h = np.nonzero((R > 0.07) & (R < 0.25))[0]; x = x[:, h]; R = R[h]
    c = (R.astype(np.float64) * 2.0 ** 27).astype(np.int64); m = where[(2 ** 43 + c // 2) // c]
    h = np.nonzero(m >= 0)[0]; m = m[h]; R = R[h]; z = np.stack([x[0, h], x[1, h], x[2, h], i[m], j[m]], 1)
    y = z.astype(np.float32) * np.float32(2.0 ** -10); u = y[:, 3]; v = y[:, 4]; lim = np.float32(0.0625); right = ((R * u) * v) < lim
    m24, m26 = [(((np.rint(R * np.float32(2.0 ** b)) * np.float32(2.0 ** -b)) * u) * v) < lim for b in (24, 26)]
    return z[((R * (u * v)) < lim) != right], z[(m24 != right) | (m26 != right)]
def setup_inputs(rng):
    nm, s = names(rng)
    return pack(codes(rng, 12, 15), plainvals(rng), nm, s)
def setup_inputs_spread(rng):
    nm, s = names(rng); weak = rng.random((N, 8, 1, W)) < 0.3
    k = np.where(weak, codes(rng, 4, 11), codes(rng, 14, 15)); s = np.where(rng.random(s.shape) < 0.5, s, (W * rng.random(s.shape) ** 4).astype(np.int64))
    return pack(k, vals(rng, rng.integers(-3, 4, (N, 8, 1, W))), nm, s)
def setup_inputs_ends(rng):
    k = 15 * (rng.random((N, 8, 16, W)) < rng.choice(np.array([0.0, 0.25, 0.25, 0.5, 1.0]), (N, 8, 1, W))).astype(np.int64)
    four = 15 * (rng.permutation(16) < 4).astype(np.int64); kind = np.argsort(rng.random((N, 8)), axis=1) % 3; kind[N - 1, 7] = 0
    k[..., 0] = np.where(kind[..., None] == 1, 15, four); k[..., W - 1] = np.where(kind[..., None] == 0, 15, four)
    e = (W - 1) * rng.integers(0, 2, (N, 8, 16, W // 2)); m = rng.random(e.shape) < 0.66
    nm = np.concatenate([np.where(m, e, rng.integers(0, W, e.shape)), np.where(m, e, rng.integers(0, W, e.shape))], axis=3)
    s = np.where(rng.random((N, 8, L)) < 0.72, (W - 1) * rng.integers(0, 2, (N, 8, L)), rng.integers(0, W, (N, 8, L))); s[..., L - 1] = W - 1
    v = plainvals(rng); v = np.where(rng.random(v.shape) < 0.3, np.where(rng.random(v.shape) < 0.5, 64.0, -64.0), v)
    return pack(k, v, nm, s)
def setup_inputs_crowd(rng):
    nm, s = names(rng); k = rng.integers(2, 7, (N, 8, 16, W)); k[1::2] = rng.integers(11, 16, (N // 2, 8, 16, W))
    o = rng.permutation(W); n = (H + 1) * L; ch = o[:H * L].reshape(H, L); u = o[H * L:n]; nul = o[n:n + 16]; big = o[n + 16:n + 80]; pk = o[n + 80:n + 80 + H]; top = o[n + 96:n + 112]
    def lead(r, g, keys, to):
        k[r, g][:, nul] = 0; nm[r, g][:, keys] = nul[rng.integers(0, 16, (16, len(keys)))]; nm[r, g, 15, keys] = to
    for r in range(0, N, 2):
        kind = rng.permutation(8); h5 = (int(np.nonzero(kind == 5)[0][0]) - 1) % 8
        nm[r, h5][rng.random((16, W)) < 0.25] = pk[0]
        for g in range(8):
            p = int(rng.choice(np.array([0, W - 1, rng.integers(0, W), rng.integers(0, W)])))
            if kind[g] in (0, 1, 7): nm[r, g, 15] = p
            if kind[g] == 2: nm[r, g, 15] = rng.choice(rng.integers(0, W, 3), W)
            if kind[g] == 1:
                x = (p + 1 + rng.permutation(W - 1)[:H + 1]) % W; nm[r, g, 15, x[:H]] = x[1:]
                a = s[r, g].copy(); a[np.isin(a, x)] = p; a[int(rng.choice(np.array([0, L - 1, rng.integers(0, L)])))] = x[0]; s[r, g] = a
            if kind[g] in (4, 6):
                x = k[r, g]; x[:, ch[0]] = rng.integers(12, 16, (16, L)); x[:, big] = rng.integers(11, 16, (16, 64))
                for h in range(1, H):
                    x[:, ch[h]] = 0; lead(r, g, ch[h - 1], ch[h])
                nm[r, g][:, ch[H - 1]] = big[rng.integers(0, 64, (16, L))]; a = rng.permutation(ch[0])
                if kind[g] == 6: a[int(rng.choice(np.array([0, L - 1, rng.integers(0, L)])))] = nul[0]
                s[r, g] = a; b, c = (r - 1) % N, (g - 1) % 8
                k[b, c][:, ch[0]] = 0; lead(b, c, u, rng.permutation(ch[0])); lead(b, c, ch[0], ch[0]); s[b, c] = rng.permutation(u)
            if kind[g] == 5:
                k[r, g][:, u] = rng.integers(4, 8, (16, L)); k[r, g][:, pk[0]] = 0
                lead(r, g, u, pk[0]); lead(r, g, pk[:1], pk[:1]); s[r, g] = rng.permutation(u); b, c = r + 1, (g + 1) % 8
                k[b, c][:, top] = 15
                for h in range(1, H):
                    k[b, c][:, pk[h]] = 0; lead(b, c, pk[h - 1:h], pk[h:h + 1])
                nm[b, c][:, pk[H - 1]] = rng.permutation(top); s[b, c] = np.where(s[b, c] == pk[0], top[0], s[b, c])
    return pack(k, plainvals(rng), nm, s)
def setup_inputs_corners(rng):
    nm, s = names(rng); k = codes(rng, 12, 15); own = np.arange(W)
    for r in range(N):
        kind = rng.permutation(8) % 4
        for g in range(8):
            if kind[g] == 0:
                nm[r, g, :15] = own; nm[r, g, 15] = np.where(rng.random(W) < 0.5, own, nm[r, g, 15])
            if kind[g] == 1:
                e = rng.integers(0, 3, (15, W)); nm[r, g, :15] = np.where(e == 0, 0, np.where(e == 1, W - 1, own)); nm[r, g, 15] = (own - 1) % W
            if kind[g] == 2:
                hot = rng.permutation(W) < W // 2; a = np.nonzero(hot)[0]; b = np.nonzero(~hot)[0]
                k[r, g] = np.where(hot, rng.integers(12, 16, (16, W)), 0); page = b[rng.integers(0, len(b), (16, W))]
                one = own[rng.random(W) < 0.7]; page[rng.integers(0, 16, len(one)), one] = a[rng.integers(0, len(a), len(one))]
                nm[r, g] = page; s[r, g] = a[rng.integers(0, len(a), L)]
            if kind[g] == 3:
                k[r, g] = rng.integers(0, 3, (16, W)); s[r, g, 0] = 0; s[r, g, L - 1] = W - 1
    return pack(k, plainvals(rng), nm, s)
def setup_inputs_order(rng):
    nm, s = names(rng); k = codes(rng, 12, 15); z = near(); zp, zm = over(rng); lane = np.arange(L); row = np.arange(16)[:, None]
    o = rng.permutation(W); a, b, d, nul, fac = o[:L], o[L:2 * L], o[2 * L:3 * L], o[3 * L:3 * L + 16], o[3 * L + 16:3 * L + 784]
    w = rng.permutation(16); e = w[:8, None]; sc = A + 1024 - np.arange(256, 1024)
    for r in range(N):
        kind = rng.permutation(8) % 2
        for g in range(8):
            x = k[r, g]; v = nm[r, g]
            x[w[:9, None], nul] = 0
            x[:, fac] = rng.integers(0, 16, (16, 768))
            x[e, fac] = (sc[None, :] + 15 * np.arange(8)[:, None]) // 15 // 8; x[w[8], fac] = sc % 15
            if kind[g]: continue
            x[:, a] = 0; x[e, a] = 15; x[w[8], a] = 1
            x[w[:9, None], o[L:3 * L]] = 0
            lay = rng.integers(0, 4 if r % 2 else 6, L); full = lane[lay < 3]; half = lane[lay == 3]; far = lane[lay > 3]
            y = fac[z[rng.integers(0, len(z), L)] - 256]
            y5 = fac[np.where((lay == 4)[:, None], zp[rng.integers(0, len(zp), L)], zm[rng.integers(0, len(zm), L)]) - 256]
            page = np.where((lay < 3) & (row >= 4 * lay + 4), v[:, a], nul[rng.integers(0, 16, (16, L))])
            for n in range(4): page[4 * lay[full] + n, full] = y[full, n]
            page[:2, half] = y[half, :2].T; page[15, half] = b[half]
            page[:3, far] = y5[far, :3].T; page[15, far] = d[far]
            v[:, a] = page; v[:2, b] = y[:, 2:].T; s[r, g] = a
            v[:, d[far]] = nul[rng.integers(0, 16, (16, len(far)))]; v[15, d[far]] = d[far]
            nm[(r + 1) % N, (g + 1) % 8][:2, d[far]] = y5[far, 3:].T
    return pack(k, plainvals(rng), nm, s)
def check_ranges(d):
    bad = []
    a = np.asarray(d["kt"]).astype(np.float64)
    if not np.all((a >= 0) & (a <= 15) & (a == np.floor(a))): bad.append("range of kt")
    a = np.asarray(d["vt"]).astype(np.float64)
    if not np.all((a >= -64) & (a <= 64)): bad.append("range of vt")
    for n, hi in (("bp", W * W - 1), ("st", W - 1)):
        if np.min(d[n]) < 0 or np.max(d[n]) > hi: bad.append("range of " + n)
    return bad
def take(tab, c):
    return np.take_along_axis(tab, c[:, :, None, :], 3)
def reference(kt, vt, bp, st):
    k = kt.astype(np.float32).astype(np.int64).reshape(N, 8, 16, W)
    sg = np.reciprocal(1.0 + np.exp(-vt.astype(np.float64))).reshape(N, 8, 16, W)
    u = bp.astype(np.int64).reshape(N, 8, 16, W // 2); pg = np.concatenate([u & (W - 1), u >> B], axis=3)
    c = np.stack([gentries(a) for a in st]).astype(np.int64)
    q = take(k, c); R = np.ones((N, 8, L), np.float32); acc = np.zeros((N, 8, 16, L)); one = np.float32(1); out = []
    for t in range(T):
        if t:
            c, q, R, acc = [np.roll(np.roll(a, 1, axis=0), t, axis=1) for a in (c, q, R, acc)]
        came = c; whole = np.ones((N, 8, L), bool)
        for h in range(H):
            nm = take(pg, c); flat = nm.reshape(N, 8, 16 * L)
            s = np.add.reduce(q[:, :, :, None, :] * take(k, flat).reshape(N, 8, 16, 16, L), axis=2)
            beta = np.minimum(np.maximum(s - A, 0), 960).astype(np.float32) * np.float32(2.0 ** -10)
            v = take(sg, flat).reshape(N, 8, 16, 16, L)
            broke = np.zeros((N, 8, L), bool); nxt = nm[:, :, 15]
            for i in range(16):
                on = ~broke; bi = beta[:, :, i]
                acc = acc + np.where(on, R.astype(np.float64) * bi.astype(np.float64), 0.0)[:, :, None, :] * v[:, :, :, i]
                R = np.where(on, R * (one - bi), R)
                hit = on & (R < np.float32(0.0625))
                nxt = np.where(hit, nm[:, :, i], nxt); broke = broke | hit
            c = nxt; q = np.where(broke[:, :, None, :], take(k, c), q); R = np.where(broke, one, R)
            cut = whole & broke; whole = whole & ~broke
        out.append((acc + R.astype(np.float64)[:, :, None, :] * take(sg, c)).reshape(N, 128, L))
        if t < T - 1:
            for j in range(L - 1, -1, -1):
                a, g = np.nonzero(cut[:, :, j])
                pg[a, g, 15, came[a, g, j]] = c[a, g, j]
    return {"ya": np.concatenate(out, axis=2).astype(np.float32)}

def check_inputs(d):
    bad = list(check_ranges(d))
    if not bad:
        for name, y in reference(**d).items():
            for q in range(N):
                v = np.abs(np.asarray(y[q], np.float64))
                if v.max() > 7 * np.sqrt(np.mean(v * v)): bad.append('%s of rank %d is uneven' % (name, q))
    return bad

@@ -1,0 +1,570 @@
+from concourse.mybir import AluOpType as A, ActivationFunctionType as F
+
+W, L, NB, NV, NH = 2048, 192, 12, 4, 2
+SB, PS = "sbuf", "psum"
+f32, b16, i32, u16 = "float32", "bfloat16", "int32", "uint16"
+
+SCRATCH = {
+    "KW": (SB, [128, W + 2 * L], b16), "VT": (SB, [128, W], b16), "BP": (SB, [128, W // 2], i32),
+    "PG": (SB, [128, W + 16], i32), "ST": (SB, [128, NB], i32),
+    "MG": (SB, [128, 8], f32), "LB": (SB, [128, 40 * L], b16), "NL": (SB, [128, NB * 128], f32), "EQS": (SB, [128, NB * 128], b16),
+    "KG": (SB, [128, 16 * L], b16), "VG0": (SB, [128, 16 * L], f32), "VG1": (SB, [128, 16 * L], f32),
+    "NV0": (SB, [128, L], u16), "NV1": (SB, [128, L], u16), "VO": (SB, [128, NB], u16),
+    "J1": (SB, [128, NB], f32), "J2": (SB, [128, NB], i32), "J3": (SB, [128, NB], f32),
+    "PR": (SB, [128, 16 * L], f32), "SO": (SB, [128, 16 * L], f32),
+    "NM0": (SB, [128, L], u16), "NM1": (SB, [128, L], u16),
+    "OMB": (SB, [128, 204], f32), "RIN": (SB, [128, 204], f32), "ON": (SB, [128, 204], f32),
+    "TT": (SB, [128, 204], f32), "CS": (SB, [128, 208], f32), "BT": (SB, [128, 204], f32),
+    "WH": (SB, [128, NB, 17], b16), "WL": (SB, [128, NB, 17], b16), "BR": (SB, [128, NB], f32),
+    "CA": (SB, [128, NB], u16), "CL0": (SB, [128, NB], u16), "CL1": (SB, [128, NB], u16), "QO": (SB, [128, NB], u16),
+    "C2": (SB, [128, NB], f32), "DJ": (SB, [128, NB], f32), "KEY": (SB, [128, 16], f32), "CW": (SB, [128, L], f32),
+    "EQ": (SB, [128, L], b16), "CUT": (SB, [128, NB], b16), "T12": (SB, [128, NB], f32), "OFF": (SB, [128, 2 * NB], u16),
+    "NZ": (SB, [128, L], f32), "MC": (SB, [128, L], f32), "VAL": (SB, [128, L], i32),
+    "QS": (SB, [128, L], b16), "VC": (SB, [128, L], f32), "RV": (SB, [128, L], f32),
+    "Z": (SB, [128, 256], f32), "P2": (SB, [128, 256], f32), "ID2": (SB, [128, 256], f32), "IB2": (SB, [128, 256], b16),
+    "PI": (SB, [128, 128], f32), "G15": (SB, [128, 128], f32), "SEL": (SB, [128, 2048], b16), "IO2": (SB, [128, W], f32),
+    "DM": (SB, [128, 17], f32), "D1": (SB, [128, 17], f32), "D2": (SB, [128, 17], f32), "R17": (SB, [128, 17], f32),
+    "CJ": (SB, [128, 204], b16), "CJA": (SB, [128, 204], b16), "CJB": (SB, [128, 204], b16), "M17": (SB, [128, 204], f32), "MK": (SB, [128, 768], f32),
+    "ONE": (SB, [128, 128], b16), "BIA": (SB, [128, 204], b16), "CM": (SB, [128, L], b16),
+    "MCL": (SB, [128, L], f32), "TRI": (SB, [128, L], b16), "RL": (SB, [128, L], f32), "TA": (SB, [128, L], f32),
+    "PP": (SB, [128, 1], i32), "PC": (SB, [128, 4], i32), "PF": (SB, [128, 4], f32), "PX": (SB, [128, 8], f32),
+    "RB": (SB, [128, NB], f32), "EI": (SB, [128, NB], i32),
+    "LO": (SB, [128, NB], u16), "NO": (SB, [128, NB], u16), "EO": (SB, [128, NB], u16), "RO": (SB, [128, NB], u16),
+    "BL": (SB, [128, NB], u16), "C15": (SB, [128, NB], u16),
+    "pS": (PS, [128, 512], f32), "pD": (PS, [128, 512], f32), "pW": (PS, [128, 512], f32), "pM": (PS, [128, 512], f32),
+    "pX": (PS, [128, 512], f32), "pE0": (PS, [128, 512], f32), "pE1": (PS, [128, 512], f32), "pE2": (PS, [128, 512], f32),
+}
+for _t in range(NV):
+    SCRATCH["AC%d" % _t] = (SB, [128, L], f32)
+    SCRATCH["RP%d" % _t] = (SB, [128, L], f32)
+for _t in range(1, NV):
+    SCRATCH["MO%d" % _t] = (SB, [128, 2 * NB], f32)
+    SCRATCH["MI%d" % _t] = (SB, [128, 2 * NB], f32)
+    SCRATCH["QT%d" % _t] = (SB, [128, L], b16)
+    SCRATCH["QI%d" % _t] = (SB, [128, L], b16)
+    SCRATCH["AI%d" % _t] = (SB, [128, L], f32)
+
+SEMAPHORES = (["cV", "cA", "cT", "cG", "sent"] + ["d%d" % k for k in range(9)]
+              + ["r%s%d" % (x, t) for x in "mqa" for t in range(1, NV)])
+
+LAT = 110
+KCH = [4, 4, 3, 1]
+LOOK = 150
+RED = [64] * 7 + [96]
+ORDER = {}
+L_ON_ACT = ()
+FAC, GA, SC = 1.25, 1.56, 3.8
+COSTS = [(GA, SC, 0.5, 30, 110), (1.95, 3.0, 0.5, 20, 150), (1.2, 5.0, 0.6, 40, 80)]
+WEIGHTS = [2, 1, 1]
+TRIES = 4500
+
+
+def collect(g, T, topo, core, nxt):
+    ops = []
+    last_w, readers, bank = {}, {}, {}
+
+    def op(eng, calls, r, w, cost, after=0, sem=None, n=0):
+        k = len(ops)
+        hard, soft = set(), set()
+        for x in r:
+            if x[0] != "#" and x in last_w: hard.add(last_w[x])
+        for x in w:
+            if x[0] == "#": continue
+            if x in last_w: hard.add(last_w[x])
+            hard.update(readers.get(x, []))
+        for x in list(r) + list(w):
+            if x[0] == "#":
+                for e, j in bank.setdefault(x, {}).items():
+                    (soft if e == eng else hard).add(j)
+                bank[x][eng] = k
+        for x in r:
+            if x[0] != "#": readers.setdefault(x, []).append(k)
+        for x in w:
+            if x[0] != "#":
+                last_w[x] = k
+                readers[x] = []
+        hard.discard(k)
+        soft.discard(k)
+        if eng == "T":
+            for j in list(hard):
+                if ops[j]["e"] == "T":
+                    hard.discard(j)
+                    soft.add(j)
+        ops.append({"e": eng, "c": calls, "h": hard, "s": soft, "t": cost, "a": after, "sem": sem, "n": n})
+        return k
+
+    V, S, PE = g.vector, g.scalar, g.tensor
+
+    def ts(out, in0, s1, s2, o0, o1, r, w, n, f=1.0):
+        if o1 is None:
+            op("V", [lambda: V.tensor_scalar(out, in0, s1, None, o0)], r, w, (n, f))
+        else:
+            op("V", [lambda: V.tensor_scalar(out, in0, s1, s2, o0, o1)], r, w, (n, f))
+
+    def tt(out, in0, in1, o, r, w, n, f=1.0):
+        op("V", [lambda: V.tensor_tensor(out, in0, in1, o)], r, w, (n, f))
+
+    def cp(out, in_, r, w, n, f=1.0):
+        op("V", [lambda: V.tensor_copy(out, in_)], r, w, (n, f))
+
+    def ms(ap, c, w, n):
+        op("V", [lambda: V.memset(ap, c)], [], w, (n, 1.0))
+
+    def scan(out, d0, d1, o0, o1, r, w, n):
+        op("V", [lambda: V.tensor_tensor_scan(out, d0, d1, 0.0, o0, o1)], r, w, (n, 1.0))
+
+    def act(out, in_, fn, r, w, n, f=1.0, **kw):
+        op("A", [lambda: S.activation(out, in_, fn, **kw)], r, w, (n, f))
+
+    def mm(lst, r, w, cyc):
+        op("T", [(lambda a=a: PE.matmul(a[0], a[1], a[2], a[3], a[4])) for a in lst], r, w, (cyc, 1.0))
+
+    def iota(out, pat, base, cm, w, n, small=True):
+        if small:
+            op("G", [lambda: g.iota(out, pat, base, cm, allow_small_or_imprecise_dtypes=True)], [], w, (200 + 2.5 * n, 1.0))
+        else:
+            op("G", [lambda: g.iota(out, pat, base, cm)], [], w, (200 + 2.5 * n, 1.0))
+
+    def asel(out, in_, pat, cm, r, w, n, base=0):
+        op("G", [lambda: g.affine_select(out, in_, pat, A.not_equal, 1.0, base, cm)], r, w, (250 + 2.5 * n, 1.0))
+
+    nd = [0]
+
+    def dma(q, out, in_, r, w, after):
+        s = "d%d" % nd[0]
+        nd[0] += 1
+        e = g.sync if q == "S" else g.scalar
+        op(q, [lambda: e.dma_start(out, in_)], r, w, (60, 1.0), after, s, 16)
+
+    rid, pid = topo.addr(nxt, core)
+    eng = topo.engines(core, nxt)[:8]
+    mask = sum(1 << e for e in eng)
+    sends = [0]
+
+    def send(dst, src, sem, r, w, after):
+        k = op("G", [lambda: g.remote_dma(dst, src, T.sem[sem], T.sem.sent, pid, rid, mask)], r, ["@" + sem], (900, 1.0), 0, "sent", 0)
+        sends[0] += len(eng)
+        op("R", [], ["@" + sem], w, (0, 1.0), after, sem, len(eng))
+        return k
+
+    K = T.KW[:, L:L + W]
+    qA, qB = T.KW[:, 0:L], T.KW[:, L + W:L + W + L]
+    h = W // 4
+    dma("S", T.BP[:, 0:h], T.bp[:, 0:h], [], ["BPa"], 3600)
+    dma("A", T.BP[:, h:2 * h], T.bp[:, h:2 * h], [], ["BPb"], 4600)
+    dma("S", T.ST[:], T.st[:], ["@0"], ["ST"], 4600)
+    dma("A", K, T.kt[:], ["@1"], ["K"], 6600)
+    dma("S", T.VT[:], T.vt[:], ["@2"], ["VT"], 8600)
+    ops[2]["s"].add(0)
+    ops[3]["s"].add(1)
+    ops[4]["s"].add(2)
+    for j, nm in enumerate(("BPa", "BPb")):
+        ts(T.PG[:, j * h:(j + 1) * h], T.BP[:, j * h:(j + 1) * h], W - 1, None, A.bitwise_and, None, [nm], ["PG%d" % j], h)
+        ts(T.PG[:, (2 + j) * h:(3 + j) * h], T.BP[:, j * h:(j + 1) * h], 11, None, A.logical_shift_right, None, [nm], ["PG%d" % (2 + j)], h)
+    ms(T.PG[:, W:W + 16], 0, ["PG4"], 16)
+    PGR = ["PG%d" % j for j in range(4)]
+    iota(T.PP[:], [[0, 1]], 0, 1, ["PP"], 1, False)
+    iota(T.RB[:], [[1, NB]], 0, 0, ["RB"], NB)
+    iota(T.R17[:], [[1, 17]], 0, 0, ["R17"], 17)
+    iota(T.EI[:], [[128, NB]], 0, 1, ["EI"], NB, False)
+    iota(T.RL[:], [[0, NB], [1, 16]], 0, 0, ["RL"], L)
+    ms(T.Z[:], 0.0, ["Z"], 256)
+    asel(T.ID2[:], T.Z[:], [[0, 2], [-1, 128]], 1, ["Z"], ["ID2"], 256)
+    asel(T.P2[:], T.Z[:], [[0, 2], [-1, 8], [-8, 16]], 1, ["Z"], ["P2"], 256)
+    iota(T.SEL[:], [[0, 2048]], 0, 0, ["SEL"], 2048)
+    asel(T.SEL[:], T.SEL[:], [[-8, 16], [-1, 8], [0, 16]], 1, ["SEL"], ["SEL"], 2048)
+    iota(T.IO2[:], [[2, W]], 0, 0, ["IO2"], W)
+    asel(T.PI[:], T.Z[:, 0:128], [[-1, 16], [-16, 8]], 1, ["Z"], ["PI"], 128)
+    for j, (o, c) in enumerate(((A.bitwise_and, 15), (A.logical_shift_right, 4), (A.bitwise_and, 3), (A.logical_shift_right, 3))):
+        ts(T.PC[:, j:j + 1], T.PP[:], c, None, o, None, ["PP"], ["PC%d" % j], 1)
+    cp(T.PF[:], T.PC[:], ["PC0", "PC1", "PC2", "PC3"], ["PF"], 4)
+    lf, gf, l4, lc = [T.PF[:, j:j + 1] for j in range(4)]
+    X = [T.PX[:, j:j + 1] for j in range(8)]
+    ts(X[0], lf, 8.0, gf, A.mult, A.add, ["PF"], ["X0"], 1)
+    ts(X[1], lf, -1.0, float(-W), A.mult, A.add, ["PF"], ["X1"], 1)
+    ts(X[2], lf, 40.0, gf, A.mult, A.add, ["PF"], ["X2"], 1)
+    ts(T.MG[:], T.RB[:, 0:8], gf, -1.0 / 1024, A.is_equal, A.mult, ["RB", "PF"], ["MG"], 8)
+    ts(X[3], lf, 12.0, None, A.mult, None, ["PF"], ["X3"], 1)
+    ts(X[4], lf, float(W), None, A.add, None, ["PF"], ["X4"], 1)
+    ts(X[5], lf, 15.0, None, A.is_lt, None, ["PF"], ["X5"], 1)
+    ts(X[6], lc, -8.0, None, A.mult, None, ["PF"], ["X6"], 1)
+    ts(T.LO[:], T.RB[:], 640.0, X[2], A.mult, A.add, ["RB", "X2"], ["LO"], NB)
+    ts(T.NO[:], T.RB[:], 128.0, X[0], A.mult, A.add, ["RB", "X0"], ["NO"], NB)
+    ts(T.RO[:], T.RB[:], X[3], None, A.add, None, ["RB", "X3"], ["RO"], NB)
+    ts(T.C15[:], T.RB[:], 17.0, 15.0, A.mult, A.add, ["RB"], ["C15"], NB)
+    ts(T.J1[:], T.RB[:], 16.0, lf, A.mult, A.add, ["RB", "PF"], ["J1"], NB)
+    ts(T.J3[:], T.J1[:], -5.5, 1.0 / 12, A.add, A.mult, ["J1"], ["J3"], NB)
+    cp(T.J2[:], T.J3[:], ["J3"], ["J2"], NB)
+    ts(T.J3[:], T.J2[:], -1528.0, gf, A.mult, A.add, ["J2", "PF"], ["J3"], NB)
+    ts(T.J1[:], T.J1[:], 128.0, None, A.mult, None, ["J1"], ["J1"], NB)
+    tt(T.J1[:], T.J1[:], T.J3[:], A.add, ["J1", "J3"], ["J1"], NB)
+    cp(T.VO[:], T.J1[:], ["J1"], ["VO"], NB)
+    cp(T.BL[:], T.RB[:], ["RB"], ["BL"], NB)
+    cp(T.EO[:], T.EI[:], ["EI"], ["EO"], NB)
+    ts(T.D1[:], T.R17[:], lf, None, A.is_equal, None, ["R17", "PF"], ["D1"], 17)
+    ts(T.D2[:], T.R17[:], -1.0, lf, A.add, A.is_equal, ["R17", "PF"], ["D2"], 17)
+    tt(T.DM[:], T.D1[:], T.D2[:], A.subtract, ["D1", "D2"], ["DM"], 17, 2)
+    for nm in ("CJ", "CJA", "CJB"):
+        ms(T[nm][:], 0.0, [nm], 102)
+    ts(T.CJ[:, 16::17], T.RB[:], 0.0, lc, A.mult, A.add, ["RB", "PF"], ["CJ"], NB)
+    ts(T.CJA[:, 16::17], T.RB[:], 16.0, float(-L), A.mult, A.add, ["RB"], ["CJA"], NB)
+    ts(T.CJB[:, 16::17], T.RB[:], 16.0, float(W), A.mult, A.add, ["RB"], ["CJB"], NB)
+    ms(T.LB[:, 0:2048], 0.0, ["LBz0"], 1024)
+    ms(T.LB[:, 2048:5632], 0.0, ["LBz1"], 1792)
+    act(T.NL[:], T.LB[:, 0:1536], F.Copy, ["LBz0"], ["NLz"], 1536)
+    act(T.LB[:, 5632:7680], T.LB[:, 0:2048], F.Copy, ["LBz0"], ["LBz2"], 2048)
+    LBS = ["LB%d" % j for j in range(8)]
+    act(T.MK[:], T.LB[:, 0:768], F.Identity, ["LBz0"], ["MK"], 768, bias=1.0)
+    act(T.M17[:], T.LB[:, 0:204], F.Identity, ["LBz0"], ["M17"], 204, bias=1.0)
+    act(T.RIN[:], T.LB[:, 0:204], F.Copy, ["LBz0"], ["RIN"], 204)
+    ms(T.M17[:, 0::17], 0.0, ["M17"], NB)
+    ms(T.MK[:, 0::16], 0.0, ["MK"], 48)
+    ms(T.ONE[:], 1.0, ["ONE"], 64)
+    ms(T.BIA[:], 1712.0 / 2048, ["BIA"], 102)
+    ms(T.BIA[:, 0::17], 0.0, ["BIA"], 6)
+    ms(T.CM[:], -1.0 / 1024, ["CM"], 96)
+    ms(T.RIN[:, 0::17], 1.0, ["RIN"], NB)
+    ms(T.BT[:, 200:204], 0.0, ["BT"], 4)
+    ms(T.CS[:, 204:208], 0.0, ["CSp"], 4)
+    ms(T.KEY[:], 0.0, ["KEY"], 16)
+    ms(T.EQS[:], 0.0, ["EQS"], 768)
+    ts(T.MCL[:], T.RL[:], lc, None, A.is_equal, None, ["RL", "PF"], ["MCL"], L)
+    ts(T.TA[:], T.RL[:], lf, -2.0, A.is_gt, A.mult, ["RL", "PF"], ["TA"], L)
+    ts(T.NZ[:], T.RL[:], lf, None, A.is_ge, None, ["RL", "PF"], ["NZ"], L)
+    tt(T.TRI[:], T.TA[:], T.NZ[:], A.add, ["TA", "NZ"], ["TRI"], L, 2)
+    act(T.IB2[:], T.ID2[:], F.Copy, ["ID2"], ["IB2"], 256)
+    ms(T.G15[:], 0.0, ["G15"], 128)
+    cp(X[7], T.PP[:], ["PP"], ["X7"], 1)
+    ts(T.T12[:, 0:8], T.RB[:, 0:8], X[6], X[7], A.subtract, A.is_equal, ["RB", "X6", "X7"], ["T12"], 8)
+    cp(T.G15[:, 15::16], T.T12[:, 0:8], ["T12"], ["G15"], 8)
+
+    def perm(t):
+        return T.P2[:, 128 - 16 * t:256 - 16 * t]
+
+    pM = [T.pM[:, 16 * j:16 * j + NB] for j in range(8)]
+    Rs, w1, wv = T.pW[:, 0:204], T.pW[:, 256:460], T.pD[:, 256:460]
+    slot = [0]
+    for t in range(NV):
+        last = t == NV - 1
+        AC, RP = T["AC%d" % t], T["RP%d" % t]
+        if t == 0:
+            cp(T.CA[:], T.ST[:], ["ST"], ["CA"], NB)
+            act(qA, K.indirect(T.CA[:]), F.Copy, ["K", "CA"], ["qA"], L, GA)
+        else:
+            MI, QI = T["MI%d" % t], T["QI%d" % t]
+            cp(T.CA[:], MI[:, 0:NB], ["MI%d" % t], ["CA"], NB)
+            mm([(pM[6], T.PI[:], MI[:, NB:2 * NB], True, True)], ["MI%d" % t, "PI"], ["#M", "pM6"], 256)
+            act(T.RIN[:, 0::17], pM[6], F.Copy, ["#M", "pM6"], ["RIN"], NB)
+            act(qA, QI[:], F.Copy, ["QI%d" % t], ["qA"], L)
+        for hop in range(NH):
+            n = t * NH + hop
+            NM, nmn = T["NM%d" % (n % 2)], "NM%d" % (n % 2)
+            VG, vgn = T["VG%d" % (n % 2)], "VG%d" % (n % 2)
+            cl, cln = (T.CA, "CA") if hop == 0 else (T.CL0, "CL0")
+            cp(NM[:], T.PG[:, 0:W].indirect(cl[:]), PGR + [cln], [nmn], L, GA)
+            if hop == 1: q, qn = qB, "qB"
+            elif t == 0: q, qn = qA, "qA"
+            else: q, qn = T["QI%d" % t][:], "QI%d" % t
+            if n in L_ON_ACT:
+                for gg in range(8):
+                    act(T.LB[:, gg::40], q, F.Identity, [qn, "MG"], ["LB%d" % gg], L, scale=T.MG[:, gg:gg + 1])
+            else:
+                tt(T.LB[:].indirect(T.LO[:]), q, T.CM[:], A.mult, [qn, "CM", "LO", "LBz1", "LBz2"], LBS + ["LBz0"], L, SC)
+            cp(T.NL[:].indirect(T.NO[:]), NM[:], [nmn, "NO", "NLz"], ["NL"], L, SC)
+            NMV, nvn = T["NV%d" % (n % 2)], "NV%d" % (n % 2)
+            cp(NMV[:], T.NL[:].indirect(T.VO[:]), ["NL", "VO"], [nvn], L, GA)
+            CJ, cjn = (T.CJA, "CJA") if hop == 0 else (T.CJB, "CJB")
+            mm([(T.pD[:, 0:204], T.IB2[:, 0:128], T.CJ[:], True, False)], ["IB2", "CJ"], ["#D", "pD"], 204)
+            for b0 in range(0, NB, 3):
+                mm([(T.pD[:, 17 * b:17 * b + 17], T.NL[:, 128 * b:128 * b + 128], T.DM[:], False, False)
+                    for b in range(b0, b0 + 3)], ["NL", "DM"], ["#D", "pD"], 768)
+            mm([(T.pD[:, 0:204], T.ONE[0:1, :], CJ[0:1, :], False, True)], ["ONE", cjn], ["#D", "pD"], 204)
+            mm([(T.pS[:, 0:204], T.ONE[0:1, :], T.BIA[0:1, :], True, False)], ["ONE", "BIA"], ["#S", "pS"], 204)
+            b0 = 0
+            for j, nb in enumerate(KCH):
+                act(T.KG[:, 256 * b0:256 * (b0 + nb)], K.indirect(NM[:, 16 * b0:16 * (b0 + nb)]), F.Copy,
+                    ["K", nmn], ["KG%d" % j], 256 * nb, GA)
+                for b in range(b0, b0 + nb):
+                    mm([(T.pS[32 * (l // 4):32 * (l // 4) + 32, 17 * b + 1:17 * b + 17],
+                         T.LB[:, 40 * (16 * b + l) - 8 * (l % 4):40 * (16 * b + l) - 8 * (l % 4) + 32],
+                         T.KG[:, 16 * (16 * b + l):16 * (16 * b + l) + 16],
+                         False, False) for l in range(16)], LBS + ["KG%d" % j], ["#S", "pS"], 512)
+                b0 += nb
+            mm([(T.pS[:, 0:204], T.ONE[0:1, :], T.BIA[0:1, :], False, True)], ["ONE", "BIA"], ["#S", "pS"], 204)
+            if hop == 0 and not last:
+                act(T.NZ[:], T.NL[:].indirect(T.NO[:]), F.Identity, ["NL", "NO", "X5"], ["NZ"], L, GA, scale=X[5])
+                if t == 0:
+                    ts(T.C2[:], T.CA[:], 2.0, None, A.mult, None, ["CA"], ["C2"], NB)
+                    ts(T.DJ[:], T.CA[:], X[4], None, A.subtract, None, ["CA", "X4"], ["DJ"], NB)
+                else:
+                    act(T.C2[:], MI[:, 0:NB], F.Identity, ["MI%d" % t], ["C2"], NB, scale=2.0)
+                    act(T.DJ[:], MI[:, 0:NB], F.Identity, ["MI%d" % t, "X1"], ["DJ"], NB, bias=X[1])
+                act(T.CW[:], T.IO2[:].indirect(T.CA[:]), F.Copy, ["IO2", "CA"], ["CW"], L, GA)
+            ts(T.OMB[:], T.pS[:, 0:204], 0.0625, 1.0, A.max, A.min, ["#S", "pS"], ["OMB"], 204)
+            scan(Rs, T.OMB[:], T.RIN[:], A.mult, A.max, ["OMB", "RIN"], ["Rs"], 204)
+            ts(T.ON[:], Rs, 0.0625, None, A.is_ge, None, ["Rs"], ["ON"], 204)
+            ts(T.BR[:], T.pW[:, 16:204:17], 0.0625, None, A.is_lt, None, ["Rs"], ["BR"], NB)
+            tt(T.RIN[:, 0::17], T.pW[:, 16:204:17], T.BR[:], A.max, ["Rs", "BR"], ["RIN"], NB)
+            if not last:
+                mm([(pM[0], perm(0), T.BR[:], True, True)], ["P2", "BR"], ["#M", "pM0"], 256)
+                if hop == 0:
+                    tt(T.KEY[:, 0:NB], pM[0], T.C2[:], A.add, ["#M", "pM0", "C2"], ["KEY"], NB)
+                else:
+                    cp(T.CUT[:], pM[0], ["#M", "pM0"], ["CUT"], NB)
+            tt(T.TT[:], T.pD[:, 0:204], T.ON[:], A.mult, ["#D", "pD", "ON"], ["TT"], 204)
+            scan(T.CS[:, 0:204], T.M17[:], T.TT[:], A.mult, A.add, ["M17", "TT"], ["CS"], 204)
+            cn, qo = T.CS[:, 15:204:17], T.CS[:, 16:204:17]
+            if hop == 0:
+                mm([(pM[1], perm(0), cn, True, True), (pM[2], perm(0), qo, True, True)], ["P2", "CS"], ["#M", "pM1", "pM2"], 512)
+                cp(T.CL0[:], pM[1], ["#M", "pM1"], ["CL0"], NB)
+                ts(T.QO[:], pM[2], float(L), None, A.add, None, ["#M", "pM2"], ["QO"], NB)
+                act(qB, T.KW[:, 0:L + W].indirect(T.QO[:]), F.Copy, ["K", "qA", "QO"], ["qB"], L, GA)
+                if not last:
+                    tt(T.EQ[:], T.KEY[:].indirect(T.BL[:]), T.CW[:], A.is_equal, ["KEY", "BL", "CW"], ["EQ"], L, GA)
+                    tt(T.EQS[:].indirect(T.EO[:]), T.EQ[:], T.TRI[:], A.mult, ["EQ", "TRI", "EO"], ["EQS"], L, SC)
+            elif last:
+                mm([(pM[1], perm(0), cn, True, True)], ["P2", "CS"], ["#M", "pM1"], 256)
+                cp(T.CL1[:], pM[1], ["#M", "pM1"], ["CL1"], NB)
+            else:
+                u = t + 1
+                MO, QT = T["MO%d" % u], T["QT%d" % u]
+                mm([(T.pX[:, 400 + b:401 + b], T.EQS[:, 128 * b:128 * b + 128], T.CUT[:, b:b + 1], True, True) for b in range(NB)],
+                   ["EQS", "CUT"], ["#X", "pXe"], 768)
+                mm([(T.pM[:, 60:72], perm(u), T.RIN[:, 0::17], True, True), (T.pM[:, 48:60], perm(u), cn, True, True),
+                    (pM[2], perm(0), qo, True, True), (pM[1], perm(0), cn, True, True)],
+                   ["P2", "CS", "RIN"], ["#M", "pM1", "pM2", "pM3"], 1024)
+                cp(MO[:], T.pM[:, 48:72], ["#M", "pM3"], ["MO%d" % u], 2 * NB)
+                send(T["MI%d" % u][:], MO[:], "rm%d" % u, ["MO%d" % u], ["MI%d" % u], 3000)
+                cp(T.QO[:], pM[2], ["#M", "pM2"], ["QO"], NB)
+                cp(T.CL1[:], pM[1], ["#M", "pM1"], ["CL1"], NB)
+                tt(T.T12[:], T.pX[:, 400:412], T.DJ[:], A.mult, ["#X", "pXe", "DJ"], ["T12"], NB)
+                ts(T.OFF[:, 0::2], T.T12[:], 0.0, X[4], A.min, A.add, ["T12", "X4"], ["OFF"], NB)
+                tt(T.MC[:], T.CS[:].indirect(T.C15[:]), T.MCL[:], A.mult, ["CS", "CSp", "C15", "MCL"], ["MC"], L, GA)
+                mm([(T.pX[:, 0:L], T.G15[:], T.MC[:], True, True)], ["G15", "MC"], ["#X", "pXa"], 768)
+                tt(T.VAL[:], T.pX[:, 0:L], T.NZ[:], A.add, ["#X", "pXa", "NZ"], ["VAL"], L)
+                for b in range(NB - 1, -1, -1):
+                    cp(T.PG[:].indirect(T.OFF[:, 2 * b:2 * b + 1]), T.VAL[:, 16 * b:16 * b + 16], ["VAL", "OFF"], PGR + ["PG4"], 16, SC)
+                act(T.QS[:], T.KW[:, L:].indirect(T.QO[:]), F.Copy, ["K", "qB", "QO"], ["QS"], L, GA)
+                mm([(T.pX[:, L:2 * L], T.IB2[:, 128 - 16 * u:256 - 16 * u], T.QS[:], True, True)], ["IB2", "QS"], ["#X", "pXb"], L)
+                act(QT[:], T.pX[:, L:2 * L], F.Copy, ["#X", "pXb"], ["QT%d" % u], L)
+                send(T["QI%d" % u][:], QT[:], "rq%d" % u, ["QT%d" % u], ["QI%d" % u], 3400)
+            for j in range(4):
+                act(VG[:, 768 * j:768 * (j + 1)], T.VT[:].indirect(NMV[:, 48 * j:48 * (j + 1)]), F.Sigmoid,
+                    ["VT", nvn], ["%s_%d" % (vgn, j)], 768, GA)
+            act(T.BT[:, 0:203], T.OMB[:, 1:204], F.Identity, ["OMB"], ["BT"], 204, bias=1.0, scale=-1.0)
+            tt(w1, Rs, T.ON[:], A.mult, ["Rs", "ON"], ["w1"], 204)
+            tt(wv, w1, T.BT[:], A.mult, ["w1", "BT"], ["#D", "wv"], 204)
+            if hop == 1:
+                cp(T.pD[:, 272:460:17], T.RIN[:, 0::17], ["RIN", "wv"], ["#D", "wv"], NB)
+            act(T.WH[:], wv, F.Copy, ["#D", "wv"], ["WH"], 204)
+            tt(T.WL[:], wv, T.WH[:], A.subtract, ["#D", "wv", "WH"], ["WL"], 204)
+            acn = "AC%d" % t
+            if hop == 1:
+                act(T.VC[:], T.VT[:].indirect(T.CL1[:]), F.Sigmoid, ["VT", "CL1"], ["VC"], L, GA)
+                lst = []
+                for l in range(16):
+                    o = T.pX[:, l:L:16]
+                    sel = T.SEL[:, 128 * l:128 * l + 128]
+                    lst += [(o, sel, T.WH[:, :, 16], True, False), (o, sel, T.WL[:, :, 16], False, True)]
+                mm(lst, ["SEL", "WH", "WL"], ["#X", "pXa"], 2048)
+                tt(T.RV[:], T.pX[:, 0:L], T.VC[:], A.mult, ["#X", "pXa", "VC"], ["RV"], L)
+            nr = RED[n]
+            lo = 16 * nr
+            sos = []
+            for l0 in range(0, 16, 2):
+                e = slot[0] % 3
+                slot[0] += 1
+                pE = T["pE%d" % e]
+                lst = []
+                for l in (l0, l0 + 1):
+                    o = pE[:, L * (l - l0):L * (l - l0 + 1)]
+                    sel = T.SEL[:, 128 * l:128 * l + 128]
+                    lst += [(o, sel, T.WH[:, :, 0:16], True, False), (o, sel, T.WL[:, :, 0:16], False, True)]
+                mm(lst, ["SEL", "WH", "WL"], ["#E%d" % e, "pE%d" % e], 4 * L)
+                tt(T.PR[:, L * l0:L * (l0 + 2)], VG[:, L * l0:L * (l0 + 2)], pE[:, 0:2 * L], A.mult,
+                   ["%s_%d" % (vgn, l0 // 4), "#E%d" % e, "pE%d" % e], ["PR%d" % l0], 2 * L)
+                hi = L * (l0 + 2)
+                if l0 % 4 == 2 and hi > lo:
+                    sos.append("SO%d" % (l0 // 4))
+                    scan(T.SO[:, lo:hi], T.MK[:, 0:hi - lo], T.PR[:, lo:hi], A.mult, A.add,
+                         ["MK", "PR%d" % (l0 - 2), "PR%d" % l0], sos[-1:], hi - lo)
+                    lo = hi
+            rot = T.ID2[:, 128 - 16 * t:256 - 16 * t]
+            if nr:
+                pR = T.pX[:, 416:416 + nr]
+                prs = ["PR%d" % l0 for l0 in range(0, 16, 2) if L * l0 < 16 * nr]
+                for i0 in range(0, 16, 4):
+                    mm([(pR, T.ID2[:, 0:128], T.PR[:, i:16 * nr:16], i == 0, n == 0 and i == 15) for i in range(i0, i0 + 4)],
+                       ["ID2"] + prs, ["#X", "pXr"], 16 * max(64, nr))
+                if hop == 1:
+                    mm([(pR, T.ID2[:, 0:128], AC[:, 0:nr], False, True)], ["ID2", acn], ["#X", "pXr"], 4 * max(64, nr))
+                elif t:
+                    mm([(pR, rot, T["AI%d" % t][:, 0:nr], False, True)], ["ID2", "AI%d" % t], ["#X", "pXr"], 4 * max(64, nr))
+                act(AC[:, 0:nr], pR, F.Copy, ["#X", "pXr"], [acn + "r"], nr)
+            so, m = T.SO[:, 16 * nr + 15::16], L - nr
+            if hop == 1:
+                tt(AC[:, nr:L], so, AC[:, nr:L], A.add, sos + [acn, acn + "r"], [acn], m, 2)
+                if not last:
+                    send(T["AI%d" % (t + 1)][:], AC[:], "ra%d" % (t + 1), [acn], ["AI%d" % (t + 1)], 3800)
+                tt(RP[:], AC[:].indirect(T.RO[:]), T.RV[:], A.add, [acn, "RO", "RV"], ["RP%d" % t], L, GA)
+                dma("S", T.ya[:, L * t:L * (t + 1)], RP[:], ["RP%d" % t], ["ya%d" % t], 2500)
+            elif t == 0:
+                cp(AC[:, nr:L], so, sos + [acn + "r"], [acn], m)
+            else:
+                mm([(T.pX[:, L:L + m], rot, T["AI%d" % t][:, nr:L], True, True)], ["ID2", "AI%d" % t], ["#X", "pXb"], 4 * m)
+                tt(AC[:, nr:L], T.pX[:, L:L + m], so, A.add, sos + ["#X", "pXb", acn + "r"], [acn], m)
+    return ops, sends[0]
+
+
+def costs(ops, s):
+    out = []
+    for o in ops:
+        e, n, f = o["e"], o["t"][0], o["t"][1]
+        if o["sem"] or e in "GSR": c = n
+        elif e == "T": c = FAC * n * s[2]
+        elif f == GA: c = FAC * (s[3] + 30 + n * s[0])
+        elif f == SC: c = FAC * (s[3] + 30 + n * s[1])
+        else: c = FAC * (s[3] + (20 if e == "A" else 0) + max(n * f, 64 - s[3]))
+        out.append(c)
+    return out
+
+
+def prepare(ops):
+    succ = [[] for _ in ops]
+    pred = []
+    for k, o in enumerate(ops):
+        pred.append([(j, ops[j]["a"], j in o["h"]) for j in o["h"] | o["s"]])
+        for j in o["h"] | o["s"]:
+            succ[j].append((k, j in o["h"]))
+    return [o["e"] for o in ops], [o["a"] for o in ops], pred, succ
+
+
+def span(pre, order, cost, lat):
+    eng, aft, pred, succ = pre
+    end = [0.0] * len(eng)
+    free = {}
+    for k in order:
+        s = free.get(eng[k], 0.0)
+        for j, a, hard in pred[k]:
+            x = end[j] + a + lat if hard else end[j]
+            if x > s: s = x
+        end[k] = s + cost[k]
+        if eng[k] != "R": free[eng[k]] = end[k]
+    return max(x + a for x, a in zip(end, aft))
+
+
+def listsched(pre, cost, lat, off):
+    eng, aft, pred, succ = pre
+    n = len(eng)
+    need = [len(p) for p in pred]
+    pr = [0.0] * n
+    for k in range(n - 1, -1, -1):
+        m = 0.0
+        for j, hard in succ[k]:
+            x = pr[j] + aft[k] + LAT if hard else pr[j]
+            if x > m: m = x
+        pr[k] = cost[k] + max(m, aft[k])
+    pr = [p + float(z) for p, z in zip(pr, off)]
+    ready = [0.0] * n
+    free = {e: 0.0 for e in "VATGSR"}
+    pool = {e: [] for e in "VATGSR"}
+    for k in range(n):
+        if need[k] == 0: pool[eng[k]].append(k)
+    pick = {}
+    order = []
+    while len(order) < n:
+        for e, mine in pool.items():
+            if e not in pick and mine:
+                t0 = max(free[e], min([ready[k] for k in mine]))
+                k = max([(pr[k], -k) for k in mine if ready[k] <= t0 + LOOK])[1]
+                pick[e] = (max(t0, ready[-k]), -k)
+        s, k = min(pick.values())
+        e = eng[k]
+        del pick[e]
+        pool[e].remove(k)
+        order.append(k)
+        end = s + cost[k]
+        if e != "R": free[e] = end
+        for j, hard in succ[k]:
+            x = end + aft[k] + lat if hard else end
+            if x > ready[j]: ready[j] = x
+            need[j] -= 1
+            if need[j] == 0:
+                pool[eng[j]].append(j)
+                pick.pop(eng[j], None)
+    return order
+
+
+def schedule(ops):
+    n = len(ops)
+    pre = prepare(ops)
+    cs = [costs(ops, s) for s in COSTS]
+    seed = [12345]
+
+    def rnd(m):
+        seed[0] = (seed[0] * 1103515245 + 12345) % 2 ** 31
+        return (seed[0] >> 8) % m
+
+    def score(off):
+        order = listsched(pre, cs[0], COSTS[0][4], off)
+        return sum(w * span(pre, order, c, s[4]) for w, c, s in zip(WEIGHTS, cs, COSTS)), order
+
+    off = [0.0] * n
+    best, order = score(off)
+    for _ in range(TRIES):
+        o2 = list(off)
+        for _k in range(1 + rnd(7)):
+            o2[rnd(n)] += 100.0 * (rnd(15) + rnd(15) - 14)
+        s, od = score(o2)
+        if s <= best: best, order, off = s, od, o2
+    return order
+
+
+def rank_program(g, core, T, topo):
+    rank = T.rank_of(core)
+    if rank is None:
+        return
+    nxt = T.cores[(rank + 1) % len(T.cores)]
+    ops, nsent = collect(g, T, topo, core, nxt)
+    if "o" not in ORDER:
+        ORDER["o"] = schedule(ops)
+    order = ORDER["o"]
+    Q = {"V": g.vector, "A": g.scalar, "T": g.tensor, "G": g, "S": g.sync}
+    cnt = {"V": 0, "A": 0, "T": 0, "G": 0}
+    known = {e: {} for e in Q}
+    done = {}
+    total = {}
+    for k in order:
+        o = ops[k]
+        e = o["e"]
+        if e == "R":
+            done[k] = (o["sem"], o["n"], {})
+            total[o["sem"]] = o["n"]
+            continue
+        kn = known[e]
+        want = sorted((done[j] for j in o["h"]), key=lambda d: -len(d[2]))
+        top = {}
+        for s, v, clock in want:
+            top[s] = max(top.get(s, 0), v)
+        for s, v, clock in want:
+            if v == top[s] and kn.get(s, 0) < v:
+                Q[e].wait_ge(T.sem[s], v)
+                kn[s] = v
+                for s2, v2 in clock.items():
+                    if kn.get(s2, 0) < v2: kn[s2] = v2
+        if o["sem"] == "sent":
+            o["c"][0]()
+            done[k] = ("sent", 0, {})
+        elif o["sem"]:
+            o["c"][0]().then_inc(T.sem[o["sem"]], o["n"])
+            done[k] = (o["sem"], o["n"], dict(kn))
+            total[o["sem"]] = o["n"]
+        else:
+            for c in o["c"]:
+                c().then_inc(T.sem["c" + e], 1)
+                cnt[e] += 1
+            done[k] = ("c" + e, cnt[e], dict(kn))
+            total["c" + e] = cnt[e]
+    total["sent"] = nsent
+    for s, v in total.items():
+        g.wait_ge(T.sem[s], v)

@@ -54,9 +54,10 @@ RED = [64] * 7 + [96]
 ORDER = {}
 L_ON_ACT = ()
 FAC, GA, SC = 1.25, 1.56, 3.8
-COSTS = [(GA, SC, 0.5, 30, 110), (1.95, 3.0, 0.5, 20, 150), (1.2, 5.0, 0.6, 40, 80)]
+K_ON_DVE = ((0, 2), (0, 3))
+COSTS = [(GA, SC, 0.5, 5, 70), (1.95, 3.0, 0.5, 5, 100), (1.2, 5.0, 0.5, 10, 60)]
 WEIGHTS = [2, 1, 1]
-TRIES = 4500
+TRIES, MOVES = 300, 110000
 
 
 def collect(g, T, topo, core, nxt):
@@ -282,8 +283,11 @@ def collect(g, T, topo, core, nxt):
             mm([(T.pS[:, 0:204], T.ONE[0:1, :], T.BIA[0:1, :], True, False)], ["ONE", "BIA"], ["#S", "pS"], 204)
             b0 = 0
             for j, nb in enumerate(KCH):
-                act(T.KG[:, 256 * b0:256 * (b0 + nb)], K.indirect(NM[:, 16 * b0:16 * (b0 + nb)]), F.Copy,
-                    ["K", nmn], ["KG%d" % j], 256 * nb, GA)
+                if (n, j) in K_ON_DVE:
+                    cp(T.KG[:, 256 * b0:256 * (b0 + nb)], K.indirect(NM[:, 16 * b0:16 * (b0 + nb)]), ["K", nmn], ["KG%d" % j], 256 * nb, GA)
+                else:
+                    act(T.KG[:, 256 * b0:256 * (b0 + nb)], K.indirect(NM[:, 16 * b0:16 * (b0 + nb)]), F.Copy,
+                        ["K", nmn], ["KG%d" % j], 256 * nb, GA)
                 for b in range(b0, b0 + nb):
                     mm([(T.pS[32 * (l // 4):32 * (l // 4) + 32, 17 * b + 1:17 * b + 17],
                          T.LB[:, 40 * (16 * b + l) - 8 * (l % 4):40 * (16 * b + l) - 8 * (l % 4) + 32],
@@ -517,7 +521,91 @@ def schedule(ops):
             o2[rnd(n)] += 100.0 * (rnd(15) + rnd(15) - 14)
         s, od = score(o2)
         if s <= best: best, order, off = s, od, o2
-    return order
+    return refine(pre, order, cs)
+
+
+def refine(pre, order, cs):
+    eng, aft, pred, succ = pre
+    n = len(eng)
+    en = ["VATGSR".index(e) for e in eng]
+    P = [[[(j, a + s[4] if hard else 0.0) for j, a, hard in pred[k]] for k in range(n)] for s in COSTS]
+    ps = [set(x[0] for x in p) for p in pred]
+    ss = [set(x[0] for x in p) for p in succ]
+    seed = [99]
+
+    def rnd(m):
+        seed[0] = (seed[0] * 1103515245 + 12345) % 2 ** 31
+        return (seed[0] >> 8) % m
+
+    def score(order, p0, ends):
+        lastop = [-1] * 6
+        for i in range(p0 - 1, -1, -1):
+            e = en[order[i]]
+            if lastop[e] < 0:
+                lastop[e] = order[i]
+                if min(lastop[:4]) >= 0 and i < p0 - 60: break
+        tot, out, rest = 0.0, [], order[p0:]
+        for c, p, w, old in zip(cs, P, WEIGHTS, ends):
+            end = list(old)
+            free = [end[k] if k >= 0 else 0.0 for k in lastop]
+            free[5] = 0.0
+            for k in rest:
+                e = en[k]
+                s = free[e]
+                for j, a in p[k]:
+                    x = end[j] + a
+                    if x > s: s = x
+                s += c[k]
+                end[k] = s
+                if e != 5: free[e] = s
+            tot += w * (end[n - 1] + 0.02 * (free[0] + free[1] + free[2]))
+            out.append(end)
+        return tot, out
+
+    def critical(order, ends):
+        pos = {k: i for i, k in enumerate(order)}
+        prev, lastop = {}, {}
+        for k in order:
+            prev[k] = lastop.get(en[k], -1)
+            lastop[en[k]] = k
+        out = []
+        for c, p, end in zip(cs, P, ends):
+            k = n - 1
+            while k >= 0:
+                out.append(pos[k])
+                s, nx = end[k] - c[k] - 0.5, -1
+                for j, a in p[k]:
+                    if end[j] + a >= s: nx = j
+                if nx < 0 and en[k] != 5 and prev[k] >= 0 and end[prev[k]] >= s: nx = prev[k]
+                k = nx
+        return out
+
+    cur, ends = score(order, 0, [[0.0] * n for _ in cs])
+    best, bo, crit = cur, list(order), []
+    for it in range(MOVES):
+        if it % 64 == 0: crit = critical(order, ends)
+        i = rnd(n) if rnd(3) == 0 else min(n - 1, max(0, crit[rnd(len(crit))] + rnd(5) - 2))
+        k = order[i]
+        e = en[k]
+        if e > 3: continue
+        m, j = 1 + rnd(3), i
+        if rnd(2):
+            while j > 0 and m and order[j - 1] not in ps[k]:
+                j -= 1
+                if en[order[j]] == e: m -= 1
+        else:
+            while j < n - 1 and m and order[j + 1] not in ss[k]:
+                j += 1
+                if en[order[j]] == e: m -= 1
+        if j == i: continue
+        o2 = list(order)
+        o2.pop(i)
+        o2.insert(j, k)
+        s, e2 = score(o2, min(i, j), ends)
+        if s <= cur + 0.4 * rnd(100) * (1 - it / MOVES):
+            cur, order, ends = s, o2, e2
+            if s < best: best, bo = s, o2
+    return bo
 
 
 def rank_program(g, core, T, topo):

@@ -2,81 +2,93 @@ from concourse.mybir import AluOpType as A, ActivationFunctionType as F
 
 W, L, NB, NV, NH = 2048, 192, 12, 4, 2
 SB, PS = "sbuf", "psum"
-f32, b16, i32, u16 = "float32", "bfloat16", "int32", "uint16"
+f32, b16, i32, u16, f16 = "float32", "bfloat16", "int32", "uint16", "float16"
+BAT = ((6, 12), (0, 6))
+HB, HL, HC = 6, 96, 102
+KB = 8 * HL
 
 SCRATCH = {
-    "KW": (SB, [128, W + 2 * L], b16), "VT": (SB, [128, W], b16), "BP": (SB, [128, W // 2], i32),
-    "PG": (SB, [128, W + 16], i32), "ST": (SB, [128, NB], i32),
-    "MG": (SB, [128, 8], f32), "LB": (SB, [128, 40 * L], b16), "NL": (SB, [128, NB * 128], f32), "EQS": (SB, [128, NB * 128], b16),
-    "KG": (SB, [128, 16 * L], b16), "VG0": (SB, [128, 16 * L], f32), "VG1": (SB, [128, 16 * L], f32),
-    "NV0": (SB, [128, L], u16), "NV1": (SB, [128, L], u16), "VO": (SB, [128, NB], u16),
-    "J1": (SB, [128, NB], f32), "J2": (SB, [128, NB], i32), "J3": (SB, [128, NB], f32),
-    "PR": (SB, [128, 16 * L], f32), "SO": (SB, [128, 16 * L], f32),
+    "KW": (SB, [128, KB + W + L], b16), "VT": (SB, [128, W], b16), "BP": (SB, [128, W // 2], i32),
+    "PG": (SB, [128, KB + W + 16], i32), "ST": (SB, [128, NB], i32),
+    "LB": (SB, [128, 24 * L], b16), "KG": (SB, [128, 16 * L], b16),
     "NM0": (SB, [128, L], u16), "NM1": (SB, [128, L], u16),
-    "OMB": (SB, [128, 204], f32), "RIN": (SB, [128, 204], f32), "ON": (SB, [128, 204], f32),
-    "TT": (SB, [128, 204], f32), "CS": (SB, [128, 208], f32), "BT": (SB, [128, 204], f32),
-    "WH": (SB, [128, NB, 17], b16), "WL": (SB, [128, NB, 17], b16), "BR": (SB, [128, NB], f32),
-    "CA": (SB, [128, NB], u16), "CL0": (SB, [128, NB], u16), "CL1": (SB, [128, NB], u16), "QO": (SB, [128, NB], u16),
-    "C2": (SB, [128, NB], f32), "DJ": (SB, [128, NB], f32), "KEY": (SB, [128, 16], f32), "CW": (SB, [128, L], f32),
-    "EQ": (SB, [128, L], b16), "CUT": (SB, [128, NB], b16), "T12": (SB, [128, NB], f32), "OFF": (SB, [128, 2 * NB], u16),
-    "NZ": (SB, [128, L], f32), "MC": (SB, [128, L], f32), "VAL": (SB, [128, L], i32),
-    "QS": (SB, [128, L], b16), "VC": (SB, [128, L], f32), "RV": (SB, [128, L], f32),
-    "Z": (SB, [128, 256], f32), "P2": (SB, [128, 256], f32), "ID2": (SB, [128, 256], f32), "IB2": (SB, [128, 256], b16),
-    "PI": (SB, [128, 128], f32), "G15": (SB, [128, 128], f32), "SEL": (SB, [128, 2048], b16), "IO2": (SB, [128, W], f32),
-    "DM": (SB, [128, 17], f32), "D1": (SB, [128, 17], f32), "D2": (SB, [128, 17], f32), "R17": (SB, [128, 17], f32),
-    "CJ": (SB, [128, 204], b16), "CJA": (SB, [128, 204], b16), "CJB": (SB, [128, 204], b16), "M17": (SB, [128, 204], f32), "MK": (SB, [128, 768], f32),
-    "ONE": (SB, [128, 128], b16), "BIA": (SB, [128, 204], b16), "CM": (SB, [128, L], b16),
-    "MCL": (SB, [128, L], f32), "TRI": (SB, [128, L], b16), "RL": (SB, [128, L], f32), "TA": (SB, [128, L], f32),
-    "PP": (SB, [128, 1], i32), "PC": (SB, [128, 4], i32), "PF": (SB, [128, 4], f32), "PX": (SB, [128, 8], f32),
-    "RB": (SB, [128, NB], f32), "EI": (SB, [128, NB], i32),
-    "LO": (SB, [128, NB], u16), "NO": (SB, [128, NB], u16), "EO": (SB, [128, NB], u16), "RO": (SB, [128, NB], u16),
-    "BL": (SB, [128, NB], u16), "C15": (SB, [128, NB], u16),
-    "pS": (PS, [128, 512], f32), "pD": (PS, [128, 512], f32), "pW": (PS, [128, 512], f32), "pM": (PS, [128, 512], f32),
-    "pX": (PS, [128, 512], f32), "pE0": (PS, [128, 512], f32), "pE1": (PS, [128, 512], f32), "pE2": (PS, [128, 512], f32),
+    "NH0": (SB, [128, L], f16), "NH1": (SB, [128, L], f16), "NZ": (SB, [128, L], f16), "C3": (SB, [128, 6, 2, 16], f16),
+    "OMB0": (SB, [128, 204], f32), "OMB1": (SB, [128, 204], f32), "ON0": (SB, [128, 204], f32), "ON1": (SB, [128, 204], f32),
+    "R0": (SB, [128, HC], f32), "RIN": (SB, [128, 204], f32), "RN": (SB, [128, NB], f32),
+    "TT": (SB, [128, 204], f32), "CS": (SB, [128, 204], f32), "BT": (SB, [128, 204], f32),
+    "BR0": (SB, [128, NB], f32), "BR1": (SB, [128, NB], f32), "CUT": (SB, [128, NB], f32),
+    "CA": (SB, [128, NB], u16), "CL": (SB, [128, 2 * NB], u16), "CQ": (SB, [128, 2 * NB], u16),
+    "CAS": (SB, [128, NB], f32), "KEY": (SB, [128, 32], f32), "CW": (SB, [128, L], f32), "EQ": (SB, [128, L], b16),
+    "OFF": (SB, [128, 2 * NB], u16), "VAL": (SB, [128, L], i32), "QS": (SB, [128, L], b16),
+    "MO": (SB, [128, 6 * HB, 17], f32), "MI": (SB, [128, 6 * HC], f32), "QT": (SB, [128, 6 * HL], b16),
+    "CI": (SB, [128, 256], b16), "LAM": (SB, [128, 1024], b16), "CI3": (SB, [128, 16, 16], b16),
+    "P2": (SB, [128, 256], f32), "NP2": (SB, [128, 256], f32), "ID2": (SB, [128, 256], f32), "IB2": (SB, [128, 256], b16),
+    "C2": (SB, [128, 384], f32), "SEL": (SB, [128, 1024], b16), "IO": (SB, [128, W], f32), "IC": (SB, [128, W], f32),
+    "PD": (SB, [128, 12 * 128], b16), "BO": (SB, [128, 144], b16), "INI": (SB, [128, 3, 4, 17], b16), "IND": (SB, [128, 3, 4, 17], b16),
+    "CV": (SB, [128, 10 * 128], b16), "M17": (SB, [128, HC], f32), "CM": (SB, [128, HL], b16),
+    "MSK": (SB, [128, L], f32), "RL": (SB, [128, L], f32),
+    "PP": (SB, [128, 1], i32), "PC": (SB, [128, 8], i32), "PF": (SB, [128, 9], f32), "PX": (SB, [128, 16], f32),
+    "RB": (SB, [128, NB], f32), "LO": (SB, [128, HB], u16), "BL": (SB, [128, NB], u16),
+    "pS0": (PS, [128, 4, 128], f32), "pS1": (PS, [128, 4, 128], f32), "pW": (PS, [128, 512], f32), "pM": (PS, [128, 512], f32),
+    "pN": (PS, [128, 8, 2, 2, 16], f32), "pR": (PS, [128, 512], f32), "pE0": (PS, [128, 512], f32), "pE1": (PS, [128, 512], f32),
 }
+DEPTH = 3
+for _t in range(DEPTH):
+    SCRATCH["VG%d" % _t] = (SB, [128, 17 * L], f32)
+    SCRATCH["NV%d" % _t] = (SB, [128, L], u16)
+    SCRATCH["XA%d" % _t] = (SB, [128, NB, 17], b16)
+    SCRATCH["XB%d" % _t] = (SB, [128, NB, 17], b16)
+for _t in range(8):
+    SCRATCH["B%d" % _t] = (SB, [128, NB, 8, 16], f32)
+for _t in range(2):
+    SCRATCH["RV%d" % _t] = (SB, [128, L], f32)
 for _t in range(NV):
-    SCRATCH["AC%d" % _t] = (SB, [128, L], f32)
     SCRATCH["RP%d" % _t] = (SB, [128, L], f32)
 for _t in range(1, NV):
-    SCRATCH["MO%d" % _t] = (SB, [128, 2 * NB], f32)
-    SCRATCH["MI%d" % _t] = (SB, [128, 2 * NB], f32)
-    SCRATCH["QT%d" % _t] = (SB, [128, L], b16)
-    SCRATCH["QI%d" % _t] = (SB, [128, L], b16)
+    SCRATCH["AC%d" % _t] = (SB, [128, L], f32)
     SCRATCH["AI%d" % _t] = (SB, [128, L], f32)
 
-SEMAPHORES = (["cV", "cA", "cT", "cG", "sent"] + ["d%d" % k for k in range(9)]
-              + ["r%s%d" % (x, t) for x in "mqa" for t in range(1, NV)])
+SEMAPHORES = (["cV", "cA", "cT", "cG", "sent"] + ["d%d" % k for k in range(12)] + ["e%d" % k for k in range(16)]
+              + ["r%s%d" % (x, m) for x in "mq" for m in range(6)] + ["ra%d" % t for t in range(1, NV)])
 
-LAT = 110
-KCH = [4, 4, 3, 1]
-LOOK = 150
-RED = [64] * 7 + [96]
+SHAKE, KEEP, SPAN, BIAS, SEED = (300, 1000, 2500), 0.002, 8000, 2000, 12345
 ORDER = {}
-L_ON_ACT = ()
-FAC, GA, SC = 1.25, 1.56, 3.8
-K_ON_DVE = ((0, 2), (0, 3))
-COSTS = [(GA, SC, 0.5, 5, 70), (1.95, 3.0, 0.5, 5, 100), (1.2, 5.0, 0.5, 10, 60)]
+GA, SC = 1.56, 3.8
+KCH = {"a": ((3, "A"), (2, "V"), (1, "A")), "b": ((3, "A"), (1, "V"), (2, "A")), "c": ((2, "A"), (2, "V"), (1, "V"), (1, "A")),
+       "d": ((3, "A"), (2, "A"), (1, "A")), "x": ((2, "X"), (2, "X"), (1, "X"), (1, "X")), "y": ((3, "X"), (2, "X"), (1, "X")),
+       "z": ((2, "X"), (2, "X"), (2, "X")), "w": ((1, "X"),) * 6}
+KPLAN = "y" * 16
+HI = "V"
+SPLIT_CUT = False
+SOFT = False
+VADD = {}
+FLAT = ()
+ONTO = {(3, 3): 2, (3, 1): 0}
+ADDS = ((1, 2), (1, 2), (1, 2), ())
+ASP, VSP = True, 1
+ACC = 6000
+COSTS = [(GA, SC, 1.1, 20, 110, 1.0), (1.95, 3.0, 1.4, 10, 100, 1.2), (1.3, 4.5, 1.0, 40, 180, 0.9)]
 WEIGHTS = [2, 1, 1]
-TRIES, MOVES = 300, 110000
+TRIES, MOVES = 8000, 30000
 
 
 def collect(g, T, topo, core, nxt):
     ops = []
     last_w, readers, bank = {}, {}, {}
 
-    def op(eng, calls, r, w, cost, after=0, sem=None, n=0):
+    def op(eng, calls, r, w, cost, after=0, sem=None, n=0, dd=0):
         k = len(ops)
         hard, soft = set(), set()
         for x in r:
             if x[0] != "#" and x in last_w: hard.add(last_w[x])
         for x in w:
             if x[0] == "#": continue
-            if x in last_w: hard.add(last_w[x])
-            hard.update(readers.get(x, []))
+            for j in readers.get(x, []) + ([last_w[x]] if x in last_w else []):
+                (soft if SOFT and eng in "VA" and ops[j]["e"] == eng and not (sem or ops[j]["sem"]) else hard).add(j)
         for x in list(r) + list(w):
             if x[0] == "#":
                 for e, j in bank.setdefault(x, {}).items():
-                    (soft if e == eng else hard).add(j)
+                    (soft if e == eng != "X" else hard).add(j)
                 bank[x][eng] = k
         for x in r:
             if x[0] != "#": readers.setdefault(x, []).append(k)
@@ -91,7 +103,7 @@ def collect(g, T, topo, core, nxt):
                 if ops[j]["e"] == "T":
                     hard.discard(j)
                     soft.add(j)
-        ops.append({"e": eng, "c": calls, "h": hard, "s": soft, "t": cost, "a": after, "sem": sem, "n": n})
+        ops.append({"e": eng, "c": calls, "h": hard, "s": soft, "t": cost, "a": after, "sem": sem, "n": n, "d": dd, "w": w})
         return k
 
     V, S, PE = g.vector, g.scalar, g.tensor
@@ -117,6 +129,15 @@ def collect(g, T, topo, core, nxt):
     def act(out, in_, fn, r, w, n, f=1.0, **kw):
         op("A", [lambda: S.activation(out, in_, fn, **kw)], r, w, (n, f))
 
+    def move(e, out, in_, r, w, n, f=1.0):
+        if e == "V": cp(out, in_, r, w, n, f)
+        elif e == "A": act(out, in_, F.Copy, r, w, n, f)
+        else: op("X", [lambda q="V": V.tensor_copy(out, in_) if q == "V" else S.activation(out, in_, F.Copy)], r, w, (n, f))
+
+    def affine(out, in_, a, b, r, w, n):
+        op("X", [lambda q="V": V.tensor_scalar(out, in_, a, b, A.mult, A.add) if q == "V"
+                 else S.activation(out, in_, F.Identity, bias=b, scale=a)], r, w, (n, 1.0))
+
     def mm(lst, r, w, cyc):
         op("T", [(lambda a=a: PE.matmul(a[0], a[1], a[2], a[3], a[4])) for a in lst], r, w, (cyc, 1.0))
 
@@ -126,297 +147,383 @@ def collect(g, T, topo, core, nxt):
         else:
             op("G", [lambda: g.iota(out, pat, base, cm)], [], w, (200 + 2.5 * n, 1.0))
 
-    def asel(out, in_, pat, cm, r, w, n, base=0):
-        op("G", [lambda: g.affine_select(out, in_, pat, A.not_equal, 1.0, base, cm)], r, w, (250 + 2.5 * n, 1.0))
+    nd, ne = [0], [0]
 
-    nd = [0]
-
-    def dma(q, out, in_, r, w, after):
+    def dma(q, out, in_, r, w, dd, after=2400):
         s = "d%d" % nd[0]
         nd[0] += 1
         e = g.sync if q == "S" else g.scalar
-        op(q, [lambda: e.dma_start(out, in_)], r, w, (60, 1.0), after, s, 16)
+        return op(q, [lambda: e.dma_start(out, in_)], r, w, (60, 1.0), after, s, 16, dd)
+
+    def add_dma(out, in_, r, w, dd):
+        s = "e%d" % ne[0]
+        ne[0] += 1
+        op("G", [lambda: g.dma_start(out, in_, accum_op=A.add)], r, w, (1100, 1.0), 2000, s, 16, dd)
 
     rid, pid = topo.addr(nxt, core)
     eng = topo.engines(core, nxt)[:8]
     mask = sum(1 << e for e in eng)
     sends = [0]
 
-    def send(dst, src, sem, r, w, after):
-        k = op("G", [lambda: g.remote_dma(dst, src, T.sem[sem], T.sem.sent, pid, rid, mask)], r, ["@" + sem], (900, 1.0), 0, "sent", 0)
+    def send(dst, src, sem, r, w, dd):
+        op("G", [lambda: g.remote_dma(dst, src, T.sem[sem], T.sem.sent, pid, rid, mask)], r, ["@" + sem], (900, 1.0), 2600, "sent", 0, dd)
         sends[0] += len(eng)
-        op("R", [], ["@" + sem], w, (0, 1.0), after, sem, len(eng))
-        return k
+        op("R", [], ["@" + sem], w, (0, 1.0), 0, sem, len(eng))
 
-    K = T.KW[:, L:L + W]
-    qA, qB = T.KW[:, 0:L], T.KW[:, L + W:L + W + L]
+    K = T.KW[:, KB:KB + W]
     h = W // 4
-    dma("S", T.BP[:, 0:h], T.bp[:, 0:h], [], ["BPa"], 3600)
-    dma("A", T.BP[:, h:2 * h], T.bp[:, h:2 * h], [], ["BPb"], 4600)
-    dma("S", T.ST[:], T.st[:], ["@0"], ["ST"], 4600)
-    dma("A", K, T.kt[:], ["@1"], ["K"], 6600)
-    dma("S", T.VT[:], T.vt[:], ["@2"], ["VT"], 8600)
-    ops[2]["s"].add(0)
-    ops[3]["s"].add(1)
-    ops[4]["s"].add(2)
+    k0 = dma("S", T.BP[:, 0:h], T.bp[:, 0:h], [], ["BPa"], 1000)
+    k1 = dma("A", T.BP[:, h:2 * h], T.bp[:, h:2 * h], [], ["BPb"], 1000)
+    ops[dma("S", T.ST[:], T.st[:], [], ["ST"], 100)]["s"].add(k0)
+    ops[dma("A", K, T.kt[:], [], ["K"], 2000)]["s"].add(k1)
+    ops[dma("S", T.VT[:], T.vt[:], [], ["VT"], 2000)]["s"].update((2, 3))
     for j, nm in enumerate(("BPa", "BPb")):
-        ts(T.PG[:, j * h:(j + 1) * h], T.BP[:, j * h:(j + 1) * h], W - 1, None, A.bitwise_and, None, [nm], ["PG%d" % j], h)
-        ts(T.PG[:, (2 + j) * h:(3 + j) * h], T.BP[:, j * h:(j + 1) * h], 11, None, A.logical_shift_right, None, [nm], ["PG%d" % (2 + j)], h)
-    ms(T.PG[:, W:W + 16], 0, ["PG4"], 16)
+        bp = T.BP[:, j * h:(j + 1) * h]
+        ts(T.PG[:, KB + j * h:KB + (j + 1) * h], bp, W - 1, None, A.bitwise_and, None, [nm], ["PG%d" % j], h)
+        ts(T.PG[:, KB + (2 + j) * h:KB + (3 + j) * h], bp, 11, None, A.logical_shift_right, None, [nm], ["PG%d" % (2 + j)], h)
+    ms(T.PG[:, KB + W:KB + W + 16], 0, ["PG4"], 16)
+    iota(T.PG[:, 0:KB], [[0, KB]], 0, 0, ["PGz"], KB, False)
     PGR = ["PG%d" % j for j in range(4)]
     iota(T.PP[:], [[0, 1]], 0, 1, ["PP"], 1, False)
     iota(T.RB[:], [[1, NB]], 0, 0, ["RB"], NB)
-    iota(T.R17[:], [[1, 17]], 0, 0, ["R17"], 17)
-    iota(T.EI[:], [[128, NB]], 0, 1, ["EI"], NB, False)
+    iota(T.CI[:], [[0, 2], [1, 128]], 0, 0, ["CI"], 256)
+    iota(T.CV[0:32, 0:256], [[-HL, 2], [0, 128]], -HL, 0, ["CV0", "CV1"], 256)
+    iota(T.CV[0:32, 1024:1280], [[HL, 2], [0, 128]], W, 0, ["CV8", "CV9"], 256)
+    iota(T.CV[0:32, 256:1024], [[-HL, 6], [0, 128]], -3 * HL, 0, ["CV%d" % j for j in range(2, 8)], 768)
+    iota(T.LAM[:], [[1, 64], [0, 16]], 0, 0, ["LAM"], 1024)
     iota(T.RL[:], [[0, NB], [1, 16]], 0, 0, ["RL"], L)
-    ms(T.Z[:], 0.0, ["Z"], 256)
-    asel(T.ID2[:], T.Z[:], [[0, 2], [-1, 128]], 1, ["Z"], ["ID2"], 256)
-    asel(T.P2[:], T.Z[:], [[0, 2], [-1, 8], [-8, 16]], 1, ["Z"], ["P2"], 256)
-    iota(T.SEL[:], [[0, 2048]], 0, 0, ["SEL"], 2048)
-    asel(T.SEL[:], T.SEL[:], [[-8, 16], [-1, 8], [0, 16]], 1, ["SEL"], ["SEL"], 2048)
-    iota(T.IO2[:], [[2, W]], 0, 0, ["IO2"], W)
-    asel(T.PI[:], T.Z[:, 0:128], [[-1, 16], [-16, 8]], 1, ["Z"], ["PI"], 128)
-    for j, (o, c) in enumerate(((A.bitwise_and, 15), (A.logical_shift_right, 4), (A.bitwise_and, 3), (A.logical_shift_right, 3))):
+    iota(T.CI3[:], [[8, 16], [0, 2], [1, 8]], 0, 0, ["CI3"], 256)
+    iota(T.IO[:], [[1, W]], 2 * W, 0, ["IO"], W)
+    iota(T.IC[0:32, :], [[1, W]], 0, 0, ["IC"], W)
+    dma("S", T.IO[15::16, :], T.IC[0:8, :], ["IC"], ["IO"], 300)
+    bits = ((A.bitwise_and, 15), (A.logical_shift_right, 4), (A.logical_shift_right, 3), (A.bitwise_and, 7),
+            (A.logical_shift_right, 5), (A.bitwise_and, 16), (A.bitwise_and, 63), (A.bitwise_and, 3))
+    for j, (o, c) in enumerate(bits):
         ts(T.PC[:, j:j + 1], T.PP[:], c, None, o, None, ["PP"], ["PC%d" % j], 1)
-    cp(T.PF[:], T.PC[:], ["PC0", "PC1", "PC2", "PC3"], ["PF"], 4)
-    lf, gf, l4, lc = [T.PF[:, j:j + 1] for j in range(4)]
-    X = [T.PX[:, j:j + 1] for j in range(8)]
-    ts(X[0], lf, 8.0, gf, A.mult, A.add, ["PF"], ["X0"], 1)
-    ts(X[1], lf, -1.0, float(-W), A.mult, A.add, ["PF"], ["X1"], 1)
-    ts(X[2], lf, 40.0, gf, A.mult, A.add, ["PF"], ["X2"], 1)
-    ts(T.MG[:], T.RB[:, 0:8], gf, -1.0 / 1024, A.is_equal, A.mult, ["RB", "PF"], ["MG"], 8)
-    ts(X[3], lf, 12.0, None, A.mult, None, ["PF"], ["X3"], 1)
+    iota(T.PF[:, 8:9], [[0, 1]], 0, 1, ["PF"], 1)
+    cp(T.PF[:, 0:8], T.PC[:], ["PC%d" % j for j in range(8)] + ["PF"], ["PF"], 8)
+    lf, gf, lc, gc, pa, up, k64, r4, pf = [T.PF[:, j:j + 1] for j in range(9)]
+    X = [T.PX[:, j:j + 1] for j in range(16)]
+    ts(X[12], r4, 2.0, -8.0, A.is_ge, A.mult, ["PF"], ["X12"], 1)
+    ts(X[13], r4, 8.0, gf, A.mult, A.add, ["PF"], ["X13"], 1)
+    ts(X[0], lf, 24.0, X[12], A.mult, A.add, ["PF", "X12"], ["X0"], 1)
+    ts(X[0], X[0], X[13], None, A.add, None, ["X0", "X13"], ["X0"], 1)
+    ts(X[1], gc, 16.0, lc, A.mult, A.add, ["PF"], ["X1"], 1)
+    ts(X[2], lf, 4.0, pa, A.mult, A.add, ["PF"], ["X2"], 1)
+    ts(X[2], X[2], 2.0, None, A.mult, None, ["X2"], ["X2"], 1)
+    ts(X[3], pa, 32.0, lf, A.mult, A.add, ["PF"], ["X3"], 1)
     ts(X[4], lf, float(W), None, A.add, None, ["PF"], ["X4"], 1)
     ts(X[5], lf, 15.0, None, A.is_lt, None, ["PF"], ["X5"], 1)
-    ts(X[6], lc, -8.0, None, A.mult, None, ["PF"], ["X6"], 1)
-    ts(T.LO[:], T.RB[:], 640.0, X[2], A.mult, A.add, ["RB", "X2"], ["LO"], NB)
-    ts(T.NO[:], T.RB[:], 128.0, X[0], A.mult, A.add, ["RB", "X0"], ["NO"], NB)
-    ts(T.RO[:], T.RB[:], X[3], None, A.add, None, ["RB", "X3"], ["RO"], NB)
-    ts(T.C15[:], T.RB[:], 17.0, 15.0, A.mult, A.add, ["RB"], ["C15"], NB)
-    ts(T.J1[:], T.RB[:], 16.0, lf, A.mult, A.add, ["RB", "PF"], ["J1"], NB)
-    ts(T.J3[:], T.J1[:], -5.5, 1.0 / 12, A.add, A.mult, ["J1"], ["J3"], NB)
-    cp(T.J2[:], T.J3[:], ["J3"], ["J2"], NB)
-    ts(T.J3[:], T.J2[:], -1528.0, gf, A.mult, A.add, ["J2", "PF"], ["J3"], NB)
-    ts(T.J1[:], T.J1[:], 128.0, None, A.mult, None, ["J1"], ["J1"], NB)
-    tt(T.J1[:], T.J1[:], T.J3[:], A.add, ["J1", "J3"], ["J1"], NB)
-    cp(T.VO[:], T.J1[:], ["J1"], ["VO"], NB)
+    ts(X[6], lf, 15.0, 8192.0, A.is_equal, A.mult, ["PF"], ["X6"], 1)
+    ts(X[7], gf, 16.0, 15.0, A.mult, A.add, ["PF"], ["X7"], 1)
+    for l2 in range(2):
+        ts(X[8 + l2], up, 16.0 * l2, None, A.is_equal, None, ["PF"], ["X%d" % (8 + l2)], 1)
+        ts(X[10 + l2], up, 16.0 * l2, -1.0, A.is_equal, A.mult, ["PF"], ["X%d" % (10 + l2)], 1)
+    ts(T.LO[:], T.RB[:, 0:HB], 384.0, X[0], A.mult, A.add, ["RB", "X0"], ["LO"], HB)
     cp(T.BL[:], T.RB[:], ["RB"], ["BL"], NB)
-    cp(T.EO[:], T.EI[:], ["EI"], ["EO"], NB)
-    ts(T.D1[:], T.R17[:], lf, None, A.is_equal, None, ["R17", "PF"], ["D1"], 17)
-    ts(T.D2[:], T.R17[:], -1.0, lf, A.add, A.is_equal, ["R17", "PF"], ["D2"], 17)
-    tt(T.DM[:], T.D1[:], T.D2[:], A.subtract, ["D1", "D2"], ["DM"], 17, 2)
-    for nm in ("CJ", "CJA", "CJB"):
-        ms(T[nm][:], 0.0, [nm], 102)
-    ts(T.CJ[:, 16::17], T.RB[:], 0.0, lc, A.mult, A.add, ["RB", "PF"], ["CJ"], NB)
-    ts(T.CJA[:, 16::17], T.RB[:], 16.0, float(-L), A.mult, A.add, ["RB"], ["CJA"], NB)
-    ts(T.CJB[:, 16::17], T.RB[:], 16.0, float(W), A.mult, A.add, ["RB"], ["CJB"], NB)
-    ms(T.LB[:, 0:2048], 0.0, ["LBz0"], 1024)
-    ms(T.LB[:, 2048:5632], 0.0, ["LBz1"], 1792)
-    act(T.NL[:], T.LB[:, 0:1536], F.Copy, ["LBz0"], ["NLz"], 1536)
-    act(T.LB[:, 5632:7680], T.LB[:, 0:2048], F.Copy, ["LBz0"], ["LBz2"], 2048)
-    LBS = ["LB%d" % j for j in range(8)]
-    act(T.MK[:], T.LB[:, 0:768], F.Identity, ["LBz0"], ["MK"], 768, bias=1.0)
-    act(T.M17[:], T.LB[:, 0:204], F.Identity, ["LBz0"], ["M17"], 204, bias=1.0)
-    act(T.RIN[:], T.LB[:, 0:204], F.Copy, ["LBz0"], ["RIN"], 204)
-    ms(T.M17[:, 0::17], 0.0, ["M17"], NB)
-    ms(T.MK[:, 0::16], 0.0, ["MK"], 48)
-    ms(T.ONE[:], 1.0, ["ONE"], 64)
-    ms(T.BIA[:], 1712.0 / 2048, ["BIA"], 102)
-    ms(T.BIA[:, 0::17], 0.0, ["BIA"], 6)
-    ms(T.CM[:], -1.0 / 1024, ["CM"], 96)
-    ms(T.RIN[:, 0::17], 1.0, ["RIN"], NB)
-    ms(T.BT[:, 200:204], 0.0, ["BT"], 4)
-    ms(T.CS[:, 204:208], 0.0, ["CSp"], 4)
-    ms(T.KEY[:], 0.0, ["KEY"], 16)
-    ms(T.EQS[:], 0.0, ["EQS"], 768)
-    ts(T.MCL[:], T.RL[:], lc, None, A.is_equal, None, ["RL", "PF"], ["MCL"], L)
-    ts(T.TA[:], T.RL[:], lf, -2.0, A.is_gt, A.mult, ["RL", "PF"], ["TA"], L)
-    ts(T.NZ[:], T.RL[:], lf, None, A.is_ge, None, ["RL", "PF"], ["NZ"], L)
-    tt(T.TRI[:], T.TA[:], T.NZ[:], A.add, ["TA", "NZ"], ["TRI"], L, 2)
-    act(T.IB2[:], T.ID2[:], F.Copy, ["ID2"], ["IB2"], 256)
-    ms(T.G15[:], 0.0, ["G15"], 128)
-    cp(X[7], T.PP[:], ["PP"], ["X7"], 1)
-    ts(T.T12[:, 0:8], T.RB[:, 0:8], X[6], X[7], A.subtract, A.is_equal, ["RB", "X6", "X7"], ["T12"], 8)
-    cp(T.G15[:, 15::16], T.T12[:, 0:8], ["T12"], ["G15"], 8)
 
-    def perm(t):
-        return T.P2[:, 128 - 16 * t:256 - 16 * t]
+    def pd(kind, l2, g2):
+        j = 4 * kind + 2 * l2 + g2
+        return T.PD[:, 128 * j:128 * j + 128]
 
-    pM = [T.pM[:, 16 * j:16 * j + NB] for j in range(8)]
-    Rs, w1, wv = T.pW[:, 0:204], T.pW[:, 256:460], T.pD[:, 256:460]
-    slot = [0]
-    for t in range(NV):
-        last = t == NV - 1
-        AC, RP = T["AC%d" % t], T["RP%d" % t]
-        if t == 0:
-            cp(T.CA[:], T.ST[:], ["ST"], ["CA"], NB)
-            act(qA, K.indirect(T.CA[:]), F.Copy, ["K", "CA"], ["qA"], L, GA)
+    for l2 in range(2):
+        for g2 in range(2):
+            for kind in range(3):
+                s0 = 128 - (16 * g2 if kind == 2 else g2)
+                x, m = 3 if kind == 2 else 2, (10 if kind == 1 else 8) + l2
+                ts(pd(kind, l2, g2), T.CI[:, s0:s0 + 128], X[x], X[m], A.is_equal, A.mult, ["CI", "X%d" % x, "X%d" % m],
+                   ["PD%d%d%d" % (kind, l2, g2)], 64)
+    PDS = [["PD%d%d%d" % (kind, l2, g2) for l2 in range(2) for g2 in range(2)] for kind in range(3)]
+    ts(T.IB2[:], T.CI[:], pf, None, A.is_equal, None, ["CI", "PF"], ["IB2"], 128)
+    ts(T.P2[:], T.CI[:], X[1], None, A.is_equal, None, ["CI", "X1"], ["P2"], 256)
+    act(T.NP2[:], T.P2[:], F.Identity, ["P2"], ["NP2"], 256, scale=-1.0)
+    act(T.ID2[:], T.IB2[:], F.Copy, ["IB2"], ["ID2"], 256)
+    for u in range(1, NV):
+        ts(T.C2[:, 128 * (u - 1):128 * u], T.CI3[:, :, 8 - u:16 - u], pf, None, A.is_equal, None, ["CI3", "PF"], ["C2%d" % u], 128)
+    ts(T.SEL[:], T.LAM[:], k64, None, A.is_equal, None, ["LAM", "PF"], ["SEL"], 512)
+    ts(T.BO[:], T.CI[:, 0:144], X[7], X[5], A.is_equal, A.mult, ["CI", "X7", "X5"], ["BO"], 72)
+    ts(T.MSK[:], T.RL[:], lf, 0.5, A.is_le, A.subtract, ["RL", "PF"], ["MSK"], L)
+    act(T.MSK[:], T.MSK[:], F.Identity, ["MSK"], ["MSK"], L, scale=1.0 / W)
+    ms(T.LB[:, 0:1152], 0.0, ["LBz0"], 576)
+    for j in range(1, 4):
+        act(T.LB[:, 1152 * j:1152 * (j + 1)], T.LB[:, 0:1152], F.Copy, ["LBz0"], ["LBz%d" % j], 1152)
+    LBZ = (["LBz2", "LBz3"], ["LBz0", "LBz1"])
+    ms(T.INI[:], 0.0, ["INI"], 102)
+    ms(T.INI[:, :, 0:2, 1:17], 1712.0 / 1024, ["INI"], 48)
+    ts(T.INI[:, :, 2:4, 16], T.RB[:, 0:HB], 16.0, lc, A.mult, A.add, ["RB", "PF"], ["INI"], HB)
+    ms(T.IND[0:32], 0.0, ["IND"], 102)
+    ms(T.IND[0:32, :, 2:4, 16], 1.0, ["IND"], HB)
+    ms(T.CM[:], -1.0 / 1024, ["CM"], 48)
+    act(T.M17[:], T.LB[:, 0:HC], F.Identity, ["LBz0"], ["M17"], HC, bias=1.0)
+    ms(T.M17[:, 0::17], 0.0, ["M17"], HB)
+    act(T.R0[:], T.LB[:, 0:HC], F.Copy, ["LBz0"], ["R0"], HC)
+    ms(T.R0[:, 0::17], 1.0, ["R0"], HB)
+    act(T.RIN[:], T.LB[:, 0:204], F.Copy, ["LBz0"], ["RIN0", "RIN1"], 204)
+    act(T.BT[:], T.LB[:, 0:204], F.Copy, ["LBz0"], ["BT0", "BT1"], 204)
+    act(T.MO[:], T.LB[:, 0:612], F.Copy, ["LBz0"], ["MO%d" % m for m in range(6)], 612)
+    ms(T.KEY[:], 0.0, ["KEY0", "KEY1"], 32)
+
+    def rot(M, u):
+        return M[:, 128 - 16 * u:256 - 16 * u]
+
+    slot, first = [0], []
+
+    def chain(t, hop, x):
+        n, last = t * NH + hop, t == NV - 1
+        p = n % 2
+        b0, b1 = BAT[x]
+        j0, j1, c0, c1, k0, k1 = 16 * b0, 16 * b1, b0 // 2, b1 // 2, 17 * b0, 17 * b1
+        s = str(x)
+        ps = "%d%d" % (p, x)
+        m = 2 * t + x
+        q0 = HL * (7 - m)
+        qa, qb = T.KW[:, q0:q0 + HL], T.KW[:, KB + W + HL * x:KB + W + HL * (x + 1)]
+        pS, bS = T["pS" + s], "#S" + s
+        NM, NHh = T["NM%d" % p], T["NH%d" % p]
+        OMB, ON, BR = T["OMB%d" % p][:, k0:k1], T["ON%d" % p][:, k0:k1], T["BR%d" % hop][:, b0:b1]
+        if hop == 0:
+            CA = T.CA[:, b0:b1]
+            if t == 0:
+                cp(CA, T.ST[:, b0:b1], ["ST"], ["CA" + s], HB)
+                move("X", qa, K.indirect(CA), ["K", "CA" + s], ["q%d" % m], HL, GA)
+                rin, rn = T.R0[:], "R0"
+                ts(T.CAS[:, b0:b1], T.ST[:, b0:b1], 1.0 / 4096, 1.0, A.mult, A.add, ["ST"], ["CAS" + s], HB)
+            else:
+                rin, rn = T.MI[:, HC * (m - 2):HC * (m - 1)], "MI%d" % (m - 2)
+                mc = T.MI[:, HC * (m - 2) + 1:HC * (m - 1):17]
+                ts(CA, mc, -1.0, None, A.mult, None, [rn], ["CA" + s], HB)
+                if not last:
+                    affine(T.CAS[:, b0:b1], mc, -1.0 / 4096, 1.0, [rn], ["CAS" + s], HB)
+            cl, cln, q, qn, cv = CA, "CA" + s, qa, "q%d" % m, m
         else:
-            MI, QI = T["MI%d" % t], T["QI%d" % t]
-            cp(T.CA[:], MI[:, 0:NB], ["MI%d" % t], ["CA"], NB)
-            mm([(pM[6], T.PI[:], MI[:, NB:2 * NB], True, True)], ["MI%d" % t, "PI"], ["#M", "pM6"], 256)
-            act(T.RIN[:, 0::17], pM[6], F.Copy, ["#M", "pM6"], ["RIN"], NB)
-            act(qA, QI[:], F.Copy, ["QI%d" % t], ["qA"], L)
-        for hop in range(NH):
-            n = t * NH + hop
-            NM, nmn = T["NM%d" % (n % 2)], "NM%d" % (n % 2)
-            VG, vgn = T["VG%d" % (n % 2)], "VG%d" % (n % 2)
-            cl, cln = (T.CA, "CA") if hop == 0 else (T.CL0, "CL0")
-            cp(NM[:], T.PG[:, 0:W].indirect(cl[:]), PGR + [cln], [nmn], L, GA)
-            if hop == 1: q, qn = qB, "qB"
-            elif t == 0: q, qn = qA, "qA"
-            else: q, qn = T["QI%d" % t][:], "QI%d" % t
-            if n in L_ON_ACT:
-                for gg in range(8):
-                    act(T.LB[:, gg::40], q, F.Identity, [qn, "MG"], ["LB%d" % gg], L, scale=T.MG[:, gg:gg + 1])
-            else:
-                tt(T.LB[:].indirect(T.LO[:]), q, T.CM[:], A.mult, [qn, "CM", "LO", "LBz1", "LBz2"], LBS + ["LBz0"], L, SC)
-            cp(T.NL[:].indirect(T.NO[:]), NM[:], [nmn, "NO", "NLz"], ["NL"], L, SC)
-            NMV, nvn = T["NV%d" % (n % 2)], "NV%d" % (n % 2)
-            cp(NMV[:], T.NL[:].indirect(T.VO[:]), ["NL", "VO"], [nvn], L, GA)
-            CJ, cjn = (T.CJA, "CJA") if hop == 0 else (T.CJB, "CJB")
-            mm([(T.pD[:, 0:204], T.IB2[:, 0:128], T.CJ[:], True, False)], ["IB2", "CJ"], ["#D", "pD"], 204)
-            for b0 in range(0, NB, 3):
-                mm([(T.pD[:, 17 * b:17 * b + 17], T.NL[:, 128 * b:128 * b + 128], T.DM[:], False, False)
-                    for b in range(b0, b0 + 3)], ["NL", "DM"], ["#D", "pD"], 768)
-            mm([(T.pD[:, 0:204], T.ONE[0:1, :], CJ[0:1, :], False, True)], ["ONE", cjn], ["#D", "pD"], 204)
-            mm([(T.pS[:, 0:204], T.ONE[0:1, :], T.BIA[0:1, :], True, False)], ["ONE", "BIA"], ["#S", "pS"], 204)
-            b0 = 0
-            for j, nb in enumerate(KCH):
-                if (n, j) in K_ON_DVE:
-                    cp(T.KG[:, 256 * b0:256 * (b0 + nb)], K.indirect(NM[:, 16 * b0:16 * (b0 + nb)]), ["K", nmn], ["KG%d" % j], 256 * nb, GA)
-                else:
-                    act(T.KG[:, 256 * b0:256 * (b0 + nb)], K.indirect(NM[:, 16 * b0:16 * (b0 + nb)]), F.Copy,
-                        ["K", nmn], ["KG%d" % j], 256 * nb, GA)
-                for b in range(b0, b0 + nb):
-                    mm([(T.pS[32 * (l // 4):32 * (l // 4) + 32, 17 * b + 1:17 * b + 17],
-                         T.LB[:, 40 * (16 * b + l) - 8 * (l % 4):40 * (16 * b + l) - 8 * (l % 4) + 32],
-                         T.KG[:, 16 * (16 * b + l):16 * (16 * b + l) + 16],
-                         False, False) for l in range(16)], LBS + ["KG%d" % j], ["#S", "pS"], 512)
-                b0 += nb
-            mm([(T.pS[:, 0:204], T.ONE[0:1, :], T.BIA[0:1, :], False, True)], ["ONE", "BIA"], ["#S", "pS"], 204)
-            if hop == 0 and not last:
-                act(T.NZ[:], T.NL[:].indirect(T.NO[:]), F.Identity, ["NL", "NO", "X5"], ["NZ"], L, GA, scale=X[5])
-                if t == 0:
-                    ts(T.C2[:], T.CA[:], 2.0, None, A.mult, None, ["CA"], ["C2"], NB)
-                    ts(T.DJ[:], T.CA[:], X[4], None, A.subtract, None, ["CA", "X4"], ["DJ"], NB)
-                else:
-                    act(T.C2[:], MI[:, 0:NB], F.Identity, ["MI%d" % t], ["C2"], NB, scale=2.0)
-                    act(T.DJ[:], MI[:, 0:NB], F.Identity, ["MI%d" % t, "X1"], ["DJ"], NB, bias=X[1])
-                act(T.CW[:], T.IO2[:].indirect(T.CA[:]), F.Copy, ["IO2", "CA"], ["CW"], L, GA)
-            ts(T.OMB[:], T.pS[:, 0:204], 0.0625, 1.0, A.max, A.min, ["#S", "pS"], ["OMB"], 204)
-            scan(Rs, T.OMB[:], T.RIN[:], A.mult, A.max, ["OMB", "RIN"], ["Rs"], 204)
-            ts(T.ON[:], Rs, 0.0625, None, A.is_ge, None, ["Rs"], ["ON"], 204)
-            ts(T.BR[:], T.pW[:, 16:204:17], 0.0625, None, A.is_lt, None, ["Rs"], ["BR"], NB)
-            tt(T.RIN[:, 0::17], T.pW[:, 16:204:17], T.BR[:], A.max, ["Rs", "BR"], ["RIN"], NB)
-            if not last:
-                mm([(pM[0], perm(0), T.BR[:], True, True)], ["P2", "BR"], ["#M", "pM0"], 256)
-                if hop == 0:
-                    tt(T.KEY[:, 0:NB], pM[0], T.C2[:], A.add, ["#M", "pM0", "C2"], ["KEY"], NB)
-                else:
-                    cp(T.CUT[:], pM[0], ["#M", "pM0"], ["CUT"], NB)
-            tt(T.TT[:], T.pD[:, 0:204], T.ON[:], A.mult, ["#D", "pD", "ON"], ["TT"], 204)
-            scan(T.CS[:, 0:204], T.M17[:], T.TT[:], A.mult, A.add, ["M17", "TT"], ["CS"], 204)
-            cn, qo = T.CS[:, 15:204:17], T.CS[:, 16:204:17]
-            if hop == 0:
-                mm([(pM[1], perm(0), cn, True, True), (pM[2], perm(0), qo, True, True)], ["P2", "CS"], ["#M", "pM1", "pM2"], 512)
-                cp(T.CL0[:], pM[1], ["#M", "pM1"], ["CL0"], NB)
-                ts(T.QO[:], pM[2], float(L), None, A.add, None, ["#M", "pM2"], ["QO"], NB)
-                act(qB, T.KW[:, 0:L + W].indirect(T.QO[:]), F.Copy, ["K", "qA", "QO"], ["qB"], L, GA)
-                if not last:
-                    tt(T.EQ[:], T.KEY[:].indirect(T.BL[:]), T.CW[:], A.is_equal, ["KEY", "BL", "CW"], ["EQ"], L, GA)
-                    tt(T.EQS[:].indirect(T.EO[:]), T.EQ[:], T.TRI[:], A.mult, ["EQ", "TRI", "EO"], ["EQS"], L, SC)
-            elif last:
-                mm([(pM[1], perm(0), cn, True, True)], ["P2", "CS"], ["#M", "pM1"], 256)
-                cp(T.CL1[:], pM[1], ["#M", "pM1"], ["CL1"], NB)
-            else:
-                u = t + 1
-                MO, QT = T["MO%d" % u], T["QT%d" % u]
-                mm([(T.pX[:, 400 + b:401 + b], T.EQS[:, 128 * b:128 * b + 128], T.CUT[:, b:b + 1], True, True) for b in range(NB)],
-                   ["EQS", "CUT"], ["#X", "pXe"], 768)
-                mm([(T.pM[:, 60:72], perm(u), T.RIN[:, 0::17], True, True), (T.pM[:, 48:60], perm(u), cn, True, True),
-                    (pM[2], perm(0), qo, True, True), (pM[1], perm(0), cn, True, True)],
-                   ["P2", "CS", "RIN"], ["#M", "pM1", "pM2", "pM3"], 1024)
-                cp(MO[:], T.pM[:, 48:72], ["#M", "pM3"], ["MO%d" % u], 2 * NB)
-                send(T["MI%d" % u][:], MO[:], "rm%d" % u, ["MO%d" % u], ["MI%d" % u], 3000)
-                cp(T.QO[:], pM[2], ["#M", "pM2"], ["QO"], NB)
-                cp(T.CL1[:], pM[1], ["#M", "pM1"], ["CL1"], NB)
-                tt(T.T12[:], T.pX[:, 400:412], T.DJ[:], A.mult, ["#X", "pXe", "DJ"], ["T12"], NB)
-                ts(T.OFF[:, 0::2], T.T12[:], 0.0, X[4], A.min, A.add, ["T12", "X4"], ["OFF"], NB)
-                tt(T.MC[:], T.CS[:].indirect(T.C15[:]), T.MCL[:], A.mult, ["CS", "CSp", "C15", "MCL"], ["MC"], L, GA)
-                mm([(T.pX[:, 0:L], T.G15[:], T.MC[:], True, True)], ["G15", "MC"], ["#X", "pXa"], 768)
-                tt(T.VAL[:], T.pX[:, 0:L], T.NZ[:], A.add, ["#X", "pXa", "NZ"], ["VAL"], L)
-                for b in range(NB - 1, -1, -1):
-                    cp(T.PG[:].indirect(T.OFF[:, 2 * b:2 * b + 1]), T.VAL[:, 16 * b:16 * b + 16], ["VAL", "OFF"], PGR + ["PG4"], 16, SC)
-                act(T.QS[:], T.KW[:, L:].indirect(T.QO[:]), F.Copy, ["K", "qB", "QO"], ["QS"], L, GA)
-                mm([(T.pX[:, L:2 * L], T.IB2[:, 128 - 16 * u:256 - 16 * u], T.QS[:], True, True)], ["IB2", "QS"], ["#X", "pXb"], L)
-                act(QT[:], T.pX[:, L:2 * L], F.Copy, ["#X", "pXb"], ["QT%d" % u], L)
-                send(T["QI%d" % u][:], QT[:], "rq%d" % u, ["QT%d" % u], ["QI%d" % u], 3400)
-            for j in range(4):
-                act(VG[:, 768 * j:768 * (j + 1)], T.VT[:].indirect(NMV[:, 48 * j:48 * (j + 1)]), F.Sigmoid,
-                    ["VT", nvn], ["%s_%d" % (vgn, j)], 768, GA)
-            act(T.BT[:, 0:203], T.OMB[:, 1:204], F.Identity, ["OMB"], ["BT"], 204, bias=1.0, scale=-1.0)
-            tt(w1, Rs, T.ON[:], A.mult, ["Rs", "ON"], ["w1"], 204)
-            tt(wv, w1, T.BT[:], A.mult, ["w1", "BT"], ["#D", "wv"], 204)
-            if hop == 1:
-                cp(T.pD[:, 272:460:17], T.RIN[:, 0::17], ["RIN", "wv"], ["#D", "wv"], NB)
-            act(T.WH[:], wv, F.Copy, ["#D", "wv"], ["WH"], 204)
-            tt(T.WL[:], wv, T.WH[:], A.subtract, ["#D", "wv", "WH"], ["WL"], 204)
-            acn = "AC%d" % t
-            if hop == 1:
-                act(T.VC[:], T.VT[:].indirect(T.CL1[:]), F.Sigmoid, ["VT", "CL1"], ["VC"], L, GA)
-                lst = []
-                for l in range(16):
-                    o = T.pX[:, l:L:16]
-                    sel = T.SEL[:, 128 * l:128 * l + 128]
-                    lst += [(o, sel, T.WH[:, :, 16], True, False), (o, sel, T.WL[:, :, 16], False, True)]
-                mm(lst, ["SEL", "WH", "WL"], ["#X", "pXa"], 2048)
-                tt(T.RV[:], T.pX[:, 0:L], T.VC[:], A.mult, ["#X", "pXa", "VC"], ["RV"], L)
-            nr = RED[n]
-            lo = 16 * nr
-            sos = []
-            for l0 in range(0, 16, 2):
-                e = slot[0] % 3
+            rin, rn = T.RIN[:, k0:k1], "RIN" + s
+            cl, cln, q, qn, cv = T.CL[:, NB * x:NB * x + HB], "CL" + s, qb, "qb" + s, 8 + x
+        nm = NM[:, j0:j1]
+        cp(nm, T.PG[:, (q0 if hop else KB):KB + W].indirect(cl), PGR + [cln, "PGz"], ["NM" + ps], HL, GA)
+        tt(T.LB[:, 24 * j0:24 * j1].indirect(T.LO[:]), q, T.CM[:], A.mult, [qn, "CM", "LO"], LBZ[x] + ["LB" + s], HL, SC)
+        cp(NHh[:, j0:j1], nm, ["NM" + ps], ["NH" + ps], HL // 2)
+        op("V", [lambda: V.transpose(T.C3[:, c0:c1], NHh[:, j0:j1])], ["NH" + ps], ["C3" + s], (HL // 2, 1.0))
+        mm([(pS[:, 0:3, 0:68], T.IB2[:, 0:128], T.INI[:], True, False)], ["IB2", "INI"], [bS, "pS" + s], 204)
+        mm([(pS[:, 0:3, 34 + 17 * l2 + kind:50 + 17 * l2 + kind], pd(kind, l2, g2), T.C3[:, c0:c1, g2, :], False, False)
+            for l2 in range(2) for g2 in range(2) for kind in range(2)], PDS[0] + PDS[1] + ["C3" + s], [bS, "pS" + s], 512)
+        b = b0
+        for nb, e in KCH[KPLAN[2 * n + x]]:
+            kn = ["KG%d" % j for j in range(b, b + nb)]
+            move(e, T.KG[:, 256 * b:256 * (b + nb)], K.indirect(NM[:, 16 * b:16 * (b + nb)]), ["K", "NM" + ps], kn, 256 * nb, GA)
+            for bb in range(b, b + nb):
+                c, l2 = (bb - b0) // 2, bb % 2
+                mm([(pS[32 * (l // 4):32 * (l // 4) + 32, c, 17 * l2 + 1:17 * l2 + 17],
+                     T.LB[:, 24 * (16 * bb + l) - 8 * (l % 4 // 2):24 * (16 * bb + l) - 8 * (l % 4 // 2) + 32],
+                     T.KG[:, 16 * (16 * bb + l):16 * (16 * bb + l) + 16],
+                     False, False) for l in range(16)], ["LB" + s, "KG%d" % bb], [bS, "pS" + s], 512)
+            b += nb
+        mm([(pS[:, 0:3, 0:68], T.CV[0:1, 128 * cv:128 * cv + 128], T.IND[0:1], False, True)], ["CV%d" % cv, "IND"], [bS, "pS" + s], 204)
+        w0 = 204 * p
+        Rs, R16 = T.pW[:, w0 + k0:w0 + k1], T.pW[:, w0 + k0 + 16:w0 + k1:17]
+        ts(OMB, pS[:, 0:3, 0:34], 0.0625, 1.0, A.max, A.min, [bS, "pS" + s], ["OMB" + ps], HC)
+        scan(Rs, OMB, rin, A.mult, A.max, ["OMB" + ps, rn], ["Rs" + ps] + WB, HC)
+        ts(ON, Rs, 0.0625, None, A.is_ge, None, ["Rs" + ps] + WB, ["ON" + ps], HC)
+        tt(T.TT[:, k0:k1], pS[:, 0:3, 34:68], ON, A.mult, [bS, "pS" + s, "ON" + ps], ["TT" + s], HC)
+        scan(T.CS[:, k0:k1], T.M17[:], T.TT[:, k0:k1], A.mult, A.add, ["M17", "TT" + s], ["CS" + s], HC)
+        ts(BR, R16, 0.0625, None, A.is_lt, None, ["Rs" + ps] + WB, ["BR%d" % hop + s], HB)
+        if hop == 0:
+            tt(T.RIN[:, k0:k1:17], R16, BR, A.max, ["Rs" + ps, "BR0" + s] + WB, ["RIN" + s], HB)
+        else:
+            tt(T.RN[:, b0:b1], R16, BR, A.max, ["Rs" + ps, "BR1" + s] + WB, ["RN" + s], HB)
+        cn, qo = T.CS[:, k0 + 15:k1:17], T.CS[:, k0 + 16:k1:17]
+        pc, pq, pcq, po = pS[:, 3, 0:HB], pS[:, 3, HB:2 * HB], pS[:, 3, 0:2 * HB], pS[:, 3, 16:28]
+        P0 = rot(T.P2, 0)
+        if hop == 0:
+            mm([(pc, P0, cn, True, True), (pq, P0, qo, True, True)], ["P2", "CS" + s], [bS, "pc" + s], 512)
+            ts(T.CL[:, NB * x:NB * (x + 1)], pcq, float(KB - q0), None, A.add, None, [bS, "pc" + s], ["CL" + s], 2 * HB)
+            move("X", qb, T.KW[:, q0:KB + W].indirect(T.CL[:, NB * x + HB:NB * (x + 1)]),
+                ["K", "CL" + s] + ["q%d" % j for j in range(m + 1)], ["qb" + s], HL, GA)
+            return
+        if last:
+            mm([(pc, P0, cn, True, True)], ["P2", "CS" + s], [bS, "pc" + s], 256)
+            cp(T.CQ[:, HB + b0:HB + b1], pc, [bS, "pc" + s], ["CQ" + s], HB)
+            return
+        u = t + 1
+        mm([(pS[:, 3, 17:28:2], rot(T.NP2, u), cn, True, True),
+            (pS[:, 3, 16:28:2], T.C2[:, 128 * t:128 * u], T.RN[:, b0:b1], True, True)],
+           ["NP2", "C2%d" % u, "CS" + s, "RN" + s], [bS, "po" + s], 512)
+        MO = T.MO[:, HB * m:HB * (m + 1), :]
+        move("X", T.MO[:, HB * m:HB * (m + 1), 0:2], po, [bS, "po" + s], ["MO%d" % m], 2 * HB)
+        send(T.MI[:, HC * m:HC * (m + 1)], MO, "rm%d" % m, ["MO%d" % m], ["MI%d" % m], 300)
+        if x == 1: pc, pq = pq, pc
+        mm([(pq, P0, qo, True, True), (pc, P0, cn, True, True)], ["P2", "CS" + s], [bS, "pc" + s], 512)
+        cp(T.CQ[:, 2 * b0:2 * b1], pcq, [bS, "pc" + s], ["CQ" + s], 2 * HB)
+        move("X", T.QS[:, j0:j1], T.KW[:, KB:KB + W + HL * (x + 1)].indirect(T.CQ[:, 3 * b0:3 * b0 + HB]),
+            ["K", "CQ" + s] + ["qb%d" % j for j in range(x + 1)], ["QS" + s], HL, GA)
+        pt = T.pM[:, 128 + HL * x:128 + HL * (x + 1)]
+        mm([(pt, rot(T.IB2, u), T.QS[:, j0:j1], True, True)], ["IB2", "QS" + s], ["#M", "pt" + s], HL)
+        QT = T.QT[:, HL * m:HL * (m + 1)]
+        move("X", QT, pt, ["#M", "pt" + s], ["QT%d" % m], HL)
+        send(T.KW[:, HL * (5 - m):HL * (6 - m)], QT, "rq%d" % m, ["QT%d" % m], ["q%d" % (m + 2)], 300)
+
+    def names(t, hop):
+        p, last = hop, t == NV - 1
+        p = (NH * t + hop) % DEPTH
+        NVv = T["NV%d" % p]
+        mm([(T.pN[:, 0:6, :, l2, 0:8], pd(2, l2, g2), T.C3[:, :, g2, :], g2 == 0, g2 == 1)
+            for l2 in range(2) for g2 in range(2)], PDS[2] + ["C30", "C31"], ["#N", "pN"], 384)
+        cp(NVv[:, 0:96], T.pN[:, 0:6, 0, :, 0:8], ["#N", "pN"], ["NVa%d" % p], 96)
+        cp(NVv[:, 96:192], T.pN[:, 0:6, 1, :, 0:8], ["#N", "pN"], ["NVb%d" % p], 96)
+        if hop == 0 and not last:
+            ts(T.NZ[:], T.NH0[:], X[6], None, A.max, None, ["NH00", "NH01", "X6"], ["NZ"], L // 2)
+            tt(T.CW[:], T.IO[:].indirect(T.CA[:]), T.MSK[:], A.mult, ["IO", "CA0", "CA1", "MSK"], ["CW0", "CW1"], L, GA)
+
+    def shortcuts(xs):
+        b0, b1 = min(BAT[x][0] for x in xs), max(BAT[x][1] for x in xs)
+        nb, x0 = b1 - b0, xs[0]
+        nm = lambda a: [a + str(x) for x in xs]
+        tt(T.CUT[:, b0:b1], T.BR1[:, b0:b1], T.BR0[:, b0:b1], A.is_gt, nm("BR0") + nm("BR1"), nm("CUT"), nb)
+        pk, pm = T.pM[:, 320 + b0:320 + b1], T.pM[:, 336 + b0:336 + b1]
+        mm([(pk, rot(T.NP2, 0), T.CUT[:, b0:b1], True, True)], ["NP2"] + nm("CUT"), ["#M"] + nm("pk"), 256)
+        tt(T.KEY[:, 16 * x0:16 * x0 + nb], pk, T.CAS[:, b0:b1], A.mult, ["#M"] + nm("pk") + nm("CAS"), nm("KEY"), nb)
+        tt(T.EQ[:, 16 * b0:16 * b1], T.KEY[:, 16 * x0:16 * x0 + 16].indirect(T.BL[:, 0:nb]), T.CW[:, 16 * b0:16 * b1], A.is_equal,
+           nm("KEY") + nm("CW") + ["BL"], nm("EQ"), 16 * nb, GA)
+        mm([(pm, T.ID2[:, 0:128], T.CAS[:, b0:b1], True, False), (pm, rot(T.NP2, 0), T.CUT[:, b0:b1], False, False)]
+           + [(pm, T.BO[:, 15 - l:143 - l], T.EQ[:, 16 * b0 + l:16 * b1:16], False, l == 15) for l in range(1, 16)],
+           ["ID2", "NP2", "BO"] + nm("CAS") + nm("CUT") + nm("EQ"), ["#M"] + nm("pm"), 512 + 960)
+        tt(T.VAL[:, 16 * b0:16 * b1], T.IO[:].indirect(T.CQ[:, HB + b0:HB + b1]), T.NZ[:, 16 * b0:16 * b1], A.min,
+           ["IO", "NZ"] + nm("CQ"), nm("VAL"), 16 * nb, GA)
+        ts(T.OFF[:, 2 * b0:2 * b1:2], pm, 4096.0, X[4], A.mult, A.min, ["#M", "X4"] + nm("pm"), nm("OFF"), nb)
+
+    def rewrite():
+        for x in range(2):
+            for b in range(BAT[x][1] - 1, BAT[x][0] - 1, -1):
+                cp(T.PG[:, KB:].indirect(T.OFF[:, 2 * b:2 * b + 1]), T.VAL[:, 16 * b:16 * b + 16], ["VAL%d" % x, "OFF%d" % x],
+                   PGR + ["PG4"], 16, SC)
+
+    def values(t, hop, xs):
+        n = t * NH + hop
+        p = n % 2
+        b0, b1 = min(BAT[x][0] for x in xs), max(BAT[x][1] for x in xs)
+        nb, k0, k1, w0 = b1 - b0, 17 * b0, 17 * b1, 204 * p
+        nm = lambda a: [a + str(x) for x in xs]
+        np_ = lambda a: [a + "%d%d" % (p, x) for x in xs]
+        wv = T.pW[:, w0 + k0:w0 + k1]
+        affine(T.BT[:, k0:k1 - 1], T["OMB%d" % p][:, k0 + 1:k1], -1.0, 1.0, np_("OMB"), nm("BT"), 17 * nb)
+        tt(wv, wv, T["ON%d" % p][:, k0:k1], A.mult, np_("ON") + WB, np_("Rs"), 17 * nb)
+        tt(wv, wv, T.BT[:, k0:k1], A.mult, nm("BT") + WB, np_("Rs"), 17 * nb)
+        if hop == 1:
+            cp(T.pW[:, w0 + k0 + 16:w0 + k1:17], T.RN[:, b0:b1], nm("RN") + WB, np_("Rs"), nb)
+        lo, hi = slice(0, 64), slice(64, 128)
+        d = n % DEPTH
+        nd_ = lambda a: [a + "%d%d" % (d, x) for x in xs]
+        XA, XB = T["XA%d" % d], T["XB%d" % d]
+        XS = nd_("XAh") + nd_("XAl") + nd_("XBh") + nd_("XBl")
+        flat = n in FLAT
+        if flat:
+            move(HI, XA[:, b0:b1, :], wv, np_("Rs") + WB, nd_("XAh") + nd_("XAl"), 17 * nb)
+            tt(XB[:, b0:b1, :], wv, XA[:, b0:b1, :], A.subtract, np_("Rs") + nd_("XAh") + nd_("XAl") + WB, nd_("XBh") + nd_("XBl"), 17 * nb)
+        else:
+            for Xt, xn, a, o in ((XA, "XA", lo, hi), (XB, "XB", hi, lo)):
+                move(HI, Xt[a, b0:b1, :], T.pW[a, w0 + k0:w0 + k1], np_("Rs") + WB, nd_(xn + "h"), 17 * nb)
+                tt(Xt[o, b0:b1, :], T.pW[a, w0 + k0:w0 + k1], Xt[a, b0:b1, :], A.subtract, np_("Rs") + nd_(xn + "h") + WB,
+                   nd_(xn + "l"), 17 * nb)
+
+        def spread(out, l, i):
+            s0 = 128 * (l % 8)
+            if not flat:
+                return [(out, T.SEL[:, s0:s0 + 128], (XA if l < 8 else XB)[:, b0:b1, i], True, True)]
+            a = lo if l < 8 else hi
+            return [(out, T.SEL[a, s0:s0 + 128], XA[a, b0:b1, i], True, False), (out, T.SEL[a, s0:s0 + 128], XB[a, b0:b1, i], False, True)]
+
+        VG, NVv = T["VG%d" % d], T["NV%d" % d]
+        if hop == 1:
+            VC, pE = VG[:, 16 * L + 16 * b0:16 * L + 16 * b1], T["pE%d" % (slot[0] % 2)]
+            e = slot[0] % 2
+            slot[0] += 1
+            act(VC, T.VT[:].indirect(T.CQ[:, HB + b0:HB + b1]), F.Sigmoid, ["VT"] + nm("CQ"), nd_("VC"), 16 * nb, GA)
+            mm(sum([spread(pE[:, l:16 * nb:16], l, 16) for l in range(16)], []), ["SEL"] + XS, ["#E%d" % e, "pE%d" % e], 1024 * (1 + flat))
+            tt(T["RV%d" % (t % 2)][:, 16 * b0:16 * b1], VC, pE[:, 0:16 * nb], A.mult, nd_("VC") + ["#E%d" % e, "pE%d" % e],
+               nm("RV%d" % (t % 2)), 16 * nb)
+        for hf in range(2):
+            ni = 8
+            y0 = 96 * hf
+            for x in xs:
+                for y in range(VSP):
+                    a0, a1 = [y0 + ni * BAT[x][0] + 2 * ((ni * HB // 2 * z) // VSP) for z in (y, y + 1)]
+                    act(VG[:, 16 * a0:16 * a1], T.VT[:].indirect(NVv[:, a0:a1]), F.Sigmoid, ["VT", "NV" + "ab"[hf] + str(d)],
+                        ["VG%d%d%d%d" % (y, hf, d, x)], 16 * (a1 - a0), GA)
+                    if not first:
+                        first.append(len(ops) - 1)
+                        ops[-1]["x"] = 1560
+                    else:
+                        ops[-1]["s"].add(first[0])
+            a0, a1, ny = y0 + ni * b0, y0 + ni * b1, ni * nb
+            into = ONTO.get((t, 2 * hop + hf))
+            bn = "B%d" % (4 * (t % 2) + (2 * hop + hf if into is None else into))
+            for s4 in range(4):
+                e = slot[0] % 2
                 slot[0] += 1
-                pE = T["pE%d" % e]
-                lst = []
-                for l in (l0, l0 + 1):
-                    o = pE[:, L * (l - l0):L * (l - l0 + 1)]
-                    sel = T.SEL[:, 128 * l:128 * l + 128]
-                    lst += [(o, sel, T.WH[:, :, 0:16], True, False), (o, sel, T.WL[:, :, 0:16], False, True)]
-                mm(lst, ["SEL", "WH", "WL"], ["#E%d" % e, "pE%d" % e], 4 * L)
-                tt(T.PR[:, L * l0:L * (l0 + 2)], VG[:, L * l0:L * (l0 + 2)], pE[:, 0:2 * L], A.mult,
-                   ["%s_%d" % (vgn, l0 // 4), "#E%d" % e, "pE%d" % e], ["PR%d" % l0], 2 * L)
-                hi = L * (l0 + 2)
-                if l0 % 4 == 2 and hi > lo:
-                    sos.append("SO%d" % (l0 // 4))
-                    scan(T.SO[:, lo:hi], T.MK[:, 0:hi - lo], T.PR[:, lo:hi], A.mult, A.add,
-                         ["MK", "PR%d" % (l0 - 2), "PR%d" % l0], sos[-1:], hi - lo)
-                    lo = hi
-            rot = T.ID2[:, 128 - 16 * t:256 - 16 * t]
-            if nr:
-                pR = T.pX[:, 416:416 + nr]
-                prs = ["PR%d" % l0 for l0 in range(0, 16, 2) if L * l0 < 16 * nr]
-                for i0 in range(0, 16, 4):
-                    mm([(pR, T.ID2[:, 0:128], T.PR[:, i:16 * nr:16], i == 0, n == 0 and i == 15) for i in range(i0, i0 + 4)],
-                       ["ID2"] + prs, ["#X", "pXr"], 16 * max(64, nr))
-                if hop == 1:
-                    mm([(pR, T.ID2[:, 0:128], AC[:, 0:nr], False, True)], ["ID2", acn], ["#X", "pXr"], 4 * max(64, nr))
-                elif t:
-                    mm([(pR, rot, T["AI%d" % t][:, 0:nr], False, True)], ["ID2", "AI%d" % t], ["#X", "pXr"], 4 * max(64, nr))
-                act(AC[:, 0:nr], pR, F.Copy, ["#X", "pXr"], [acn + "r"], nr)
-            so, m = T.SO[:, 16 * nr + 15::16], L - nr
-            if hop == 1:
-                tt(AC[:, nr:L], so, AC[:, nr:L], A.add, sos + [acn, acn + "r"], [acn], m, 2)
-                if not last:
-                    send(T["AI%d" % (t + 1)][:], AC[:], "ra%d" % (t + 1), [acn], ["AI%d" % (t + 1)], 3800)
-                tt(RP[:], AC[:].indirect(T.RO[:]), T.RV[:], A.add, [acn, "RO", "RV"], ["RP%d" % t], L, GA)
-                dma("S", T.ya[:, L * t:L * (t + 1)], RP[:], ["RP%d" % t], ["ya%d" % t], 2500)
-            elif t == 0:
-                cp(AC[:, nr:L], so, sos + [acn + "r"], [acn], m)
-            else:
-                mm([(T.pX[:, L:L + m], rot, T["AI%d" % t][:, nr:L], True, True)], ["ID2", "AI%d" % t], ["#X", "pXb"], 4 * m)
-                tt(AC[:, nr:L], T.pX[:, L:L + m], so, A.add, sos + ["#X", "pXb", acn + "r"], [acn], m)
+                pE, en = T["pE%d" % e], ["#E%d" % e, "pE%d" % e]
+                mm(sum([spread(pE[:, lq:4 * ny:4], 4 * lq + s4, slice(8 * hf, 8 * hf + 8)) for lq in range(4)], []),
+                   ["SEL"] + XS, en, 4 * max(64, ny) * (1 + flat))
+                B, bs, vs = T[bn][:, b0:b1, :, s4::4], nm(bn + "s%d" % s4), sum([nd_("VG%d%d" % (y, hf)) for y in range(VSP)], [])
+                if into is None:
+                    tt(B, VG[:, 16 * a0 + s4:16 * a1:4], pE[:, 0:4 * ny], A.mult, vs + en, bs, 4 * ny)
+                else:
+                    tt(pE[:, 0:4 * ny], VG[:, 16 * a0 + s4:16 * a1:4], pE[:, 0:4 * ny], A.mult, vs + en, en, 4 * ny)
+                    tt(B, pE[:, 0:4 * ny], B, A.add, en + bs, bs, 4 * ny)
+
+    def parts(j, xs=(0, 1)):
+        return ["B%ds%d%d" % (j, s4, x) for s4 in range(4) for x in xs]
+
+    def add(j, k):
+        for xs in (((0,), (1,)) if ASP else ((0, 1),)):
+            b0, b1 = min(BAT[x][0] for x in xs), max(BAT[x][1] for x in xs)
+            add_dma(T["B%d" % j][:, b0:b1], T["B%d" % k][:, b0:b1], parts(k, xs), parts(j, xs), ACC * len(xs) // 2)
+
+    def report(t, xs, srcs, pR, bR):
+        b0, b1 = min(BAT[x][0] for x in xs), max(BAT[x][1] for x in xs)
+        j0, j1 = 16 * b0, 16 * b1
+        rn = "pR%d" % xs[0]
+        lst = []
+        for j in srcs:
+            B, k = T["B%d" % j], 8
+            for _ in range(VADD.get((t, j % 4, xs), 0)):
+                k //= 2
+                tt(B[:, b0:b1, 0:k, :], B[:, b0:b1, 0:k, :], B[:, b0:b1, k:2 * k, :], A.add, parts(j, xs), parts(j, xs), k * (j1 - j0), 2)
+            lst += [(B[:, b0:b1, i, :], T.ID2[:, 0:128], parts(j, xs)) for i in range(k)]
+        if t:
+            lst.insert(0, (T["AI%d" % t][:, j0:j1], rot(T.ID2, t), ["AI%d" % t]))
+        for k, (src, M, r) in enumerate(lst):
+            mm([(pR, M, src, k == 0, k == len(lst) - 1)], ["ID2"] + r, [bR, rn], 4 * (j1 - j0))
+        RP = T["RP%d" % t]
+        if t < NV - 1:
+            move("X", T["AC%d" % (t + 1)][:], pR, [bR, rn], ["AC%d" % (t + 1)], L)
+            send(T["AI%d" % (t + 1)][:], T["AC%d" % (t + 1)][:], "ra%d" % (t + 1), ["AC%d" % (t + 1)], ["AI%d" % (t + 1)], 600)
+        tt(RP[:, j0:j1], pR, T["RV%d" % (t % 2)][:, j0:j1], A.add, [bR, rn] + ["RV%d%d" % (t % 2, x) for x in xs], ["RP%d%d" % (t, xs[0])], j1 - j0)
+        dma("S", T.ya[:, L * t + j0:L * t + j1], RP[:, j0:j1], ["RP%d%d" % (t, xs[0])], ["ya%d%d" % (t, xs[0])], 300, 2200)
+
+    WB = ["#W"] if HI != "V" else []
+    for t in range(NV):
+        last, o = t == NV - 1, 4 * (t % 2)
+        chain(t, 0, 0)
+        chain(t, 0, 1)
+        names(t, 0)
+        values(t, 0, (0, 1))
+        if 1 in ADDS[t]: add(o, o + 1)
+        srcs = [o + j for j in range(4) if j not in ADDS[t] and (t, j) not in ONTO]
+        chain(t, 1, 0)
+        if not last and SPLIT_CUT: shortcuts((0,))
+        chain(t, 1, 1)
+        names(t, 1)
+        if not last:
+            shortcuts((1,) if SPLIT_CUT else (0, 1))
+            rewrite()
+            values(t, 1, (0, 1))
+            for j in (2, 3):
+                if j in ADDS[t]: add(o, o + j)
+            report(t, (0, 1), srcs[::-1], T.pR[:, 0:L], "#R")
+        else:
+            values(t, 1, (0,))
+            values(t, 1, (1,))
+            report(t, (0,), srcs, T.pR[:, 0:HL], "#R")
+            report(t, (1,), srcs, T.pM[:, 0:HL], "#M")
     return ops, sends[0]
 
 
@@ -425,165 +532,204 @@ def costs(ops, s):
     for o in ops:
         e, n, f = o["e"], o["t"][0], o["t"][1]
         if o["sem"] or e in "GSR": c = n
-        elif e == "T": c = FAC * n * s[2]
-        elif f == GA: c = FAC * (s[3] + 30 + n * s[0])
-        elif f == SC: c = FAC * (s[3] + 30 + n * s[1])
-        else: c = FAC * (s[3] + (20 if e == "A" else 0) + max(n * f, 64 - s[3]))
-        out.append(c)
+        elif e == "T": c = s[2] * n * 0.5
+        elif f == GA: c = s[2] * ((60 if e == "V" else 78) + n * s[0]) + o.get("x", 0)
+        elif f == SC: c = s[2] * (60 + n * s[1])
+        else: c = s[2] * (s[3] + max(n * f, 64))
+        out.append(int(c))
     return out
 
 
+ENG = "VATGSR"
+
+
 def prepare(ops):
+    n = len(ops)
+    en = [ENG.index(o["e"]) if o["e"] != "X" else 1 for o in ops]
+    pred = [[j + n for j in o["h"]] + [j for j in o["s"] if j not in o["h"]] for o in ops]
     succ = [[] for _ in ops]
-    pred = []
     for k, o in enumerate(ops):
-        pred.append([(j, ops[j]["a"], j in o["h"]) for j in o["h"] | o["s"]])
         for j in o["h"] | o["s"]:
-            succ[j].append((k, j in o["h"]))
-    return [o["e"] for o in ops], [o["a"] for o in ops], pred, succ
+            succ[j].append(k)
+    cs = [(costs(ops, s), [int(o["d"] * s[5]) for o in ops], [o["a"] + (0 if o["e"] == "R" else s[4]) for o in ops]) for s in COSTS]
+    return en, pred, succ, cs, [o["e"] == "X" for o in ops]
 
 
-def span(pre, order, cost, lat):
-    eng, aft, pred, succ = pre
-    end = [0.0] * len(eng)
-    free = {}
-    for k in order:
-        s = free.get(eng[k], 0.0)
-        for j, a, hard in pred[k]:
-            x = end[j] + a + lat if hard else end[j]
-            if x > s: s = x
-        end[k] = s + cost[k]
-        if eng[k] != "R": free[eng[k]] = end[k]
-    return max(x + a for x, a in zip(end, aft))
+def play(pre, c, rest, tm, free):
+    en, pred = pre[0], pre[1]
+    cost, dd, aft = c
+    n = len(en)
+    for k in rest:
+        e = en[k]
+        s = free[e]
+        for j in pred[k]:
+            if tm[j] > s: s = tm[j]
+        s += cost[k]
+        tm[k] = s
+        if e != 5: free[e] = s
+        if dd[k]:
+            if free[6] > s: s = free[6]
+            s += dd[k]
+            free[6] = s
+        tm[n + k] = s + aft[k]
+    return tm
 
 
-def listsched(pre, cost, lat, off):
-    eng, aft, pred, succ = pre
-    n = len(eng)
-    need = [len(p) for p in pred]
-    pr = [0.0] * n
-    for k in range(n - 1, -1, -1):
-        m = 0.0
-        for j, hard in succ[k]:
-            x = pr[j] + aft[k] + LAT if hard else pr[j]
-            if x > m: m = x
-        pr[k] = cost[k] + max(m, aft[k])
-    pr = [p + float(z) for p, z in zip(pr, off)]
-    ready = [0.0] * n
-    free = {e: 0.0 for e in "VATGSR"}
-    pool = {e: [] for e in "VATGSR"}
-    for k in range(n):
-        if need[k] == 0: pool[eng[k]].append(k)
-    pick = {}
-    order = []
-    while len(order) < n:
-        for e, mine in pool.items():
-            if e not in pick and mine:
-                t0 = max(free[e], min([ready[k] for k in mine]))
-                k = max([(pr[k], -k) for k in mine if ready[k] <= t0 + LOOK])[1]
-                pick[e] = (max(t0, ready[-k]), -k)
-        s, k = min(pick.values())
-        e = eng[k]
-        del pick[e]
-        pool[e].remove(k)
-        order.append(k)
-        end = s + cost[k]
-        if e != "R": free[e] = end
-        for j, hard in succ[k]:
-            x = end + aft[k] + lat if hard else end
-            if x > ready[j]: ready[j] = x
-            need[j] -= 1
-            if need[j] == 0:
-                pool[eng[j]].append(j)
-                pick.pop(eng[j], None)
-    return order
+def place(busy, t, c):
+    lo, hi = 0, len(busy)
+    while lo < hi:
+        mid = (lo + hi) // 2
+        if busy[mid][1] <= t: lo = mid + 1
+        else: hi = mid
+    while lo < len(busy) and busy[lo][0] < t + c:
+        t = busy[lo][1]
+        lo += 1
+    return t, lo
+
+
+def sweep(pre, c, seq, back, bias):
+    en, pred, succ = pre[0], pre[1], pre[2]
+    cost, dd, aft = c
+    n = len(en)
+    busy = [[] for _ in range(7)]
+    st = [0] * n
+    low = [0] * n
+    for k in seq:
+        e, ck, d = en[k], cost[k], dd[k]
+        if back:
+            t = max(low[k], aft[k] + d)
+        else:
+            t = 0
+            for j in pred[k]:
+                x = st[j - n] + cost[j - n] + dd[j - n] + aft[j - n] if j >= n else st[j] + cost[j]
+                if x > t: t = x
+        if pre[4][k]:
+            e = en[k] = 0 if place(busy[0], t, ck)[0] + bias[k] < place(busy[1], t, ck)[0] else 1
+        if e != 5:
+            while True:
+                t, i = place(busy[e], t, ck)
+                if not d: break
+                u = t - d if back else t + ck
+                v, i2 = place(busy[6], u, d)
+                if v == u:
+                    busy[6].insert(i2, (u, u + d))
+                    break
+                t += v - u
+            busy[e].insert(i, (t, t + ck))
+        st[k] = t
+        if back:
+            for j in pred[k]:
+                x = t + ck
+                if j >= n:
+                    j -= n
+                    x += dd[j] + aft[j]
+                if x > low[j]: low[j] = x
+    if back:
+        top = max([a + b for a, b in zip(st, cost)])
+        return [top - a - b for a, b in zip(st, cost)]
+    return st
+
+
+def length(pre, order):
+    n = len(order)
+    return [max(play(pre, c, order, [0.0] * (2 * n), [0.0] * 7)[n:]) for c in pre[3]]
 
 
 def schedule(ops):
     n = len(ops)
     pre = prepare(ops)
-    cs = [costs(ops, s) for s in COSTS]
-    seed = [12345]
+    en, pred, succ, cs, free = pre
+    c = cs[0]
+    seed = [SEED]
 
     def rnd(m):
         seed[0] = (seed[0] * 1103515245 + 12345) % 2 ** 31
         return (seed[0] >> 8) % m
 
-    def score(off):
-        order = listsched(pre, cs[0], COSTS[0][4], off)
-        return sum(w * span(pre, order, c, s[4]) for w, c, s in zip(WEIGHTS, cs, COSTS)), order
+    def legal(key, back):
+        key = list(key)
+        for k in (range(n - 1, -1, -1) if back else range(n)):
+            for j in (succ[k] if back else pred[k]):
+                if key[j % n] > key[k]: key[k] = key[j % n]
+        return sorted(range(n), key=lambda k: (key[k], -k if back else k))
 
-    off = [0.0] * n
-    best, order = score(off)
-    for _ in range(TRIES):
-        o2 = list(off)
-        for _k in range(1 + rnd(7)):
-            o2[rnd(n)] += 100.0 * (rnd(15) + rnd(15) - 14)
-        s, od = score(o2)
-        if s <= best: best, order, off = s, od, o2
-    return refine(pre, order, cs)
+    pr = [0] * n
+    for k in range(n - 1, -1, -1):
+        pr[k] = c[0][k] + c[1][k] + c[2][k] + max([pr[j] for j in succ[k]] + [0])
+    bias = [BIAS] * n
+    flex = [k for k in range(n) if free[k]]
+    st = sweep(pre, c, legal([-x for x in pr], False), False, bias)
+    best, cur, order, keep, where = 1e18, 1e18, None, st, None
+    for it in range(TRIES):
+        amp = SHAKE[it % len(SHAKE)]
+        t0 = rnd(max(keep) + SPAN) - SPAN
+        shake = [rnd(amp) if t0 <= a < t0 + SPAN else 0 for a in keep]
+        b2 = list(bias)
+        for k in flex:
+            if shake[k] and rnd(4) == 0: b2[k] = 400 * rnd(12) - 1600
+        st = sweep(pre, c, legal([-(a + b) + z for a, b, z in zip(keep, c[0], shake)], True), True, b2)
+        st = sweep(pre, c, legal([a + z for a, z in zip(st, shake)], False), False, b2)
+        od = sorted(range(n), key=lambda k: (st[k], k))
+        s = sum(w * x for w, x in zip(WEIGHTS, length(pre, od)))
+        if s < cur * (1 + KEEP * (1 - it / TRIES)): cur, keep, bias = s, st, b2
+        if s < best: best, order, where = s, od, list(en)
+    en[:] = where
+    return refine(pre, order), en
 
 
-def refine(pre, order, cs):
-    eng, aft, pred, succ = pre
-    n = len(eng)
-    en = ["VATGSR".index(e) for e in eng]
-    P = [[[(j, a + s[4] if hard else 0.0) for j, a, hard in pred[k]] for k in range(n)] for s in COSTS]
-    ps = [set(x[0] for x in p) for p in pred]
-    ss = [set(x[0] for x in p) for p in succ]
+def refine(pre, order):
+    en, pred, succ, cs = pre[:4]
+    n = len(en)
+    ps = [set(j % n for j in p) for p in pred]
+    ss = [set(p) for p in succ]
+    tails = [n + k for k in range(n) if not succ[k] and en[k] == 4]
+    isd = [c > 0 for c in cs[0][1]]
     seed = [99]
 
     def rnd(m):
         seed[0] = (seed[0] * 1103515245 + 12345) % 2 ** 31
         return (seed[0] >> 8) % m
 
-    def score(order, p0, ends):
-        lastop = [-1] * 6
+    def score(order, p0, tms):
+        lastop = [-1] * 7
         for i in range(p0 - 1, -1, -1):
-            e = en[order[i]]
-            if lastop[e] < 0:
-                lastop[e] = order[i]
-                if min(lastop[:4]) >= 0 and i < p0 - 60: break
+            k = order[i]
+            if lastop[en[k]] < 0: lastop[en[k]] = k
+            if isd[k] and lastop[6] < 0: lastop[6] = k
+            if i < p0 - 40 and min(lastop[:5]) >= 0 and lastop[6] >= 0: break
         tot, out, rest = 0.0, [], order[p0:]
-        for c, p, w, old in zip(cs, P, WEIGHTS, ends):
-            end = list(old)
-            free = [end[k] if k >= 0 else 0.0 for k in lastop]
+        for c, w, old in zip(cs, WEIGHTS, tms):
+            tm = list(old)
+            free = [tm[k] if k >= 0 else 0.0 for k in lastop]
             free[5] = 0.0
-            for k in rest:
-                e = en[k]
-                s = free[e]
-                for j, a in p[k]:
-                    x = end[j] + a
-                    if x > s: s = x
-                s += c[k]
-                end[k] = s
-                if e != 5: free[e] = s
-            tot += w * (end[n - 1] + 0.02 * (free[0] + free[1] + free[2]))
-            out.append(end)
+            if lastop[6] >= 0: free[6] = tm[n + lastop[6]] - c[2][lastop[6]]
+            play(pre, c, rest, tm, free)
+            tot += w * (max([tm[k] for k in tails]) + 0.02 * (free[0] + free[1] + free[2]))
+            out.append(tm)
         return tot, out
 
-    def critical(order, ends):
+    def critical(order, tms):
         pos = {k: i for i, k in enumerate(order)}
         prev, lastop = {}, {}
         for k in order:
             prev[k] = lastop.get(en[k], -1)
             lastop[en[k]] = k
         out = []
-        for c, p, end in zip(cs, P, ends):
-            k = n - 1
+        for c, tm in zip(cs, tms):
+            k = max([(tm[j], j) for j in tails])[1] - n
             while k >= 0:
                 out.append(pos[k])
-                s, nx = end[k] - c[k] - 0.5, -1
-                for j, a in p[k]:
-                    if end[j] + a >= s: nx = j
-                if nx < 0 and en[k] != 5 and prev[k] >= 0 and end[prev[k]] >= s: nx = prev[k]
+                s, nx = tm[k] - c[0][k] - 0.5, -1
+                for j in pred[k]:
+                    if tm[j] >= s: nx = j % n
+                if nx < 0 and en[k] != 5 and prev[k] >= 0 and tm[prev[k]] >= s: nx = prev[k]
                 k = nx
         return out
 
-    cur, ends = score(order, 0, [[0.0] * n for _ in cs])
+    cur, tms = score(order, 0, [[0.0] * (2 * n) for _ in cs])
     best, bo, crit = cur, list(order), []
     for it in range(MOVES):
-        if it % 64 == 0: crit = critical(order, ends)
+        if it % 64 == 0: crit = critical(order, tms)
         i = rnd(n) if rnd(3) == 0 else min(n - 1, max(0, crit[rnd(len(crit))] + rnd(5) - 2))
         k = order[i]
         e = en[k]
@@ -601,9 +747,9 @@ def refine(pre, order, cs):
         o2 = list(order)
         o2.pop(i)
         o2.insert(j, k)
-        s, e2 = score(o2, min(i, j), ends)
+        s, e2 = score(o2, min(i, j), tms)
         if s <= cur + 0.4 * rnd(100) * (1 - it / MOVES):
-            cur, order, ends = s, o2, e2
+            cur, order, tms = s, o2, e2
             if s < best: best, bo = s, o2
     return bo
 
@@ -616,7 +762,7 @@ def rank_program(g, core, T, topo):
     ops, nsent = collect(g, T, topo, core, nxt)
     if "o" not in ORDER:
         ORDER["o"] = schedule(ops)
-    order = ORDER["o"]
+    order, where = ORDER["o"]
     Q = {"V": g.vector, "A": g.scalar, "T": g.tensor, "G": g, "S": g.sync}
     cnt = {"V": 0, "A": 0, "T": 0, "G": 0}
     known = {e: {} for e in Q}
@@ -624,7 +770,7 @@ def rank_program(g, core, T, topo):
     total = {}
     for k in order:
         o = ops[k]
-        e = o["e"]
+        e = ENG[where[k]]
         if e == "R":
             done[k] = (o["sem"], o["n"], {})
             total[o["sem"]] = o["n"]
@@ -649,7 +795,7 @@ def rank_program(g, core, T, topo):
             total[o["sem"]] = o["n"]
         else:
             for c in o["c"]:
-                c().then_inc(T.sem["c" + e], 1)
+                (c(e) if o["e"] == "X" else c()).then_inc(T.sem["c" + e], 1)
                 cnt[e] += 1
             done[k] = ("c" + e, cnt[e], dict(kn))
             total["c" + e] = cnt[e]

from concourse.mybir import AluOpType as A, ActivationFunctionType as F

W, L, NB, NV, NH = 2048, 192, 12, 4, 2
SB, PS = "sbuf", "psum"
f32, b16, i32, u16, f16 = "float32", "bfloat16", "int32", "uint16", "float16"
BAT = ((6, 12), (0, 6))
HB, HL, HC = 6, 96, 102
KB = 8 * HL

SCRATCH = {
    "KW": (SB, [128, KB + W + L], b16), "VT": (SB, [128, W], b16), "BP": (SB, [128, W // 2], i32),
    "PG": (SB, [128, KB + W + 16], i32), "ST": (SB, [128, NB], i32),
    "LB": (SB, [128, 24 * L], b16), "KG": (SB, [128, 16 * L], b16),
    "NM0": (SB, [128, L], u16), "NM1": (SB, [128, L], u16),
    "NH0": (SB, [128, L], f16), "NH1": (SB, [128, L], f16), "NZ": (SB, [128, L], f16), "C3": (SB, [128, 6, 2, 16], f16),
    "OMB0": (SB, [128, 204], f32), "OMB1": (SB, [128, 204], f32), "ON0": (SB, [128, 204], f32), "ON1": (SB, [128, 204], f32),
    "R0": (SB, [128, HC], f32), "RIN": (SB, [128, 204], f32), "RN": (SB, [128, NB], f32),
    "TT": (SB, [128, 204], f32), "CS": (SB, [128, 204], f32), "BT": (SB, [128, 204], f32),
    "BR0": (SB, [128, NB], f32), "BR1": (SB, [128, NB], f32), "CUT": (SB, [128, NB], f32),
    "CA": (SB, [128, NB], u16), "CL": (SB, [128, 2 * NB], u16), "CQ": (SB, [128, 2 * NB], u16),
    "CAS": (SB, [128, NB], f32), "KEY": (SB, [128, 32], f32), "CW": (SB, [128, L], f32), "EQ": (SB, [128, L], b16),
    "OFF": (SB, [128, 2 * NB], u16), "VAL": (SB, [128, L], i32), "QS": (SB, [128, L], b16),
    "MO": (SB, [128, 6 * HB, 17], f32), "MI": (SB, [128, 6 * HC], f32), "QT": (SB, [128, 6 * HL], b16),
    "CI": (SB, [128, 256], b16), "LAM": (SB, [128, 1024], b16), "CI3": (SB, [128, 16, 16], b16),
    "P2": (SB, [128, 256], f32), "NP2": (SB, [128, 256], f32), "ID2": (SB, [128, 256], f32), "IB2": (SB, [128, 256], b16),
    "C2": (SB, [128, 384], f32), "SEL": (SB, [128, 1024], b16), "IO": (SB, [128, W], f32), "IC": (SB, [128, W], f32),
    "PD": (SB, [128, 12 * 128], b16), "BO": (SB, [128, 144], b16), "INI": (SB, [128, 3, 4, 17], b16), "IND": (SB, [128, 3, 4, 17], b16),
    "CV": (SB, [128, 10 * 128], b16), "M17": (SB, [128, HC], f32), "CM": (SB, [128, HL], b16),
    "MSK": (SB, [128, L], f32), "RL": (SB, [128, L], f32),
    "PP": (SB, [128, 1], i32), "PC": (SB, [128, 8], i32), "PF": (SB, [128, 9], f32), "PX": (SB, [128, 16], f32),
    "RB": (SB, [128, NB], f32), "LO": (SB, [128, HB], u16), "BL": (SB, [128, NB], u16),
    "pS0": (PS, [128, 4, 128], f32), "pS1": (PS, [128, 4, 128], f32), "pW": (PS, [128, 512], f32), "pM": (PS, [128, 512], f32),
    "pN": (PS, [128, 8, 2, 2, 16], f32), "pR": (PS, [128, 512], f32), "pE0": (PS, [128, 512], f32), "pE1": (PS, [128, 512], f32),
}
DEPTH = 3
for _t in range(DEPTH):
    SCRATCH["VG%d" % _t] = (SB, [128, 17 * L], f32)
    SCRATCH["NV%d" % _t] = (SB, [128, L], u16)
    SCRATCH["XA%d" % _t] = (SB, [128, NB, 17], b16)
    SCRATCH["XB%d" % _t] = (SB, [128, NB, 17], b16)
for _t in range(8):
    SCRATCH["B%d" % _t] = (SB, [128, NB, 8, 16], f32)
for _t in range(2):
    SCRATCH["RV%d" % _t] = (SB, [128, L], f32)
for _t in range(NV):
    SCRATCH["RP%d" % _t] = (SB, [128, L], f32)
for _t in range(1, NV):
    SCRATCH["AC%d" % _t] = (SB, [128, L], f32)
    SCRATCH["AI%d" % _t] = (SB, [128, L], f32)

SEMAPHORES = (["cV", "cA", "cT", "cG", "sent"] + ["d%d" % k for k in range(12)] + ["e%d" % k for k in range(16)]
              + ["r%s%d" % (x, m) for x in "mq" for m in range(6)] + ["ra%d" % t for t in range(1, NV)])

SHAKE, KEEP, SPAN, BIAS, SEED = (300, 1000, 2500), 0.002, 8000, 2000, 12345
ORDER = {}
GA, SC = 1.56, 3.8
KCH = {"a": ((3, "A"), (2, "V"), (1, "A")), "b": ((3, "A"), (1, "V"), (2, "A")), "c": ((2, "A"), (2, "V"), (1, "V"), (1, "A")),
       "d": ((3, "A"), (2, "A"), (1, "A")), "x": ((2, "X"), (2, "X"), (1, "X"), (1, "X")), "y": ((3, "X"), (2, "X"), (1, "X")),
       "z": ((2, "X"), (2, "X"), (2, "X")), "w": ((1, "X"),) * 6}
KPLAN = "y" * 16
HI = "V"
SPLIT_CUT = False
SOFT = False
VADD = {}
FLAT = ()
ONTO = {(3, 3): 2, (3, 1): 0}
ADDS = ((1, 2), (1, 2), (1, 2), ())
ASP, VSP = True, 1
ACC = 6000
COSTS = [(GA, SC, 1.1, 20, 110, 1.0), (1.95, 3.0, 1.4, 10, 100, 1.2), (1.3, 4.5, 1.0, 40, 180, 0.9)]
WEIGHTS = [2, 1, 1]
TRIES, MOVES = 8000, 30000


def collect(g, T, topo, core, nxt):
    ops = []
    last_w, readers, bank = {}, {}, {}

    def op(eng, calls, r, w, cost, after=0, sem=None, n=0, dd=0):
        k = len(ops)
        hard, soft = set(), set()
        for x in r:
            if x[0] != "#" and x in last_w: hard.add(last_w[x])
        for x in w:
            if x[0] == "#": continue
            for j in readers.get(x, []) + ([last_w[x]] if x in last_w else []):
                (soft if SOFT and eng in "VA" and ops[j]["e"] == eng and not (sem or ops[j]["sem"]) else hard).add(j)
        for x in list(r) + list(w):
            if x[0] == "#":
                for e, j in bank.setdefault(x, {}).items():
                    (soft if e == eng != "X" else hard).add(j)
                bank[x][eng] = k
        for x in r:
            if x[0] != "#": readers.setdefault(x, []).append(k)
        for x in w:
            if x[0] != "#":
                last_w[x] = k
                readers[x] = []
        hard.discard(k)
        soft.discard(k)
        if eng == "T":
            for j in list(hard):
                if ops[j]["e"] == "T":
                    hard.discard(j)
                    soft.add(j)
        ops.append({"e": eng, "c": calls, "h": hard, "s": soft, "t": cost, "a": after, "sem": sem, "n": n, "d": dd, "w": w})
        return k

    V, S, PE = g.vector, g.scalar, g.tensor

    def ts(out, in0, s1, s2, o0, o1, r, w, n, f=1.0):
        if o1 is None:
            op("V", [lambda: V.tensor_scalar(out, in0, s1, None, o0)], r, w, (n, f))
        else:
            op("V", [lambda: V.tensor_scalar(out, in0, s1, s2, o0, o1)], r, w, (n, f))

    def tt(out, in0, in1, o, r, w, n, f=1.0):
        op("V", [lambda: V.tensor_tensor(out, in0, in1, o)], r, w, (n, f))

    def cp(out, in_, r, w, n, f=1.0):
        op("V", [lambda: V.tensor_copy(out, in_)], r, w, (n, f))

    def ms(ap, c, w, n):
        op("V", [lambda: V.memset(ap, c)], [], w, (n, 1.0))

    def scan(out, d0, d1, o0, o1, r, w, n):
        op("V", [lambda: V.tensor_tensor_scan(out, d0, d1, 0.0, o0, o1)], r, w, (n, 1.0))

    def act(out, in_, fn, r, w, n, f=1.0, **kw):
        op("A", [lambda: S.activation(out, in_, fn, **kw)], r, w, (n, f))

    def move(e, out, in_, r, w, n, f=1.0):
        if e == "V": cp(out, in_, r, w, n, f)
        elif e == "A": act(out, in_, F.Copy, r, w, n, f)
        else: op("X", [lambda q="V": V.tensor_copy(out, in_) if q == "V" else S.activation(out, in_, F.Copy)], r, w, (n, f))

    def affine(out, in_, a, b, r, w, n):
        op("X", [lambda q="V": V.tensor_scalar(out, in_, a, b, A.mult, A.add) if q == "V"
                 else S.activation(out, in_, F.Identity, bias=b, scale=a)], r, w, (n, 1.0))

    def mm(lst, r, w, cyc):
        op("T", [(lambda a=a: PE.matmul(a[0], a[1], a[2], a[3], a[4])) for a in lst], r, w, (cyc, 1.0))

    def iota(out, pat, base, cm, w, n, small=True):
        if small:
            op("G", [lambda: g.iota(out, pat, base, cm, allow_small_or_imprecise_dtypes=True)], [], w, (200 + 2.5 * n, 1.0))
        else:
            op("G", [lambda: g.iota(out, pat, base, cm)], [], w, (200 + 2.5 * n, 1.0))

    nd, ne = [0], [0]

    def dma(q, out, in_, r, w, dd, after=2400):
        s = "d%d" % nd[0]
        nd[0] += 1
        e = g.sync if q == "S" else g.scalar
        return op(q, [lambda: e.dma_start(out, in_)], r, w, (60, 1.0), after, s, 16, dd)

    def add_dma(out, in_, r, w, dd):
        s = "e%d" % ne[0]
        ne[0] += 1
        op("G", [lambda: g.dma_start(out, in_, accum_op=A.add)], r, w, (1100, 1.0), 2000, s, 16, dd)

    rid, pid = topo.addr(nxt, core)
    eng = topo.engines(core, nxt)[:8]
    mask = sum(1 << e for e in eng)
    sends = [0]

    def send(dst, src, sem, r, w, dd):
        op("G", [lambda: g.remote_dma(dst, src, T.sem[sem], T.sem.sent, pid, rid, mask)], r, ["@" + sem], (900, 1.0), 2600, "sent", 0, dd)
        sends[0] += len(eng)
        op("R", [], ["@" + sem], w, (0, 1.0), 0, sem, len(eng))

    K = T.KW[:, KB:KB + W]
    h = W // 4
    k0 = dma("S", T.BP[:, 0:h], T.bp[:, 0:h], [], ["BPa"], 1000)
    k1 = dma("A", T.BP[:, h:2 * h], T.bp[:, h:2 * h], [], ["BPb"], 1000)
    ops[dma("S", T.ST[:], T.st[:], [], ["ST"], 100)]["s"].add(k0)
    ops[dma("A", K, T.kt[:], [], ["K"], 2000)]["s"].add(k1)
    ops[dma("S", T.VT[:], T.vt[:], [], ["VT"], 2000)]["s"].update((2, 3))
    for j, nm in enumerate(("BPa", "BPb")):
        bp = T.BP[:, j * h:(j + 1) * h]
        ts(T.PG[:, KB + j * h:KB + (j + 1) * h], bp, W - 1, None, A.bitwise_and, None, [nm], ["PG%d" % j], h)
        ts(T.PG[:, KB + (2 + j) * h:KB + (3 + j) * h], bp, 11, None, A.logical_shift_right, None, [nm], ["PG%d" % (2 + j)], h)
    ms(T.PG[:, KB + W:KB + W + 16], 0, ["PG4"], 16)
    iota(T.PG[:, 0:KB], [[0, KB]], 0, 0, ["PGz"], KB, False)
    PGR = ["PG%d" % j for j in range(4)]
    iota(T.PP[:], [[0, 1]], 0, 1, ["PP"], 1, False)
    iota(T.RB[:], [[1, NB]], 0, 0, ["RB"], NB)
    iota(T.CI[:], [[0, 2], [1, 128]], 0, 0, ["CI"], 256)
    iota(T.CV[0:32, 0:256], [[-HL, 2], [0, 128]], -HL, 0, ["CV0", "CV1"], 256)
    iota(T.CV[0:32, 1024:1280], [[HL, 2], [0, 128]], W, 0, ["CV8", "CV9"], 256)
    iota(T.CV[0:32, 256:1024], [[-HL, 6], [0, 128]], -3 * HL, 0, ["CV%d" % j for j in range(2, 8)], 768)
    iota(T.LAM[:], [[1, 64], [0, 16]], 0, 0, ["LAM"], 1024)
    iota(T.RL[:], [[0, NB], [1, 16]], 0, 0, ["RL"], L)
    iota(T.CI3[:], [[8, 16], [0, 2], [1, 8]], 0, 0, ["CI3"], 256)
    iota(T.IO[:], [[1, W]], 2 * W, 0, ["IO"], W)
    iota(T.IC[0:32, :], [[1, W]], 0, 0, ["IC"], W)
    dma("S", T.IO[15::16, :], T.IC[0:8, :], ["IC"], ["IO"], 300)
    bits = ((A.bitwise_and, 15), (A.logical_shift_right, 4), (A.logical_shift_right, 3), (A.bitwise_and, 7),
            (A.logical_shift_right, 5), (A.bitwise_and, 16), (A.bitwise_and, 63), (A.bitwise_and, 3))
    for j, (o, c) in enumerate(bits):
        ts(T.PC[:, j:j + 1], T.PP[:], c, None, o, None, ["PP"], ["PC%d" % j], 1)
    iota(T.PF[:, 8:9], [[0, 1]], 0, 1, ["PF"], 1)
    cp(T.PF[:, 0:8], T.PC[:], ["PC%d" % j for j in range(8)] + ["PF"], ["PF"], 8)
    lf, gf, lc, gc, pa, up, k64, r4, pf = [T.PF[:, j:j + 1] for j in range(9)]
    X = [T.PX[:, j:j + 1] for j in range(16)]
    ts(X[12], r4, 2.0, -8.0, A.is_ge, A.mult, ["PF"], ["X12"], 1)
    ts(X[13], r4, 8.0, gf, A.mult, A.add, ["PF"], ["X13"], 1)
    ts(X[0], lf, 24.0, X[12], A.mult, A.add, ["PF", "X12"], ["X0"], 1)
    ts(X[0], X[0], X[13], None, A.add, None, ["X0", "X13"], ["X0"], 1)
    ts(X[1], gc, 16.0, lc, A.mult, A.add, ["PF"], ["X1"], 1)
    ts(X[2], lf, 4.0, pa, A.mult, A.add, ["PF"], ["X2"], 1)
    ts(X[2], X[2], 2.0, None, A.mult, None, ["X2"], ["X2"], 1)
    ts(X[3], pa, 32.0, lf, A.mult, A.add, ["PF"], ["X3"], 1)
    ts(X[4], lf, float(W), None, A.add, None, ["PF"], ["X4"], 1)
    ts(X[5], lf, 15.0, None, A.is_lt, None, ["PF"], ["X5"], 1)
    ts(X[6], lf, 15.0, 8192.0, A.is_equal, A.mult, ["PF"], ["X6"], 1)
    ts(X[7], gf, 16.0, 15.0, A.mult, A.add, ["PF"], ["X7"], 1)
    for l2 in range(2):
        ts(X[8 + l2], up, 16.0 * l2, None, A.is_equal, None, ["PF"], ["X%d" % (8 + l2)], 1)
        ts(X[10 + l2], up, 16.0 * l2, -1.0, A.is_equal, A.mult, ["PF"], ["X%d" % (10 + l2)], 1)
    ts(T.LO[:], T.RB[:, 0:HB], 384.0, X[0], A.mult, A.add, ["RB", "X0"], ["LO"], HB)
    cp(T.BL[:], T.RB[:], ["RB"], ["BL"], NB)

    def pd(kind, l2, g2):
        j = 4 * kind + 2 * l2 + g2
        return T.PD[:, 128 * j:128 * j + 128]

    for l2 in range(2):
        for g2 in range(2):
            for kind in range(3):
                s0 = 128 - (16 * g2 if kind == 2 else g2)
                x, m = 3 if kind == 2 else 2, (10 if kind == 1 else 8) + l2
                ts(pd(kind, l2, g2), T.CI[:, s0:s0 + 128], X[x], X[m], A.is_equal, A.mult, ["CI", "X%d" % x, "X%d" % m],
                   ["PD%d%d%d" % (kind, l2, g2)], 64)
    PDS = [["PD%d%d%d" % (kind, l2, g2) for l2 in range(2) for g2 in range(2)] for kind in range(3)]
    ts(T.IB2[:], T.CI[:], pf, None, A.is_equal, None, ["CI", "PF"], ["IB2"], 128)
    ts(T.P2[:], T.CI[:], X[1], None, A.is_equal, None, ["CI", "X1"], ["P2"], 256)
    act(T.NP2[:], T.P2[:], F.Identity, ["P2"], ["NP2"], 256, scale=-1.0)
    act(T.ID2[:], T.IB2[:], F.Copy, ["IB2"], ["ID2"], 256)
    for u in range(1, NV):
        ts(T.C2[:, 128 * (u - 1):128 * u], T.CI3[:, :, 8 - u:16 - u], pf, None, A.is_equal, None, ["CI3", "PF"], ["C2%d" % u], 128)
    ts(T.SEL[:], T.LAM[:], k64, None, A.is_equal, None, ["LAM", "PF"], ["SEL"], 512)
    ts(T.BO[:], T.CI[:, 0:144], X[7], X[5], A.is_equal, A.mult, ["CI", "X7", "X5"], ["BO"], 72)
    ts(T.MSK[:], T.RL[:], lf, 0.5, A.is_le, A.subtract, ["RL", "PF"], ["MSK"], L)
    act(T.MSK[:], T.MSK[:], F.Identity, ["MSK"], ["MSK"], L, scale=1.0 / W)
    ms(T.LB[:, 0:1152], 0.0, ["LBz0"], 576)
    for j in range(1, 4):
        act(T.LB[:, 1152 * j:1152 * (j + 1)], T.LB[:, 0:1152], F.Copy, ["LBz0"], ["LBz%d" % j], 1152)
    LBZ = (["LBz2", "LBz3"], ["LBz0", "LBz1"])
    ms(T.INI[:], 0.0, ["INI"], 102)
    ms(T.INI[:, :, 0:2, 1:17], 1712.0 / 1024, ["INI"], 48)
    ts(T.INI[:, :, 2:4, 16], T.RB[:, 0:HB], 16.0, lc, A.mult, A.add, ["RB", "PF"], ["INI"], HB)
    ms(T.IND[0:32], 0.0, ["IND"], 102)
    ms(T.IND[0:32, :, 2:4, 16], 1.0, ["IND"], HB)
    ms(T.CM[:], -1.0 / 1024, ["CM"], 48)
    act(T.M17[:], T.LB[:, 0:HC], F.Identity, ["LBz0"], ["M17"], HC, bias=1.0)
    ms(T.M17[:, 0::17], 0.0, ["M17"], HB)
    act(T.R0[:], T.LB[:, 0:HC], F.Copy, ["LBz0"], ["R0"], HC)
    ms(T.R0[:, 0::17], 1.0, ["R0"], HB)
    act(T.RIN[:], T.LB[:, 0:204], F.Copy, ["LBz0"], ["RIN0", "RIN1"], 204)
    act(T.BT[:], T.LB[:, 0:204], F.Copy, ["LBz0"], ["BT0", "BT1"], 204)
    act(T.MO[:], T.LB[:, 0:612], F.Copy, ["LBz0"], ["MO%d" % m for m in range(6)], 612)
    ms(T.KEY[:], 0.0, ["KEY0", "KEY1"], 32)

    def rot(M, u):
        return M[:, 128 - 16 * u:256 - 16 * u]

    slot, first = [0], []

    def chain(t, hop, x):
        n, last = t * NH + hop, t == NV - 1
        p = n % 2
        b0, b1 = BAT[x]
        j0, j1, c0, c1, k0, k1 = 16 * b0, 16 * b1, b0 // 2, b1 // 2, 17 * b0, 17 * b1
        s = str(x)
        ps = "%d%d" % (p, x)
        m = 2 * t + x
        q0 = HL * (7 - m)
        qa, qb = T.KW[:, q0:q0 + HL], T.KW[:, KB + W + HL * x:KB + W + HL * (x + 1)]
        pS, bS = T["pS" + s], "#S" + s
        NM, NHh = T["NM%d" % p], T["NH%d" % p]
        OMB, ON, BR = T["OMB%d" % p][:, k0:k1], T["ON%d" % p][:, k0:k1], T["BR%d" % hop][:, b0:b1]
        if hop == 0:
            CA = T.CA[:, b0:b1]
            if t == 0:
                cp(CA, T.ST[:, b0:b1], ["ST"], ["CA" + s], HB)
                move("X", qa, K.indirect(CA), ["K", "CA" + s], ["q%d" % m], HL, GA)
                rin, rn = T.R0[:], "R0"
                ts(T.CAS[:, b0:b1], T.ST[:, b0:b1], 1.0 / 4096, 1.0, A.mult, A.add, ["ST"], ["CAS" + s], HB)
            else:
                rin, rn = T.MI[:, HC * (m - 2):HC * (m - 1)], "MI%d" % (m - 2)
                mc = T.MI[:, HC * (m - 2) + 1:HC * (m - 1):17]
                ts(CA, mc, -1.0, None, A.mult, None, [rn], ["CA" + s], HB)
                if not last:
                    affine(T.CAS[:, b0:b1], mc, -1.0 / 4096, 1.0, [rn], ["CAS" + s], HB)
            cl, cln, q, qn, cv = CA, "CA" + s, qa, "q%d" % m, m
        else:
            rin, rn = T.RIN[:, k0:k1], "RIN" + s
            cl, cln, q, qn, cv = T.CL[:, NB * x:NB * x + HB], "CL" + s, qb, "qb" + s, 8 + x
        nm = NM[:, j0:j1]
        cp(nm, T.PG[:, (q0 if hop else KB):KB + W].indirect(cl), PGR + [cln, "PGz"], ["NM" + ps], HL, GA)
        tt(T.LB[:, 24 * j0:24 * j1].indirect(T.LO[:]), q, T.CM[:], A.mult, [qn, "CM", "LO"], LBZ[x] + ["LB" + s], HL, SC)
        cp(NHh[:, j0:j1], nm, ["NM" + ps], ["NH" + ps], HL // 2)
        op("V", [lambda: V.transpose(T.C3[:, c0:c1], NHh[:, j0:j1])], ["NH" + ps], ["C3" + s], (HL // 2, 1.0))
        mm([(pS[:, 0:3, 0:68], T.IB2[:, 0:128], T.INI[:], True, False)], ["IB2", "INI"], [bS, "pS" + s], 204)
        mm([(pS[:, 0:3, 34 + 17 * l2 + kind:50 + 17 * l2 + kind], pd(kind, l2, g2), T.C3[:, c0:c1, g2, :], False, False)
            for l2 in range(2) for g2 in range(2) for kind in range(2)], PDS[0] + PDS[1] + ["C3" + s], [bS, "pS" + s], 512)
        b = b0
        for nb, e in KCH[KPLAN[2 * n + x]]:
            kn = ["KG%d" % j for j in range(b, b + nb)]
            move(e, T.KG[:, 256 * b:256 * (b + nb)], K.indirect(NM[:, 16 * b:16 * (b + nb)]), ["K", "NM" + ps], kn, 256 * nb, GA)
            for bb in range(b, b + nb):
                c, l2 = (bb - b0) // 2, bb % 2
                mm([(pS[32 * (l // 4):32 * (l // 4) + 32, c, 17 * l2 + 1:17 * l2 + 17],
                     T.LB[:, 24 * (16 * bb + l) - 8 * (l % 4 // 2):24 * (16 * bb + l) - 8 * (l % 4 // 2) + 32],
                     T.KG[:, 16 * (16 * bb + l):16 * (16 * bb + l) + 16],
                     False, False) for l in range(16)], ["LB" + s, "KG%d" % bb], [bS, "pS" + s], 512)
            b += nb
        mm([(pS[:, 0:3, 0:68], T.CV[0:1, 128 * cv:128 * cv + 128], T.IND[0:1], False, True)], ["CV%d" % cv, "IND"], [bS, "pS" + s], 204)
        w0 = 204 * p
        Rs, R16 = T.pW[:, w0 + k0:w0 + k1], T.pW[:, w0 + k0 + 16:w0 + k1:17]
        ts(OMB, pS[:, 0:3, 0:34], 0.0625, 1.0, A.max, A.min, [bS, "pS" + s], ["OMB" + ps], HC)
        scan(Rs, OMB, rin, A.mult, A.max, ["OMB" + ps, rn], ["Rs" + ps] + WB, HC)
        ts(ON, Rs, 0.0625, None, A.is_ge, None, ["Rs" + ps] + WB, ["ON" + ps], HC)
        tt(T.TT[:, k0:k1], pS[:, 0:3, 34:68], ON, A.mult, [bS, "pS" + s, "ON" + ps], ["TT" + s], HC)
        scan(T.CS[:, k0:k1], T.M17[:], T.TT[:, k0:k1], A.mult, A.add, ["M17", "TT" + s], ["CS" + s], HC)
        ts(BR, R16, 0.0625, None, A.is_lt, None, ["Rs" + ps] + WB, ["BR%d" % hop + s], HB)
        if hop == 0:
            tt(T.RIN[:, k0:k1:17], R16, BR, A.max, ["Rs" + ps, "BR0" + s] + WB, ["RIN" + s], HB)
        else:
            tt(T.RN[:, b0:b1], R16, BR, A.max, ["Rs" + ps, "BR1" + s] + WB, ["RN" + s], HB)
        cn, qo = T.CS[:, k0 + 15:k1:17], T.CS[:, k0 + 16:k1:17]
        pc, pq, pcq, po = pS[:, 3, 0:HB], pS[:, 3, HB:2 * HB], pS[:, 3, 0:2 * HB], pS[:, 3, 16:28]
        P0 = rot(T.P2, 0)
        if hop == 0:
            mm([(pc, P0, cn, True, True), (pq, P0, qo, True, True)], ["P2", "CS" + s], [bS, "pc" + s], 512)
            ts(T.CL[:, NB * x:NB * (x + 1)], pcq, float(KB - q0), None, A.add, None, [bS, "pc" + s], ["CL" + s], 2 * HB)
            move("X", qb, T.KW[:, q0:KB + W].indirect(T.CL[:, NB * x + HB:NB * (x + 1)]),
                ["K", "CL" + s] + ["q%d" % j for j in range(m + 1)], ["qb" + s], HL, GA)
            return
        if last:
            mm([(pc, P0, cn, True, True)], ["P2", "CS" + s], [bS, "pc" + s], 256)
            cp(T.CQ[:, HB + b0:HB + b1], pc, [bS, "pc" + s], ["CQ" + s], HB)
            return
        u = t + 1
        mm([(pS[:, 3, 17:28:2], rot(T.NP2, u), cn, True, True),
            (pS[:, 3, 16:28:2], T.C2[:, 128 * t:128 * u], T.RN[:, b0:b1], True, True)],
           ["NP2", "C2%d" % u, "CS" + s, "RN" + s], [bS, "po" + s], 512)
        MO = T.MO[:, HB * m:HB * (m + 1), :]
        move("X", T.MO[:, HB * m:HB * (m + 1), 0:2], po, [bS, "po" + s], ["MO%d" % m], 2 * HB)
        send(T.MI[:, HC * m:HC * (m + 1)], MO, "rm%d" % m, ["MO%d" % m], ["MI%d" % m], 300)
        if x == 1: pc, pq = pq, pc
        mm([(pq, P0, qo, True, True), (pc, P0, cn, True, True)], ["P2", "CS" + s], [bS, "pc" + s], 512)
        cp(T.CQ[:, 2 * b0:2 * b1], pcq, [bS, "pc" + s], ["CQ" + s], 2 * HB)
        move("X", T.QS[:, j0:j1], T.KW[:, KB:KB + W + HL * (x + 1)].indirect(T.CQ[:, 3 * b0:3 * b0 + HB]),
            ["K", "CQ" + s] + ["qb%d" % j for j in range(x + 1)], ["QS" + s], HL, GA)
        pt = T.pM[:, 128 + HL * x:128 + HL * (x + 1)]
        mm([(pt, rot(T.IB2, u), T.QS[:, j0:j1], True, True)], ["IB2", "QS" + s], ["#M", "pt" + s], HL)
        QT = T.QT[:, HL * m:HL * (m + 1)]
        move("X", QT, pt, ["#M", "pt" + s], ["QT%d" % m], HL)
        send(T.KW[:, HL * (5 - m):HL * (6 - m)], QT, "rq%d" % m, ["QT%d" % m], ["q%d" % (m + 2)], 300)

    def names(t, hop):
        p, last = hop, t == NV - 1
        p = (NH * t + hop) % DEPTH
        NVv = T["NV%d" % p]
        mm([(T.pN[:, 0:6, :, l2, 0:8], pd(2, l2, g2), T.C3[:, :, g2, :], g2 == 0, g2 == 1)
            for l2 in range(2) for g2 in range(2)], PDS[2] + ["C30", "C31"], ["#N", "pN"], 384)
        cp(NVv[:, 0:96], T.pN[:, 0:6, 0, :, 0:8], ["#N", "pN"], ["NVa%d" % p], 96)
        cp(NVv[:, 96:192], T.pN[:, 0:6, 1, :, 0:8], ["#N", "pN"], ["NVb%d" % p], 96)
        if hop == 0 and not last:
            ts(T.NZ[:], T.NH0[:], X[6], None, A.max, None, ["NH00", "NH01", "X6"], ["NZ"], L // 2)
            tt(T.CW[:], T.IO[:].indirect(T.CA[:]), T.MSK[:], A.mult, ["IO", "CA0", "CA1", "MSK"], ["CW0", "CW1"], L, GA)

    def shortcuts(xs):
        b0, b1 = min(BAT[x][0] for x in xs), max(BAT[x][1] for x in xs)
        nb, x0 = b1 - b0, xs[0]
        nm = lambda a: [a + str(x) for x in xs]
        tt(T.CUT[:, b0:b1], T.BR1[:, b0:b1], T.BR0[:, b0:b1], A.is_gt, nm("BR0") + nm("BR1"), nm("CUT"), nb)
        pk, pm = T.pM[:, 320 + b0:320 + b1], T.pM[:, 336 + b0:336 + b1]
        mm([(pk, rot(T.NP2, 0), T.CUT[:, b0:b1], True, True)], ["NP2"] + nm("CUT"), ["#M"] + nm("pk"), 256)
        tt(T.KEY[:, 16 * x0:16 * x0 + nb], pk, T.CAS[:, b0:b1], A.mult, ["#M"] + nm("pk") + nm("CAS"), nm("KEY"), nb)
        tt(T.EQ[:, 16 * b0:16 * b1], T.KEY[:, 16 * x0:16 * x0 + 16].indirect(T.BL[:, 0:nb]), T.CW[:, 16 * b0:16 * b1], A.is_equal,
           nm("KEY") + nm("CW") + ["BL"], nm("EQ"), 16 * nb, GA)
        mm([(pm, T.ID2[:, 0:128], T.CAS[:, b0:b1], True, False), (pm, rot(T.NP2, 0), T.CUT[:, b0:b1], False, False)]
           + [(pm, T.BO[:, 15 - l:143 - l], T.EQ[:, 16 * b0 + l:16 * b1:16], False, l == 15) for l in range(1, 16)],
           ["ID2", "NP2", "BO"] + nm("CAS") + nm("CUT") + nm("EQ"), ["#M"] + nm("pm"), 512 + 960)
        tt(T.VAL[:, 16 * b0:16 * b1], T.IO[:].indirect(T.CQ[:, HB + b0:HB + b1]), T.NZ[:, 16 * b0:16 * b1], A.min,
           ["IO", "NZ"] + nm("CQ"), nm("VAL"), 16 * nb, GA)
        ts(T.OFF[:, 2 * b0:2 * b1:2], pm, 4096.0, X[4], A.mult, A.min, ["#M", "X4"] + nm("pm"), nm("OFF"), nb)

    def rewrite():
        for x in range(2):
            for b in range(BAT[x][1] - 1, BAT[x][0] - 1, -1):
                cp(T.PG[:, KB:].indirect(T.OFF[:, 2 * b:2 * b + 1]), T.VAL[:, 16 * b:16 * b + 16], ["VAL%d" % x, "OFF%d" % x],
                   PGR + ["PG4"], 16, SC)

    def values(t, hop, xs):
        n = t * NH + hop
        p = n % 2
        b0, b1 = min(BAT[x][0] for x in xs), max(BAT[x][1] for x in xs)
        nb, k0, k1, w0 = b1 - b0, 17 * b0, 17 * b1, 204 * p
        nm = lambda a: [a + str(x) for x in xs]
        np_ = lambda a: [a + "%d%d" % (p, x) for x in xs]
        wv = T.pW[:, w0 + k0:w0 + k1]
        affine(T.BT[:, k0:k1 - 1], T["OMB%d" % p][:, k0 + 1:k1], -1.0, 1.0, np_("OMB"), nm("BT"), 17 * nb)
        tt(wv, wv, T["ON%d" % p][:, k0:k1], A.mult, np_("ON") + WB, np_("Rs"), 17 * nb)
        tt(wv, wv, T.BT[:, k0:k1], A.mult, nm("BT") + WB, np_("Rs"), 17 * nb)
        if hop == 1:
            cp(T.pW[:, w0 + k0 + 16:w0 + k1:17], T.RN[:, b0:b1], nm("RN") + WB, np_("Rs"), nb)
        lo, hi = slice(0, 64), slice(64, 128)
        d = n % DEPTH
        nd_ = lambda a: [a + "%d%d" % (d, x) for x in xs]
        XA, XB = T["XA%d" % d], T["XB%d" % d]
        XS = nd_("XAh") + nd_("XAl") + nd_("XBh") + nd_("XBl")
        flat = n in FLAT
        if flat:
            move(HI, XA[:, b0:b1, :], wv, np_("Rs") + WB, nd_("XAh") + nd_("XAl"), 17 * nb)
            tt(XB[:, b0:b1, :], wv, XA[:, b0:b1, :], A.subtract, np_("Rs") + nd_("XAh") + nd_("XAl") + WB, nd_("XBh") + nd_("XBl"), 17 * nb)
        else:
            for Xt, xn, a, o in ((XA, "XA", lo, hi), (XB, "XB", hi, lo)):
                move(HI, Xt[a, b0:b1, :], T.pW[a, w0 + k0:w0 + k1], np_("Rs") + WB, nd_(xn + "h"), 17 * nb)
                tt(Xt[o, b0:b1, :], T.pW[a, w0 + k0:w0 + k1], Xt[a, b0:b1, :], A.subtract, np_("Rs") + nd_(xn + "h") + WB,
                   nd_(xn + "l"), 17 * nb)

        def spread(out, l, i):
            s0 = 128 * (l % 8)
            if not flat:
                return [(out, T.SEL[:, s0:s0 + 128], (XA if l < 8 else XB)[:, b0:b1, i], True, True)]
            a = lo if l < 8 else hi
            return [(out, T.SEL[a, s0:s0 + 128], XA[a, b0:b1, i], True, False), (out, T.SEL[a, s0:s0 + 128], XB[a, b0:b1, i], False, True)]

        VG, NVv = T["VG%d" % d], T["NV%d" % d]
        if hop == 1:
            VC, pE = VG[:, 16 * L + 16 * b0:16 * L + 16 * b1], T["pE%d" % (slot[0] % 2)]
            e = slot[0] % 2
            slot[0] += 1
            act(VC, T.VT[:].indirect(T.CQ[:, HB + b0:HB + b1]), F.Sigmoid, ["VT"] + nm("CQ"), nd_("VC"), 16 * nb, GA)
            mm(sum([spread(pE[:, l:16 * nb:16], l, 16) for l in range(16)], []), ["SEL"] + XS, ["#E%d" % e, "pE%d" % e], 1024 * (1 + flat))
            tt(T["RV%d" % (t % 2)][:, 16 * b0:16 * b1], VC, pE[:, 0:16 * nb], A.mult, nd_("VC") + ["#E%d" % e, "pE%d" % e],
               nm("RV%d" % (t % 2)), 16 * nb)
        for hf in range(2):
            ni = 8
            y0 = 96 * hf
            for x in xs:
                for y in range(VSP):
                    a0, a1 = [y0 + ni * BAT[x][0] + 2 * ((ni * HB // 2 * z) // VSP) for z in (y, y + 1)]
                    act(VG[:, 16 * a0:16 * a1], T.VT[:].indirect(NVv[:, a0:a1]), F.Sigmoid, ["VT", "NV" + "ab"[hf] + str(d)],
                        ["VG%d%d%d%d" % (y, hf, d, x)], 16 * (a1 - a0), GA)
                    if not first:
                        first.append(len(ops) - 1)
                        ops[-1]["x"] = 1560
                    else:
                        ops[-1]["s"].add(first[0])
            a0, a1, ny = y0 + ni * b0, y0 + ni * b1, ni * nb
            into = ONTO.get((t, 2 * hop + hf))
            bn = "B%d" % (4 * (t % 2) + (2 * hop + hf if into is None else into))
            for s4 in range(4):
                e = slot[0] % 2
                slot[0] += 1
                pE, en = T["pE%d" % e], ["#E%d" % e, "pE%d" % e]
                mm(sum([spread(pE[:, lq:4 * ny:4], 4 * lq + s4, slice(8 * hf, 8 * hf + 8)) for lq in range(4)], []),
                   ["SEL"] + XS, en, 4 * max(64, ny) * (1 + flat))
                B, bs, vs = T[bn][:, b0:b1, :, s4::4], nm(bn + "s%d" % s4), sum([nd_("VG%d%d" % (y, hf)) for y in range(VSP)], [])
                if into is None:
                    tt(B, VG[:, 16 * a0 + s4:16 * a1:4], pE[:, 0:4 * ny], A.mult, vs + en, bs, 4 * ny)
                else:
                    tt(pE[:, 0:4 * ny], VG[:, 16 * a0 + s4:16 * a1:4], pE[:, 0:4 * ny], A.mult, vs + en, en, 4 * ny)
                    tt(B, pE[:, 0:4 * ny], B, A.add, en + bs, bs, 4 * ny)

    def parts(j, xs=(0, 1)):
        return ["B%ds%d%d" % (j, s4, x) for s4 in range(4) for x in xs]

    def add(j, k):
        for xs in (((0,), (1,)) if ASP else ((0, 1),)):
            b0, b1 = min(BAT[x][0] for x in xs), max(BAT[x][1] for x in xs)
            add_dma(T["B%d" % j][:, b0:b1], T["B%d" % k][:, b0:b1], parts(k, xs), parts(j, xs), ACC * len(xs) // 2)

    def report(t, xs, srcs, pR, bR):
        b0, b1 = min(BAT[x][0] for x in xs), max(BAT[x][1] for x in xs)
        j0, j1 = 16 * b0, 16 * b1
        rn = "pR%d" % xs[0]
        lst = []
        for j in srcs:
            B, k = T["B%d" % j], 8
            for _ in range(VADD.get((t, j % 4, xs), 0)):
                k //= 2
                tt(B[:, b0:b1, 0:k, :], B[:, b0:b1, 0:k, :], B[:, b0:b1, k:2 * k, :], A.add, parts(j, xs), parts(j, xs), k * (j1 - j0), 2)
            lst += [(B[:, b0:b1, i, :], T.ID2[:, 0:128], parts(j, xs)) for i in range(k)]
        if t:
            lst.insert(0, (T["AI%d" % t][:, j0:j1], rot(T.ID2, t), ["AI%d" % t]))
        for k, (src, M, r) in enumerate(lst):
            mm([(pR, M, src, k == 0, k == len(lst) - 1)], ["ID2"] + r, [bR, rn], 4 * (j1 - j0))
        RP = T["RP%d" % t]
        if t < NV - 1:
            move("X", T["AC%d" % (t + 1)][:], pR, [bR, rn], ["AC%d" % (t + 1)], L)
            send(T["AI%d" % (t + 1)][:], T["AC%d" % (t + 1)][:], "ra%d" % (t + 1), ["AC%d" % (t + 1)], ["AI%d" % (t + 1)], 600)
        tt(RP[:, j0:j1], pR, T["RV%d" % (t % 2)][:, j0:j1], A.add, [bR, rn] + ["RV%d%d" % (t % 2, x) for x in xs], ["RP%d%d" % (t, xs[0])], j1 - j0)
        dma("S", T.ya[:, L * t + j0:L * t + j1], RP[:, j0:j1], ["RP%d%d" % (t, xs[0])], ["ya%d%d" % (t, xs[0])], 300, 2200)

    WB = ["#W"] if HI != "V" else []
    for t in range(NV):
        last, o = t == NV - 1, 4 * (t % 2)
        chain(t, 0, 0)
        chain(t, 0, 1)
        names(t, 0)
        values(t, 0, (0, 1))
        if 1 in ADDS[t]: add(o, o + 1)
        srcs = [o + j for j in range(4) if j not in ADDS[t] and (t, j) not in ONTO]
        chain(t, 1, 0)
        if not last and SPLIT_CUT: shortcuts((0,))
        chain(t, 1, 1)
        names(t, 1)
        if not last:
            shortcuts((1,) if SPLIT_CUT else (0, 1))
            rewrite()
            values(t, 1, (0, 1))
            for j in (2, 3):
                if j in ADDS[t]: add(o, o + j)
            report(t, (0, 1), srcs[::-1], T.pR[:, 0:L], "#R")
        else:
            values(t, 1, (0,))
            values(t, 1, (1,))
            report(t, (0,), srcs, T.pR[:, 0:HL], "#R")
            report(t, (1,), srcs, T.pM[:, 0:HL], "#M")
    return ops, sends[0]


def costs(ops, s):
    out = []
    for o in ops:
        e, n, f = o["e"], o["t"][0], o["t"][1]
        if o["sem"] or e in "GSR": c = n
        elif e == "T": c = s[2] * n * 0.5
        elif f == GA: c = s[2] * ((60 if e == "V" else 78) + n * s[0]) + o.get("x", 0)
        elif f == SC: c = s[2] * (60 + n * s[1])
        else: c = s[2] * (s[3] + max(n * f, 64))
        out.append(int(c))
    return out


ENG = "VATGSR"


def prepare(ops):
    n = len(ops)
    en = [ENG.index(o["e"]) if o["e"] != "X" else 1 for o in ops]
    pred = [[j + n for j in o["h"]] + [j for j in o["s"] if j not in o["h"]] for o in ops]
    succ = [[] for _ in ops]
    for k, o in enumerate(ops):
        for j in o["h"] | o["s"]:
            succ[j].append(k)
    cs = [(costs(ops, s), [int(o["d"] * s[5]) for o in ops], [o["a"] + (0 if o["e"] == "R" else s[4]) for o in ops]) for s in COSTS]
    return en, pred, succ, cs, [o["e"] == "X" for o in ops]


def play(pre, c, rest, tm, free):
    en, pred = pre[0], pre[1]
    cost, dd, aft = c
    n = len(en)
    for k in rest:
        e = en[k]
        s = free[e]
        for j in pred[k]:
            if tm[j] > s: s = tm[j]
        s += cost[k]
        tm[k] = s
        if e != 5: free[e] = s
        if dd[k]:
            if free[6] > s: s = free[6]
            s += dd[k]
            free[6] = s
        tm[n + k] = s + aft[k]
    return tm


def place(busy, t, c):
    lo, hi = 0, len(busy)
    while lo < hi:
        mid = (lo + hi) // 2
        if busy[mid][1] <= t: lo = mid + 1
        else: hi = mid
    while lo < len(busy) and busy[lo][0] < t + c:
        t = busy[lo][1]
        lo += 1
    return t, lo


def sweep(pre, c, seq, back, bias):
    en, pred, succ = pre[0], pre[1], pre[2]
    cost, dd, aft = c
    n = len(en)
    busy = [[] for _ in range(7)]
    st = [0] * n
    low = [0] * n
    for k in seq:
        e, ck, d = en[k], cost[k], dd[k]
        if back:
            t = max(low[k], aft[k] + d)
        else:
            t = 0
            for j in pred[k]:
                x = st[j - n] + cost[j - n] + dd[j - n] + aft[j - n] if j >= n else st[j] + cost[j]
                if x > t: t = x
        if pre[4][k]:
            e = en[k] = 0 if place(busy[0], t, ck)[0] + bias[k] < place(busy[1], t, ck)[0] else 1
        if e != 5:
            while True:
                t, i = place(busy[e], t, ck)
                if not d: break
                u = t - d if back else t + ck
                v, i2 = place(busy[6], u, d)
                if v == u:
                    busy[6].insert(i2, (u, u + d))
                    break
                t += v - u
            busy[e].insert(i, (t, t + ck))
        st[k] = t
        if back:
            for j in pred[k]:
                x = t + ck
                if j >= n:
                    j -= n
                    x += dd[j] + aft[j]
                if x > low[j]: low[j] = x
    if back:
        top = max([a + b for a, b in zip(st, cost)])
        return [top - a - b for a, b in zip(st, cost)]
    return st


def length(pre, order):
    n = len(order)
    return [max(play(pre, c, order, [0.0] * (2 * n), [0.0] * 7)[n:]) for c in pre[3]]


def schedule(ops):
    n = len(ops)
    pre = prepare(ops)
    en, pred, succ, cs, free = pre
    c = cs[0]
    seed = [SEED]

    def rnd(m):
        seed[0] = (seed[0] * 1103515245 + 12345) % 2 ** 31
        return (seed[0] >> 8) % m

    def legal(key, back):
        key = list(key)
        for k in (range(n - 1, -1, -1) if back else range(n)):
            for j in (succ[k] if back else pred[k]):
                if key[j % n] > key[k]: key[k] = key[j % n]
        return sorted(range(n), key=lambda k: (key[k], -k if back else k))

    pr = [0] * n
    for k in range(n - 1, -1, -1):
        pr[k] = c[0][k] + c[1][k] + c[2][k] + max([pr[j] for j in succ[k]] + [0])
    bias = [BIAS] * n
    flex = [k for k in range(n) if free[k]]
    st = sweep(pre, c, legal([-x for x in pr], False), False, bias)
    best, cur, order, keep, where = 1e18, 1e18, None, st, None
    for it in range(TRIES):
        amp = SHAKE[it % len(SHAKE)]
        t0 = rnd(max(keep) + SPAN) - SPAN
        shake = [rnd(amp) if t0 <= a < t0 + SPAN else 0 for a in keep]
        b2 = list(bias)
        for k in flex:
            if shake[k] and rnd(4) == 0: b2[k] = 400 * rnd(12) - 1600
        st = sweep(pre, c, legal([-(a + b) + z for a, b, z in zip(keep, c[0], shake)], True), True, b2)
        st = sweep(pre, c, legal([a + z for a, z in zip(st, shake)], False), False, b2)
        od = sorted(range(n), key=lambda k: (st[k], k))
        s = sum(w * x for w, x in zip(WEIGHTS, length(pre, od)))
        if s < cur * (1 + KEEP * (1 - it / TRIES)): cur, keep, bias = s, st, b2
        if s < best: best, order, where = s, od, list(en)
    en[:] = where
    return refine(pre, order), en


def refine(pre, order):
    en, pred, succ, cs = pre[:4]
    n = len(en)
    ps = [set(j % n for j in p) for p in pred]
    ss = [set(p) for p in succ]
    tails = [n + k for k in range(n) if not succ[k] and en[k] == 4]
    isd = [c > 0 for c in cs[0][1]]
    seed = [99]

    def rnd(m):
        seed[0] = (seed[0] * 1103515245 + 12345) % 2 ** 31
        return (seed[0] >> 8) % m

    def score(order, p0, tms):
        lastop = [-1] * 7
        for i in range(p0 - 1, -1, -1):
            k = order[i]
            if lastop[en[k]] < 0: lastop[en[k]] = k
            if isd[k] and lastop[6] < 0: lastop[6] = k
            if i < p0 - 40 and min(lastop[:5]) >= 0 and lastop[6] >= 0: break
        tot, out, rest = 0.0, [], order[p0:]
        for c, w, old in zip(cs, WEIGHTS, tms):
            tm = list(old)
            free = [tm[k] if k >= 0 else 0.0 for k in lastop]
            free[5] = 0.0
            if lastop[6] >= 0: free[6] = tm[n + lastop[6]] - c[2][lastop[6]]
            play(pre, c, rest, tm, free)
            tot += w * (max([tm[k] for k in tails]) + 0.02 * (free[0] + free[1] + free[2]))
            out.append(tm)
        return tot, out

    def critical(order, tms):
        pos = {k: i for i, k in enumerate(order)}
        prev, lastop = {}, {}
        for k in order:
            prev[k] = lastop.get(en[k], -1)
            lastop[en[k]] = k
        out = []
        for c, tm in zip(cs, tms):
            k = max([(tm[j], j) for j in tails])[1] - n
            while k >= 0:
                out.append(pos[k])
                s, nx = tm[k] - c[0][k] - 0.5, -1
                for j in pred[k]:
                    if tm[j] >= s: nx = j % n
                if nx < 0 and en[k] != 5 and prev[k] >= 0 and tm[prev[k]] >= s: nx = prev[k]
                k = nx
        return out

    cur, tms = score(order, 0, [[0.0] * (2 * n) for _ in cs])
    best, bo, crit = cur, list(order), []
    for it in range(MOVES):
        if it % 64 == 0: crit = critical(order, tms)
        i = rnd(n) if rnd(3) == 0 else min(n - 1, max(0, crit[rnd(len(crit))] + rnd(5) - 2))
        k = order[i]
        e = en[k]
        if e > 3: continue
        m, j = 1 + rnd(3), i
        if rnd(2):
            while j > 0 and m and order[j - 1] not in ps[k]:
                j -= 1
                if en[order[j]] == e: m -= 1
        else:
            while j < n - 1 and m and order[j + 1] not in ss[k]:
                j += 1
                if en[order[j]] == e: m -= 1
        if j == i: continue
        o2 = list(order)
        o2.pop(i)
        o2.insert(j, k)
        s, e2 = score(o2, min(i, j), tms)
        if s <= cur + 0.4 * rnd(100) * (1 - it / MOVES):
            cur, order, tms = s, o2, e2
            if s < best: best, bo = s, o2
    return bo


def rank_program(g, core, T, topo):
    rank = T.rank_of(core)
    if rank is None:
        return
    nxt = T.cores[(rank + 1) % len(T.cores)]
    ops, nsent = collect(g, T, topo, core, nxt)
    if "o" not in ORDER:
        ORDER["o"] = schedule(ops)
    order, where = ORDER["o"]
    Q = {"V": g.vector, "A": g.scalar, "T": g.tensor, "G": g, "S": g.sync}
    cnt = {"V": 0, "A": 0, "T": 0, "G": 0}
    known = {e: {} for e in Q}
    done = {}
    total = {}
    for k in order:
        o = ops[k]
        e = ENG[where[k]]
        if e == "R":
            done[k] = (o["sem"], o["n"], {})
            total[o["sem"]] = o["n"]
            continue
        kn = known[e]
        want = sorted((done[j] for j in o["h"]), key=lambda d: -len(d[2]))
        top = {}
        for s, v, clock in want:
            top[s] = max(top.get(s, 0), v)
        for s, v, clock in want:
            if v == top[s] and kn.get(s, 0) < v:
                Q[e].wait_ge(T.sem[s], v)
                kn[s] = v
                for s2, v2 in clock.items():
                    if kn.get(s2, 0) < v2: kn[s2] = v2
        if o["sem"] == "sent":
            o["c"][0]()
            done[k] = ("sent", 0, {})
        elif o["sem"]:
            o["c"][0]().then_inc(T.sem[o["sem"]], o["n"])
            done[k] = (o["sem"], o["n"], dict(kn))
            total[o["sem"]] = o["n"]
        else:
            for c in o["c"]:
                (c(e) if o["e"] == "X" else c()).then_inc(T.sem["c" + e], 1)
                cnt[e] += 1
            done[k] = ("c" + e, cnt[e], dict(kn))
            total["c" + e] = cnt[e]
    total["sent"] = nsent
    for s, v in total.items():
        g.wait_ge(T.sem[s], v)
